import numpy as np
import ml_dtypes


def mxq(x, axis, fmt="e4m3"):
    dtype, down = {"e4m3": (ml_dtypes.float8_e4m3fn, 7), "e5m2": (ml_dtypes.float8_e5m2, 14)}[fmt]
    v = np.moveaxis(np.asarray(x, np.float32).astype(ml_dtypes.bfloat16).astype(np.float64), axis, -1)
    blocks = v.reshape(v.shape[:-1] + (-1, 32))
    amax = np.abs(blocks).max(-1, keepdims=True)
    byte = np.maximum(np.where(amax > 0, np.frexp(amax)[1] - 1 + 127, 0) - down, 1)
    scale = np.exp2(byte - 127.0)
    codes = (blocks / scale).astype(np.float32).astype(dtype).astype(np.float64)
    return np.moveaxis((codes * scale).reshape(v.shape), -1, axis)


WIDE = False


def mx_kscale(k):
    if not WIDE:
        return np.ones(k)
    levels = np.array([10, -10, 5, -5, 0])
    if k % 512:
        return np.exp2(np.random.permutation(np.resize(levels, k // 32))).repeat(32)
    a = np.empty((k // 512, 16))
    for p in range(k // 512):
        a[p, :8] = np.random.permutation(np.resize(levels, 8))
        for g in range(8):
            far = levels[np.abs(levels - a[p, g]) >= 10]
            a[p, g + 8] = far[np.random.randint(len(far))]
    return np.exp2(a.ravel()).repeat(32)


def f64(x):
    return np.asarray(x).astype(np.float64)


def striped(idx):
    return np.tile(idx.reshape(-1, 16).T, (8, 1)).astype(np.uint16)


def unstriped(offs):
    return offs[:16].T.reshape(-1).astype(np.int64)


E2M1 = np.array([0.0, 0.5, 1.0, 1.5, 2.0, 3.0, 4.0, 6.0, -0.0, -0.5, -1.0, -1.5, -2.0, -3.0, -4.0, -6.0])


def pack_weight(w, fmt):
    k, n = w.shape
    w = f64(np.asarray(w, np.float32).astype(ml_dtypes.bfloat16)).reshape(k // 32, 32, n)
    amax = np.abs(w).max(1)
    if fmt == "e4m3":
        byte = np.frexp(amax)[1] - 1 + 127 - 7
    else:
        mant, ex = np.frexp(amax / 6.0)
        byte = np.where(mant > 0.5, ex, ex - 1) + 127
    byte = np.clip(np.where(amax > 0, byte, 1), 1, 254)
    scaled = (w * np.exp2(127.0 - byte)[:, None, :]).reshape(k, n).astype(np.float32)
    by_word = np.ascontiguousarray(scaled.reshape(k // 512, 128, 4, n).transpose(0, 1, 3, 2))
    if fmt == "e4m3":
        words = by_word.astype(ml_dtypes.float8_e4m3fn).view(np.uint8)
    else:
        c = by_word.astype(ml_dtypes.float4_e2m1fn).view(np.uint8) & 0xF
        words = (c[..., 0::2] | (c[..., 1::2] << 4)).reshape(k // 512, 128, 2 * n)
    return np.ascontiguousarray(words), np.ascontiguousarray(byte.astype(np.uint8).reshape(k // 512, 16, n))


def unpack_weight(words, scales, fmt):
    g, _, n = scales.shape
    words = np.ascontiguousarray(words).reshape(g, 128, n, -1)
    if fmt == "e4m3":
        vals = words.view(ml_dtypes.float8_e4m3fn).astype(np.float64)
    else:
        nib = np.empty((g, 128, n, 4), np.uint8)
        nib[..., 0::2] = words & 0xF
        nib[..., 1::2] = words >> 4
        vals = E2M1[nib]
    vals = vals * np.repeat(np.exp2(scales.astype(np.float64) - 127.0), 8, axis=1)[..., None]
    return vals.transpose(0, 1, 3, 2).reshape(g * 512, n)


def d_relu(v):
    return (v > 0).astype(np.float64)


K, T, E, C, H, N = 128, 512, 8, 128, 512, 1024


def by_expert(wq, xq):
    return np.concatenate([wq[e].T @ xq[:, e * C:(e + 1) * C] for e in range(E)], axis=1)


def setup_inputs():
    n = np.random.standard_normal
    v = mx_kscale(N)
    u = mx_kscale(H)
    first = np.random.permutation(np.repeat(np.arange(E), T // E))
    second = (first + 1 + np.random.permutation(np.repeat(np.arange(E - 1), -(-T // (E - 1)))[:T])) % E
    while np.bincount(second, minlength=E).max() != T // E:
        load = np.bincount(second, minlength=E); hi, lo = int(load.argmax()), int(load.argmin())
        t = np.flatnonzero((second == hi) & (first != lo))[0]; second[t] = lo
    slot_token = np.empty(E * C, np.int64); pos = np.empty((2, T), np.int64); fill = np.zeros(E, np.int64)
    place = np.stack([np.random.permutation(C) for _ in range(E)])
    for r, deal in enumerate((first, second)):
        for t in np.random.permutation(T):
            e = deal[t]; j = e * C + place[e, fill[e]]; fill[e] += 1; slot_token[j] = t; pos[r, t] = j
    g = np.random.uniform(0.2, 0.8, T)
    w_slot = np.empty(E * C); w_slot[pos[0]] = g; w_slot[pos[1]] = 1.0 - g
    dy = pack_weight(n((N, T)) * v[:, None], "e4m3")
    w2t = pack_weight(n((N, H)) / np.sqrt(N) / v[:, None] * u, "e4m3")
    w1t = [pack_weight(m, "e4m3") for m in n((E, H, K)) / np.sqrt(H) / u[None, :, None]]
    return {
        "dy_words": dy[0],
        "dy_scales": dy[1],
        "w2t_words": w2t[0],
        "w2t_scales": w2t[1],
        "w1t_words": np.stack([m[0] for m in w1t]),
        "w1t_scales": np.stack([m[1] for m in w1t]),
        "a": (n((H, E * C))).astype(np.float32),
        "gate": (np.tile(w_slot, (128, 1))).astype(np.float32),
        "offs": striped(slot_token),
        "pos1": striped(pos[0]),
        "pos2": striped(pos[1]),
    }


def reference(dy_words, dy_scales, w2t_words, w2t_scales, w1t_words, w1t_scales, a, gate, offs, pos1, pos2):
    w2t = unpack_weight(w2t_words, w2t_scales, "e4m3")
    w1t = np.stack([unpack_weight(w1t_words[e], w1t_scales[e], "e4m3") for e in range(E)])
    idx = unstriped(offs)
    dc = w2t.T @ unpack_weight(dy_words, dy_scales, "e4m3")
    da = f64(gate[:1]) * dc[:, idx] * d_relu(f64(a))
    dx = by_expert(w1t, mxq(da, 0, "e4m3"))
    out = dx[:, unstriped(pos1)] + dx[:, unstriped(pos2)]
    return out

@@ -1,0 +1,194 @@
+from contextlib import ExitStack
+
+import concourse.mybir as mybir
+
+K, T, E, C, H, N = 128, 512, 8, 128, 512, 1024
+S = E * C
+FLOPS = 2 * N * H * T + 2 * H * K * S
+
+F32 = mybir.dt.float32
+BF16 = mybir.dt.bfloat16
+I32 = mybir.dt.int32
+U16 = mybir.dt.uint16
+U8 = mybir.dt.uint8
+FP8X4 = mybir.dt.float8_e4m3fn_x4
+ALU = mybir.AluOpType
+
+P = 128
+PACK = 4
+PASSES = N // (P * PACK)
+PAD = 32
+CHUNKS = (512, 256, 128, 128)
+
+
+def tile_moe_sdb_relu_kernel(
+    tc, dy_words, dy_scales, w2t_words, w2t_scales, w1t_words, w1t_scales, a, gate, offs, pos1, pos2, out
+):
+    nc = tc.nc
+    starts = [sum(CHUNKS[:c]) for c in range(len(CHUNKS))]
+    last = len(CHUNKS) - 1
+
+    with ExitStack() as ctx:
+        keep = ctx.enter_context(tc.tile_pool(name="keep", bufs=1))
+        psum = ctx.enter_context(tc.psum_pool(name="psum", bufs=1))
+
+        offs_sb = keep.tile([P, S // 16], U16, name="offs_sb")
+        pos1_sb = keep.tile([P, T // 16], U16, name="pos1_sb")
+        pos2_sb = keep.tile([P, T // 16], U16, name="pos2_sb")
+
+        w2_raw = keep.tile([P, PASSES, H], I32, name="w2_raw", align_bytes=64)
+        w2_codes = keep.tile([P, PACK, PASSES, P], I32, name="w2_codes", align_bytes=64)
+        dy_codes = keep.tile([P, PASSES, T], I32, name="dy_codes", align_bytes=64)
+        w1_codes = keep.tile([P, E, K], I32, name="w1_codes", align_bytes=64)
+        w2_scales_raw = keep.tile([P, H], U8, name="w2_scales_raw", align_bytes=64)
+        dy_planes = keep.tile([P, PASSES, T], U8, name="dy_planes", align_bytes=64)
+        w2_scales = keep.tile([P, PACK, P], U8, name="w2_scales", align_bytes=64)
+        w1_scales = keep.tile([P, E, K], U8, name="w1_scales", align_bytes=64)
+        dc = [keep.tile([P, T + PAD], F32, name=f"dc{r}") for r in range(PACK)]
+        dx = keep.tile([P, S], F32, name="dx")
+        gates = [keep.tile([P, w], F32, name=f"gate{c}") for c, w in enumerate(CHUNKS)]
+        acts = [keep.tile([P, PACK, w], F32, name=f"act{c}") for c, w in enumerate(CHUNKS)]
+
+        nc.gpsimd.memset(w2_scales_raw[:].bitcast(I32), 0)
+        for r in range(PACK):
+            nc.vector.memset(dc[r][:, T:], 0.0)
+
+        a_rows = a.rearrange("(p r) j -> p r j", r=PACK)
+
+        def load_dy_scales(q):
+            nc.sync.dma_start(
+                dy_planes[32 * q : 32 * q + 4, :, :].bitcast(I32),
+                dy_scales[:, 4 * q : 4 * q + 4, :].rearrange("s b t -> b s t").bitcast(I32),
+            )
+
+        load_dy_scales(0)
+        load_dy_scales(1)
+        nc.sync.dma_start(w2_raw[:], w2t_words.rearrange("s p i d -> p s (i d)").bitcast(I32))
+        for q in range(4):
+            nc.sync.dma_start(
+                w2_scales_raw[32 * q : 32 * q + 4 * PASSES, :].bitcast(I32),
+                w2t_scales[:, 4 * q : 4 * q + 4, :].bitcast(I32),
+            )
+        nc.sync.dma_start(dy_codes[:], dy_words.rearrange("s p t d -> p s (t d)").bitcast(I32))
+        load_dy_scales(2)
+        load_dy_scales(3)
+        nc.sync.dma_start(gates[0][:], gate[:, : CHUNKS[0]])
+        nc.sync.dma_start(acts[0][:, 0, :], a_rows[:, 0, : CHUNKS[0]])
+        nc.sync.dma_start(offs_sb[:], offs)
+        nc.sync.dma_start(acts[0][:, 1:, :], a_rows[:, 1:, : CHUNKS[0]])
+        for c in range(1, len(CHUNKS)):
+            cols = slice(starts[c], starts[c] + CHUNKS[c])
+            nc.sync.dma_start(gates[c][:], gate[:, cols])
+            nc.sync.dma_start(acts[c][:], a_rows[:, :, cols])
+        nc.sync.dma_start(w1_codes[:], w1t_words.rearrange("e o p k d -> p (e o) (k d)").bitcast(I32))
+        for q in range(4):
+            nc.sync.dma_start(
+                w1_scales[32 * q : 32 * q + 4, :, :].bitcast(I32),
+                w1t_scales[:, 0, 4 * q : 4 * q + 4, :].rearrange("e b k -> b e k").bitcast(I32),
+            )
+        nc.sync.dma_start(pos1_sb[:], pos1)
+        nc.sync.dma_start(pos2_sb[:], pos2)
+
+        nc.vector.tensor_copy(
+            w2_codes[:].rearrange("p r s (c i) -> p (s c) r i", i=4),
+            w2_raw[:].rearrange("p s (c i r) -> p (s c) r i", i=4, r=PACK),
+        )
+        nc.vector.tensor_copy(w2_scales[:], w2_scales_raw[:].rearrange("p (m r) -> p r m", r=PACK))
+
+        for r in range(PACK):
+            bank = psum.tile([P, T], F32, name=f"dc_bank{r}")
+            for s in range(PASSES):
+                nc.tensor.matmul_mx(
+                    out=bank[:],
+                    lhsT=w2_codes[:, r, s, :].bitcast(FP8X4),
+                    lhsT_scale=w2_scales[4 * s :, r, :],
+                    rhs=dy_codes[:, s, :].bitcast(FP8X4),
+                    rhs_scale=dy_planes[:, s, :],
+                    start=(s == 0),
+                    stop=(s == PASSES - 1),
+                )
+            nc.scalar.copy(dc[r][:, :T], bank[:])
+
+        da = [keep.tile([P, w, PACK], BF16, name=f"da{c}", align_bytes=64) for c, w in enumerate(CHUNKS)]
+
+        def gather(c):
+            w = CHUNKS[c]
+            lists = offs_sb[:, starts[c] // 16 : (starts[c] + w) // 16]
+            picked = keep.tile([P, PACK, w], F32, name=f"picked{c}")
+            if c == last:
+                for r in range(PACK):
+                    nc.vector.tensor_tensor(picked[:, r, :], dc[r][:].indirect(lists), gates[c][:], ALU.mult)
+                return picked
+            factor = keep.tile([P, PACK, w], F32, name=f"factor{c}")
+            if c == 0:
+                for r in range(PACK):
+                    nc.vector.scalar_tensor_tensor(
+                        factor[:, r, :], acts[c][:, r, :], 0.0, gates[c][:], ALU.is_gt, ALU.mult
+                    )
+                    nc.vector.tensor_tensor(picked[:, r, :], dc[r][:].indirect(lists), factor[:, r, :], ALU.mult)
+            else:
+                nc.vector.scalar_tensor_tensor(
+                    factor[:], acts[c][:], 0.0, gates[c][:].unsqueeze(1).to_broadcast([P, PACK, w]), ALU.is_gt, ALU.mult
+                )
+                for r in range(PACK):
+                    nc.vector.tensor_tensor(picked[:, r, :], dc[r][:].indirect(lists), factor[:, r, :], ALU.mult)
+            nc.scalar.copy(
+                da[c][:].rearrange("p (c i) r -> p c r i", i=4),
+                picked[:].rearrange("p r (c i) -> p c r i", i=4),
+            )
+            return picked
+
+        def project(c):
+            w = CHUNKS[c]
+            codes = keep.tile([P, w], I32, name=f"codes{c}", align_bytes=64)
+            scales = keep.tile([P, w], U8, name=f"scales{c}", align_bytes=64)
+            nc.vector.quantize_mx(
+                out=codes[:].bitcast(FP8X4), scales=scales[:], in_=da[c][:].rearrange("p j r -> p (j r)")
+            )
+            bank = psum.tile([P, w], F32, name=f"dx_bank{c}")
+            for u in range(w // C):
+                e = starts[c] // C + u
+                cols = slice(u * C, (u + 1) * C)
+                nc.tensor.matmul_mx(
+                    out=bank[:, cols],
+                    lhsT=w1_codes[:, e, :].bitcast(FP8X4),
+                    lhsT_scale=w1_scales[:, e, :],
+                    rhs=codes[:, cols].bitcast(FP8X4),
+                    rhs_scale=scales[:, cols],
+                    start=True,
+                    stop=True,
+                )
+            nc.scalar.copy(dx[:, starts[c] : starts[c] + w], bank[:])
+
+        for c in range(len(CHUNKS)):
+            picked = gather(c)
+            if c > 0:
+                project(c - 1)
+        nc.vector.scalar_tensor_tensor(
+            da[last][:],
+            acts[last][:].rearrange("p r j -> p j r"),
+            0.0,
+            picked[:].rearrange("p r j -> p j r"),
+            ALU.is_gt,
+            ALU.mult,
+        )
+        project(last)
+
+        half = T // 2
+        first = [keep.tile([P, half], F32, name=f"first{h}") for h in range(2)]
+        second = [keep.tile([P, half], F32, name=f"second{h}") for h in range(2)]
+        result = [keep.tile([P, half], F32, name=f"result{h}") for h in range(2)]
+
+        def fetch(dst, lists, h):
+            nc.vector.tensor_copy(dst[h][:], dx[:].indirect(lists[:, h * half // 16 : (h + 1) * half // 16]))
+
+        def combine(h):
+            nc.vector.tensor_tensor(result[h][:], first[h][:], second[h][:], ALU.add)
+            nc.sync.dma_start(out[:, h * half : (h + 1) * half], result[h][:])
+
+        fetch(first, pos1_sb, 0)
+        fetch(second, pos2_sb, 0)
+        fetch(first, pos1_sb, 1)
+        combine(0)
+        fetch(second, pos2_sb, 1)
+        combine(1)

@@ -13,20 +13,23 @@ U16 = mybir.dt.uint16
 U8 = mybir.dt.uint8
 FP8X4 = mybir.dt.float8_e4m3fn_x4
 ALU = mybir.AluOpType
+ACT = mybir.ActivationFunctionType
 
 P = 128
 PACK = 4
 PASSES = N // (P * PACK)
 PAD = 32
-CHUNKS = (512, 256, 128, 128)
+HALF = T // 2
+CHUNKS = (256, 128, 128, 256, 256)
+MODES = "DDBBB"
+PARTS = (0, 384, 512)
 
 
 def tile_moe_sdb_relu_kernel(
     tc, dy_words, dy_scales, w2t_words, w2t_scales, w1t_words, w1t_scales, a, gate, offs, pos1, pos2, out
 ):
     nc = tc.nc
-    starts = [sum(CHUNKS[:c]) for c in range(len(CHUNKS))]
-    last = len(CHUNKS) - 1
+    spans = [slice(sum(CHUNKS[:c]), sum(CHUNKS[: c + 1])) for c in range(len(CHUNKS))]
 
     with ExitStack() as ctx:
         keep = ctx.enter_context(tc.tile_pool(name="keep", bufs=1))
@@ -41,51 +44,72 @@ def tile_moe_sdb_relu_kernel(
         dy_codes = keep.tile([P, PASSES, T], I32, name="dy_codes", align_bytes=64)
         w1_codes = keep.tile([P, E, K], I32, name="w1_codes", align_bytes=64)
         w2_scales_raw = keep.tile([P, H], U8, name="w2_scales_raw", align_bytes=64)
-        dy_planes = keep.tile([P, PASSES, T], U8, name="dy_planes", align_bytes=64)
         w2_scales = keep.tile([P, PACK, P], U8, name="w2_scales", align_bytes=64)
+        dy_planes = keep.tile([P, PASSES, T], U8, name="dy_planes", align_bytes=64)
         w1_scales = keep.tile([P, E, K], U8, name="w1_scales", align_bytes=64)
+        gate_sb = keep.tile([P, S], F32, name="gate_sb")
+        acts = keep.tile([P, PACK, S], F32, name="acts")
+        picked = keep.tile([P, PACK, S], F32, name="picked")
+        factor = keep.tile([P, PACK, S], F32, name="factor")
         dc = [keep.tile([P, T + PAD], F32, name=f"dc{r}") for r in range(PACK)]
         dx = keep.tile([P, S], F32, name="dx")
-        gates = [keep.tile([P, w], F32, name=f"gate{c}") for c, w in enumerate(CHUNKS)]
-        acts = [keep.tile([P, PACK, w], F32, name=f"act{c}") for c, w in enumerate(CHUNKS)]
+        signs = keep.tile([P, S, PACK], BF16, name="signs", tag="staged")
+        passed = keep.tile([P, S, PACK], BF16, name="passed")
+        da = keep.tile([P, S, PACK], BF16, name="da", align_bytes=64)
+        da_codes = keep.tile([P, S], I32, name="da_codes", align_bytes=64)
+        da_scales = keep.tile([P, S], U8, name="da_scales", align_bytes=64)
 
         nc.gpsimd.memset(w2_scales_raw[:].bitcast(I32), 0)
         for r in range(PACK):
             nc.vector.memset(dc[r][:, T:], 0.0)
 
         a_rows = a.rearrange("(p r) j -> p r j", r=PACK)
+        dy_rows = dy_words.rearrange("s p t d -> p s (t d)").bitcast(I32)
 
-        def load_dy_scales(q):
-            nc.sync.dma_start(
+        def load_dy_scales(queue, q):
+            queue.dma_start(
                 dy_planes[32 * q : 32 * q + 4, :, :].bitcast(I32),
                 dy_scales[:, 4 * q : 4 * q + 4, :].rearrange("s b t -> b s t").bitcast(I32),
             )
 
-        load_dy_scales(0)
-        load_dy_scales(1)
-        nc.sync.dma_start(w2_raw[:], w2t_words.rearrange("s p i d -> p s (i d)").bitcast(I32))
-        for q in range(4):
+        def load_w2_scales(q):
             nc.sync.dma_start(
                 w2_scales_raw[32 * q : 32 * q + 4 * PASSES, :].bitcast(I32),
                 w2t_scales[:, 4 * q : 4 * q + 4, :].bitcast(I32),
             )
-        nc.sync.dma_start(dy_codes[:], dy_words.rearrange("s p t d -> p s (t d)").bitcast(I32))
-        load_dy_scales(2)
-        load_dy_scales(3)
-        nc.sync.dma_start(gates[0][:], gate[:, : CHUNKS[0]])
-        nc.sync.dma_start(acts[0][:, 0, :], a_rows[:, 0, : CHUNKS[0]])
+
+        def load_gate(j0, j1):
+            nc.sync.dma_start(gate_sb[:, j0:j1], gate[:, j0:j1])
+
+        def load_acts(j0, j1):
+            nc.sync.dma_start(acts[:, :, j0:j1], a_rows[:, :, j0:j1])
+
+        def load_w1(queue):
+            queue.dma_start(w1_codes[:], w1t_words.rearrange("e o p k d -> p (e o) (k d)").bitcast(I32))
+            for q in range(4):
+                queue.dma_start(
+                    w1_scales[32 * q : 32 * q + 4, :, :].bitcast(I32),
+                    w1t_scales[:, 0, 4 * q : 4 * q + 4, :].rearrange("e b k -> b e k").bitcast(I32),
+                )
+
+        load_dy_scales(nc.sync, 0)
+        load_dy_scales(nc.sync, 1)
+        load_dy_scales(nc.sync, 2)
+        nc.sync.dma_start(w2_raw[:], w2t_words.rearrange("s p i d -> p s (i d)").bitcast(I32))
+        load_w2_scales(0)
+        load_w2_scales(1)
+        load_w2_scales(2)
+        load_w2_scales(3)
+        nc.sync.dma_start(dy_codes[:, :, :HALF], dy_rows[:, :, :HALF])
+        load_dy_scales(nc.sync, 3)
+        nc.sync.dma_start(dy_codes[:, :, HALF:], dy_rows[:, :, HALF:])
+        load_gate(0,512)
         nc.sync.dma_start(offs_sb[:], offs)
-        nc.sync.dma_start(acts[0][:, 1:, :], a_rows[:, 1:, : CHUNKS[0]])
-        for c in range(1, len(CHUNKS)):
-            cols = slice(starts[c], starts[c] + CHUNKS[c])
-            nc.sync.dma_start(gates[c][:], gate[:, cols])
-            nc.sync.dma_start(acts[c][:], a_rows[:, :, cols])
-        nc.sync.dma_start(w1_codes[:], w1t_words.rearrange("e o p k d -> p (e o) (k d)").bitcast(I32))
-        for q in range(4):
-            nc.sync.dma_start(
-                w1_scales[32 * q : 32 * q + 4, :, :].bitcast(I32),
-                w1t_scales[:, 0, 4 * q : 4 * q + 4, :].rearrange("e b k -> b e k").bitcast(I32),
-            )
+        load_gate(512,1024)
+        load_acts(384,768)
+        load_acts(768,1024)
+        load_acts(0,384)
+        load_w1(nc.sync)
         nc.sync.dma_start(pos1_sb[:], pos1)
         nc.sync.dma_start(pos2_sb[:], pos2)
 
@@ -95,96 +119,135 @@ def tile_moe_sdb_relu_kernel(
         )
         nc.vector.tensor_copy(w2_scales[:], w2_scales_raw[:].rearrange("p (m r) -> p r m", r=PACK))
 
-        for r in range(PACK):
-            bank = psum.tile([P, T], F32, name=f"dc_bank{r}")
+        def hidden(r, tokens, tag):
+            bank = psum.tile([P, tokens.stop - tokens.start], F32, name=f"dc_bank{r}_{tokens.start}", tag=tag)
             for s in range(PASSES):
                 nc.tensor.matmul_mx(
                     out=bank[:],
                     lhsT=w2_codes[:, r, s, :].bitcast(FP8X4),
                     lhsT_scale=w2_scales[4 * s :, r, :],
-                    rhs=dy_codes[:, s, :].bitcast(FP8X4),
-                    rhs_scale=dy_planes[:, s, :],
+                    rhs=dy_codes[:, s, tokens].bitcast(FP8X4),
+                    rhs_scale=dy_planes[:, s, tokens],
                     start=(s == 0),
                     stop=(s == PASSES - 1),
                 )
-            nc.scalar.copy(dc[r][:, :T], bank[:])
+            nc.scalar.copy(dc[r][:, tokens], bank[:])
 
-        da = [keep.tile([P, w, PACK], BF16, name=f"da{c}", align_bytes=64) for c, w in enumerate(CHUNKS)]
+        hidden(0, slice(0, HALF), "bank0")
+        hidden(0, slice(HALF, T), "bank1")
+        for r in range(1, PACK):
+            hidden(r, slice(0, T), f"bank{r + 1}")
 
-        def gather(c):
-            w = CHUNKS[c]
-            lists = offs_sb[:, starts[c] // 16 : (starts[c] + w) // 16]
-            picked = keep.tile([P, PACK, w], F32, name=f"picked{c}")
-            if c == last:
-                for r in range(PACK):
-                    nc.vector.tensor_tensor(picked[:, r, :], dc[r][:].indirect(lists), gates[c][:], ALU.mult)
-                return picked
-            factor = keep.tile([P, PACK, w], F32, name=f"factor{c}")
-            if c == 0:
-                for r in range(PACK):
-                    nc.vector.scalar_tensor_tensor(
-                        factor[:, r, :], acts[c][:, r, :], 0.0, gates[c][:], ALU.is_gt, ALU.mult
-                    )
-                    nc.vector.tensor_tensor(picked[:, r, :], dc[r][:].indirect(lists), factor[:, r, :], ALU.mult)
-            else:
+        def interleaved(ap):
+            return ap.rearrange("p (c i) r -> p c r i", i=4)
+
+        def planes(ap):
+            return ap.rearrange("p r (c i) -> p c r i", i=4)
+
+        def mask(c):
+            nc.scalar.activation(interleaved(signs[:, spans[c], :]), planes(acts[:, :, spans[c]]), ACT.Sign)
+            nc.scalar.activation(passed[:, spans[c], :], signs[:, spans[c], :], ACT.Relu)
+
+        def gm(c):
+            nc.vector.scalar_tensor_tensor(
+                factor[:, :, spans[c]],
+                acts[:, :, spans[c]],
+                0.0,
+                gate_sb[:, spans[c]].unsqueeze(1).to_broadcast([P, PACK, CHUNKS[c]]),
+                ALU.is_gt,
+                ALU.mult,
+            )
+
+        def gather(r, j0, j1, fac=False):
+            lists = offs_sb[:, j0 // 16 : j1 // 16]
+            other = factor[:, r, j0:j1] if fac else gate_sb[:, j0:j1]
+            nc.vector.tensor_tensor(picked[:, r, j0:j1], dc[r][:].indirect(lists), other, ALU.mult)
+
+        def il(c, rounded):
+            dst = rounded if MODES[c] == "B" else da
+            nc.scalar.copy(interleaved(dst[:, spans[c], :]), planes(picked[:, :, spans[c]]))
+
+        def fin(c, rounded):
+            if MODES[c] == "B":
+                nc.vector.tensor_tensor(da[:, spans[c], :], rounded[:, spans[c], :], passed[:, spans[c], :], ALU.mult)
+            if MODES[c] == "D":
                 nc.vector.scalar_tensor_tensor(
-                    factor[:], acts[c][:], 0.0, gates[c][:].unsqueeze(1).to_broadcast([P, PACK, w]), ALU.is_gt, ALU.mult
+                    da[:, spans[c], :],
+                    acts[:, :, spans[c]].rearrange("p r j -> p j r"),
+                    0.0,
+                    picked[:, :, spans[c]].rearrange("p r j -> p j r"),
+                    ALU.is_gt,
+                    ALU.mult,
                 )
-                for r in range(PACK):
-                    nc.vector.tensor_tensor(picked[:, r, :], dc[r][:].indirect(lists), factor[:, r, :], ALU.mult)
-            nc.scalar.copy(
-                da[c][:].rearrange("p (c i) r -> p c r i", i=4),
-                picked[:].rearrange("p r (c i) -> p c r i", i=4),
-            )
-            return picked
 
-        def project(c):
-            w = CHUNKS[c]
-            codes = keep.tile([P, w], I32, name=f"codes{c}", align_bytes=64)
-            scales = keep.tile([P, w], U8, name=f"scales{c}", align_bytes=64)
+        def quant(c):
             nc.vector.quantize_mx(
-                out=codes[:].bitcast(FP8X4), scales=scales[:], in_=da[c][:].rearrange("p j r -> p (j r)")
+                out=da_codes[:, spans[c]].bitcast(FP8X4),
+                scales=da_scales[:, spans[c]],
+                in_=da[:, spans[c], :].rearrange("p j r -> p (j r)"),
             )
-            bank = psum.tile([P, w], F32, name=f"dx_bank{c}")
-            for u in range(w // C):
-                e = starts[c] // C + u
-                cols = slice(u * C, (u + 1) * C)
+
+        def proj(c, tag):
+            bank = psum.tile([P, CHUNKS[c]], F32, name=f"dx_bank{c}", tag=tag)
+            for u in range(CHUNKS[c] // C):
+                e = spans[c].start // C + u
                 nc.tensor.matmul_mx(
-                    out=bank[:, cols],
+                    out=bank[:, u * C : (u + 1) * C],
                     lhsT=w1_codes[:, e, :].bitcast(FP8X4),
                     lhsT_scale=w1_scales[:, e, :],
-                    rhs=codes[:, cols].bitcast(FP8X4),
-                    rhs_scale=scales[:, cols],
+                    rhs=da_codes[:, e * C : (e + 1) * C].bitcast(FP8X4),
+                    rhs_scale=da_scales[:, e * C : (e + 1) * C],
                     start=True,
                     stop=True,
                 )
-            nc.scalar.copy(dx[:, starts[c] : starts[c] + w], bank[:])
+            if c == 2:
+                nc.vector.tensor_copy(dx[:, spans[c]], bank[:])
+            else:
+                nc.scalar.copy(dx[:, spans[c]], bank[:])
 
-        for c in range(len(CHUNKS)):
-            picked = gather(c)
-            if c > 0:
-                project(c - 1)
-        nc.vector.scalar_tensor_tensor(
-            da[last][:],
-            acts[last][:].rearrange("p r j -> p j r"),
-            0.0,
-            picked[:].rearrange("p r j -> p j r"),
-            ALU.is_gt,
-            ALU.mult,
-        )
-        project(last)
+        mask(2)
+        mask(3)
+        mask(4)
+        rounded = keep.tile([P, S, PACK], BF16, name="rounded", tag="staged")
+        gather(0,0,512)
+        gather(1,0,512)
+        gather(2,0,512)
+        gather(3,0,512)
+        gather(0,512,1024)
+        gather(1,512,1024)
+        gather(2,512,1024)
+        gather(3,512,1024)
+        il(3, rounded)
+        il(4, rounded)
+        il(2, rounded)
+        fin(0, rounded)
+        fin(1, rounded)
+        quant(0)
+        quant(1)
+        proj(0, "bank5")
+        proj(1, "bank6")
+        fin(3, rounded)
+        fin(4, rounded)
+        quant(3)
+        fin(2, rounded)
+        quant(4)
+        quant(2)
+        proj(3, "bank0")
+        proj(4, "bank1")
+        proj(2, "bank7")
 
-        half = T // 2
-        first = [keep.tile([P, half], F32, name=f"first{h}") for h in range(2)]
-        second = [keep.tile([P, half], F32, name=f"second{h}") for h in range(2)]
-        result = [keep.tile([P, half], F32, name=f"result{h}") for h in range(2)]
+        first = keep.tile([P, T], F32, name="first")
+        second = keep.tile([P, T], F32, name="second")
+        result = keep.tile([P, T], F32, name="result")
 
         def fetch(dst, lists, h):
-            nc.vector.tensor_copy(dst[h][:], dx[:].indirect(lists[:, h * half // 16 : (h + 1) * half // 16]))
+            t0, t1 = PARTS[h], PARTS[h + 1]
+            nc.vector.tensor_copy(dst[:, t0:t1], dx[:].indirect(lists[:, t0 // 16 : t1 // 16]))
 
         def combine(h):
-            nc.vector.tensor_tensor(result[h][:], first[h][:], second[h][:], ALU.add)
-            nc.sync.dma_start(out[:, h * half : (h + 1) * half], result[h][:])
+            t0, t1 = PARTS[h], PARTS[h + 1]
+            nc.vector.tensor_tensor(result[:, t0:t1], first[:, t0:t1], second[:, t0:t1], ALU.add)
+            nc.sync.dma_start(out[:, t0:t1], result[:, t0:t1])
 
         fetch(first, pos1_sb, 0)
         fetch(second, pos2_sb, 0)

@@ -22,7 +22,7 @@ PAD = 32
 HALF = T // 2
 CHUNKS = (256, 128, 128, 256, 256)
 MODES = "DDBBB"
-PARTS = (0, 384, 512)
+PARTS = (0, 256, 384, 512)
 
 
 def tile_moe_sdb_relu_kernel(
@@ -113,11 +113,14 @@ def tile_moe_sdb_relu_kernel(
         nc.sync.dma_start(pos1_sb[:], pos1)
         nc.sync.dma_start(pos2_sb[:], pos2)
 
-        nc.vector.tensor_copy(
-            w2_codes[:].rearrange("p r s (c i) -> p (s c) r i", i=4),
-            w2_raw[:].rearrange("p s (c i r) -> p (s c) r i", i=4, r=PACK),
-        )
-        nc.vector.tensor_copy(w2_scales[:], w2_scales_raw[:].rearrange("p (m r) -> p r m", r=PACK))
+        for rows in (slice(0, 1), slice(1, PACK)):
+            nc.vector.tensor_copy(
+                w2_codes[:, rows, :, :].rearrange("p r s (c i) -> p (s c) r i", i=4),
+                w2_raw[:].rearrange("p s (c i r) -> p (s c) r i", i=4, r=PACK)[:, :, rows, :],
+            )
+            nc.vector.tensor_copy(
+                w2_scales[:, rows, :], w2_scales_raw[:].rearrange("p (m r) -> p r m", r=PACK)[:, rows, :]
+            )
 
         def hidden(r, tokens, tag):
             bank = psum.tile([P, tokens.stop - tokens.start], F32, name=f"dc_bank{r}_{tokens.start}", tag=tag)
@@ -144,9 +147,15 @@ def tile_moe_sdb_relu_kernel(
         def planes(ap):
             return ap.rearrange("p r (c i) -> p c r i", i=4)
 
+        def sign(j0, j1):
+            nc.scalar.activation(interleaved(signs[:, j0:j1, :]), planes(acts[:, :, j0:j1]), ACT.Sign)
+
+        def relu(j0, j1):
+            nc.scalar.activation(passed[:, j0:j1, :], signs[:, j0:j1, :], ACT.Relu)
+
         def mask(c):
-            nc.scalar.activation(interleaved(signs[:, spans[c], :]), planes(acts[:, :, spans[c]]), ACT.Sign)
-            nc.scalar.activation(passed[:, spans[c], :], signs[:, spans[c], :], ACT.Relu)
+            sign(spans[c].start, spans[c].stop)
+            relu(spans[c].start, spans[c].stop)
 
         def gm(c):
             nc.vector.scalar_tensor_tensor(
@@ -244,14 +253,17 @@ def tile_moe_sdb_relu_kernel(
             t0, t1 = PARTS[h], PARTS[h + 1]
             nc.vector.tensor_copy(dst[:, t0:t1], dx[:].indirect(lists[:, t0 // 16 : t1 // 16]))
 
-        def combine(h):
+        def combine(h, engine):
             t0, t1 = PARTS[h], PARTS[h + 1]
-            nc.vector.tensor_tensor(result[:, t0:t1], first[:, t0:t1], second[:, t0:t1], ALU.add)
+            engine.tensor_tensor(result[:, t0:t1], first[:, t0:t1], second[:, t0:t1], ALU.add)
             nc.sync.dma_start(out[:, t0:t1], result[:, t0:t1])
 
         fetch(first, pos1_sb, 0)
         fetch(second, pos2_sb, 0)
+        combine(0, nc.gpsimd)
         fetch(first, pos1_sb, 1)
-        combine(0)
         fetch(second, pos2_sb, 1)
-        combine(1)
+        fetch(first, pos1_sb, 2)
+        fetch(second, pos2_sb, 2)
+        combine(1, nc.vector)
+        combine(2, nc.vector)

@@ -18,18 +18,19 @@ ACT = mybir.ActivationFunctionType
 P = 128
 PACK = 4
 PASSES = N // (P * PACK)
-PAD = 32
 HALF = T // 2
-CHUNKS = (256, 128, 128, 256, 256)
-MODES = "DDBBB"
-PARTS = (0, 256, 384, 512)
+MASKED = 640
+FUSED = S - MASKED
+PAD = MASKED + 32 - T
+MASK_PIECES = (0, 256, 512, MASKED)
+FUSED_PIECES = (MASKED, MASKED + 256, S)
+PARTS = (0, 384, T)
 
 
 def tile_moe_sdb_relu_kernel(
     tc, dy_words, dy_scales, w2t_words, w2t_scales, w1t_words, w1t_scales, a, gate, offs, pos1, pos2, out
 ):
     nc = tc.nc
-    spans = [slice(sum(CHUNKS[:c]), sum(CHUNKS[: c + 1])) for c in range(len(CHUNKS))]
 
     with ExitStack() as ctx:
         keep = ctx.enter_context(tc.tile_pool(name="keep", bufs=1))
@@ -40,28 +41,28 @@ def tile_moe_sdb_relu_kernel(
         pos2_sb = keep.tile([P, T // 16], U16, name="pos2_sb")
 
         w2_raw = keep.tile([P, PASSES, H], I32, name="w2_raw", align_bytes=64)
-        w2_codes = keep.tile([P, PACK, PASSES, P], I32, name="w2_codes", align_bytes=64)
+        w2_first = keep.tile([P, 1, PASSES, P], I32, name="w2_first", align_bytes=64)
         dy_codes = keep.tile([P, PASSES, T], I32, name="dy_codes", align_bytes=64)
         w1_codes = keep.tile([P, E, K], I32, name="w1_codes", align_bytes=64)
-        w2_scales_raw = keep.tile([P, H], U8, name="w2_scales_raw", align_bytes=64)
+        w2_scales_raw = keep.tile([P, H], U8, name="w2_scales_raw", tag="sorted", align_bytes=64)
         w2_scales = keep.tile([P, PACK, P], U8, name="w2_scales", align_bytes=64)
         dy_planes = keep.tile([P, PASSES, T], U8, name="dy_planes", align_bytes=64)
         w1_scales = keep.tile([P, E, K], U8, name="w1_scales", align_bytes=64)
         gate_sb = keep.tile([P, S], F32, name="gate_sb")
         acts = keep.tile([P, PACK, S], F32, name="acts")
-        picked = keep.tile([P, PACK, S], F32, name="picked")
-        factor = keep.tile([P, PACK, S], F32, name="factor")
+        picked_m = keep.tile([P, PACK, MASKED], F32, name="picked_m", tag="wide")
+        picked_f = keep.tile([P, PACK, FUSED], F32, name="picked_f", tag="late")
+        factor = keep.tile([P, PACK, FUSED], F32, name="factor")
         dc = [keep.tile([P, T + PAD], F32, name=f"dc{r}") for r in range(PACK)]
-        dx = keep.tile([P, S], F32, name="dx")
-        signs = keep.tile([P, S, PACK], BF16, name="signs", tag="staged")
-        passed = keep.tile([P, S, PACK], BF16, name="passed")
+        signs = keep.tile([P, MASKED, PACK], BF16, name="signs", tag="staged")
+        passed = keep.tile([P, MASKED, PACK], BF16, name="passed")
         da = keep.tile([P, S, PACK], BF16, name="da", align_bytes=64)
         da_codes = keep.tile([P, S], I32, name="da_codes", align_bytes=64)
         da_scales = keep.tile([P, S], U8, name="da_scales", align_bytes=64)
 
         nc.gpsimd.memset(w2_scales_raw[:].bitcast(I32), 0)
         for r in range(PACK):
-            nc.vector.memset(dc[r][:, T:], 0.0)
+            nc.gpsimd.memset(dc[r][:, T:], 0.0)
 
         a_rows = a.rearrange("(p r) j -> p r j", r=PACK)
         dy_rows = dy_words.rearrange("s p t d -> p s (t d)").bitcast(I32)
@@ -72,11 +73,17 @@ def tile_moe_sdb_relu_kernel(
                 dy_scales[:, 4 * q : 4 * q + 4, :].rearrange("s b t -> b s t").bitcast(I32),
             )
 
-        def load_w2_scales(q):
-            nc.sync.dma_start(
+        def load_w2_scales(queue, q):
+            queue.dma_start(
                 w2_scales_raw[32 * q : 32 * q + 4 * PASSES, :].bitcast(I32),
                 w2t_scales[:, 4 * q : 4 * q + 4, :].bitcast(I32),
             )
+
+        def load_w2(queue):
+            queue.dma_start(w2_raw[:], w2t_words.rearrange("s p i d -> p s (i d)").bitcast(I32))
+
+        def load_dy(queue, t0, t1):
+            queue.dma_start(dy_codes[:, :, t0:t1], dy_rows[:, :, t0:t1])
 
         def load_gate(j0, j1):
             nc.sync.dma_start(gate_sb[:, j0:j1], gate[:, j0:j1])
@@ -93,41 +100,49 @@ def tile_moe_sdb_relu_kernel(
                 )
 
         load_dy_scales(nc.sync, 0)
-        load_dy_scales(nc.sync, 1)
-        load_dy_scales(nc.sync, 2)
-        nc.sync.dma_start(w2_raw[:], w2t_words.rearrange("s p i d -> p s (i d)").bitcast(I32))
-        load_w2_scales(0)
-        load_w2_scales(1)
-        load_w2_scales(2)
-        load_w2_scales(3)
-        nc.sync.dma_start(dy_codes[:, :, :HALF], dy_rows[:, :, :HALF])
-        load_dy_scales(nc.sync, 3)
-        nc.sync.dma_start(dy_codes[:, :, HALF:], dy_rows[:, :, HALF:])
-        load_gate(0,512)
+        load_w2_scales(nc.sync, 0)
+        load_w2_scales(nc.sync, 1)
+        load_w2(nc.sync)
+        load_dy(nc.sync, 0, HALF)
+        load_w2_scales(nc.sync, 2)
+        load_w2_scales(nc.sync, 3)
+        for q in range(1, 4):
+            load_dy_scales(nc.sync, q)
+        load_dy(nc.sync, HALF, T)
+        load_gate(0, MASKED)
         nc.sync.dma_start(offs_sb[:], offs)
-        load_gate(512,1024)
-        load_acts(384,768)
-        load_acts(768,1024)
-        load_acts(0,384)
+        load_acts(0, 256)
+        load_acts(256, MASKED)
+        load_gate(MASKED, S)
+        load_acts(MASKED, S)
         load_w1(nc.sync)
         nc.sync.dma_start(pos1_sb[:], pos1)
         nc.sync.dma_start(pos2_sb[:], pos2)
 
-        for rows in (slice(0, 1), slice(1, PACK)):
+        def sort_words(dst, rows):
             nc.vector.tensor_copy(
-                w2_codes[:, rows, :, :].rearrange("p r s (c i) -> p (s c) r i", i=4),
+                dst[:].rearrange("p r s (c i) -> p (s c) r i", i=4),
                 w2_raw[:].rearrange("p s (c i r) -> p (s c) r i", i=4, r=PACK)[:, :, rows, :],
             )
+
+        def sort_scales(rows):
             nc.vector.tensor_copy(
                 w2_scales[:, rows, :], w2_scales_raw[:].rearrange("p (m r) -> p r m", r=PACK)[:, rows, :]
             )
+
+        sort_words(w2_first, slice(0, 1))
+        sort_scales(slice(0, 1))
+        sort_scales(slice(1, PACK))
+        w2_rest = keep.tile([P, PACK - 1, PASSES, P], I32, name="w2_rest", tag="sorted", align_bytes=64)
+        sort_words(w2_rest, slice(1, PACK))
+        w2_codes = [w2_first[:, 0, :, :]] + [w2_rest[:, r, :, :] for r in range(PACK - 1)]
 
         def hidden(r, tokens, tag):
             bank = psum.tile([P, tokens.stop - tokens.start], F32, name=f"dc_bank{r}_{tokens.start}", tag=tag)
             for s in range(PASSES):
                 nc.tensor.matmul_mx(
                     out=bank[:],
-                    lhsT=w2_codes[:, r, s, :].bitcast(FP8X4),
+                    lhsT=w2_codes[r][:, s, :].bitcast(FP8X4),
                     lhsT_scale=w2_scales[4 * s :, r, :],
                     rhs=dy_codes[:, s, tokens].bitcast(FP8X4),
                     rhs_scale=dy_planes[:, s, tokens],
@@ -147,61 +162,38 @@ def tile_moe_sdb_relu_kernel(
         def planes(ap):
             return ap.rearrange("p r (c i) -> p c r i", i=4)
 
-        def sign(j0, j1):
+        def mask(j0, j1):
             nc.scalar.activation(interleaved(signs[:, j0:j1, :]), planes(acts[:, :, j0:j1]), ACT.Sign)
-
-        def relu(j0, j1):
             nc.scalar.activation(passed[:, j0:j1, :], signs[:, j0:j1, :], ACT.Relu)
 
-        def mask(c):
-            sign(spans[c].start, spans[c].stop)
-            relu(spans[c].start, spans[c].stop)
+        def gather(dst, r, j0, j1, other):
+            nc.vector.tensor_tensor(dst, dc[r][:].indirect(offs_sb[:, j0 // 16 : j1 // 16]), other, ALU.mult)
 
-        def gm(c):
+        def apply_mask(rounded, j0, j1):
+            nc.vector.tensor_tensor(da[:, j0:j1, :], rounded[:, j0:j1, :], passed[:, j0:j1, :], ALU.mult)
+
+        def make_factor():
             nc.vector.scalar_tensor_tensor(
-                factor[:, :, spans[c]],
-                acts[:, :, spans[c]],
+                factor[:],
+                acts[:, :, MASKED:],
                 0.0,
-                gate_sb[:, spans[c]].unsqueeze(1).to_broadcast([P, PACK, CHUNKS[c]]),
+                gate_sb[:, MASKED:].unsqueeze(1).to_broadcast([P, PACK, FUSED]),
                 ALU.is_gt,
                 ALU.mult,
             )
 
-        def gather(r, j0, j1, fac=False):
-            lists = offs_sb[:, j0 // 16 : j1 // 16]
-            other = factor[:, r, j0:j1] if fac else gate_sb[:, j0:j1]
-            nc.vector.tensor_tensor(picked[:, r, j0:j1], dc[r][:].indirect(lists), other, ALU.mult)
-
-        def il(c, rounded):
-            dst = rounded if MODES[c] == "B" else da
-            nc.scalar.copy(interleaved(dst[:, spans[c], :]), planes(picked[:, :, spans[c]]))
-
-        def fin(c, rounded):
-            if MODES[c] == "B":
-                nc.vector.tensor_tensor(da[:, spans[c], :], rounded[:, spans[c], :], passed[:, spans[c], :], ALU.mult)
-            if MODES[c] == "D":
-                nc.vector.scalar_tensor_tensor(
-                    da[:, spans[c], :],
-                    acts[:, :, spans[c]].rearrange("p r j -> p j r"),
-                    0.0,
-                    picked[:, :, spans[c]].rearrange("p r j -> p j r"),
-                    ALU.is_gt,
-                    ALU.mult,
-                )
-
-        def quant(c):
+        def quant(j0, j1):
             nc.vector.quantize_mx(
-                out=da_codes[:, spans[c]].bitcast(FP8X4),
-                scales=da_scales[:, spans[c]],
-                in_=da[:, spans[c], :].rearrange("p j r -> p (j r)"),
+                out=da_codes[:, j0:j1].bitcast(FP8X4),
+                scales=da_scales[:, j0:j1],
+                in_=da[:, j0:j1, :].rearrange("p j r -> p (j r)"),
             )
 
-        def proj(c, tag):
-            bank = psum.tile([P, CHUNKS[c]], F32, name=f"dx_bank{c}", tag=tag)
-            for u in range(CHUNKS[c] // C):
-                e = spans[c].start // C + u
+        def proj(dx, j0, j1, tag, copy):
+            bank = psum.tile([P, j1 - j0], F32, name=f"dx_bank{j0}", tag=tag)
+            for e in range(j0 // C, j1 // C):
                 nc.tensor.matmul_mx(
-                    out=bank[:, u * C : (u + 1) * C],
+                    out=bank[:, e * C - j0 : (e + 1) * C - j0],
                     lhsT=w1_codes[:, e, :].bitcast(FP8X4),
                     lhsT_scale=w1_scales[:, e, :],
                     rhs=da_codes[:, e * C : (e + 1) * C].bitcast(FP8X4),
@@ -209,61 +201,43 @@ def tile_moe_sdb_relu_kernel(
                     start=True,
                     stop=True,
                 )
-            if c == 2:
-                nc.vector.tensor_copy(dx[:, spans[c]], bank[:])
-            else:
-                nc.scalar.copy(dx[:, spans[c]], bank[:])
+            copy(dx[:, j0:j1], bank[:])
 
-        mask(2)
-        mask(3)
-        mask(4)
-        rounded = keep.tile([P, S, PACK], BF16, name="rounded", tag="staged")
-        gather(0,0,512)
-        gather(1,0,512)
-        gather(2,0,512)
-        gather(3,0,512)
-        gather(0,512,1024)
-        gather(1,512,1024)
-        gather(2,512,1024)
-        gather(3,512,1024)
-        il(3, rounded)
-        il(4, rounded)
-        il(2, rounded)
-        fin(0, rounded)
-        fin(1, rounded)
-        quant(0)
-        quant(1)
-        proj(0, "bank5")
-        proj(1, "bank6")
-        fin(3, rounded)
-        fin(4, rounded)
-        quant(3)
-        fin(2, rounded)
-        quant(4)
-        quant(2)
-        proj(3, "bank0")
-        proj(4, "bank1")
-        proj(2, "bank7")
+        pieces = list(zip(MASK_PIECES, MASK_PIECES[1:]))
+        for j0, j1 in pieces:
+            mask(j0, j1)
+        for r in range(PACK):
+            gather(picked_m[:, r, :], r, 0, MASKED, gate_sb[:, :MASKED])
+        make_factor()
+        for r in range(PACK):
+            gather(picked_f[:, r, :], r, MASKED, S, factor[:, r, :])
+        rounded = keep.tile([P, MASKED, PACK], BF16, name="rounded", tag="staged")
+        nc.scalar.copy(interleaved(rounded[:]), planes(picked_m[:]))
+        f0, f1, f2 = FUSED_PIECES
+        for j0, j1 in ((f0, f1), (f1, f2)):
+            nc.scalar.copy(interleaved(da[:, j0:j1, :]), planes(picked_f[:, :, j0 - MASKED : j1 - MASKED]))
+        dx = keep.tile([P, S], F32, name="dx", tag="late")
+        apply_mask(rounded, *pieces[0])
+        apply_mask(rounded, *pieces[1])
+        quant(*pieces[0])
+        proj(dx, *pieces[0], "bank0", nc.scalar.copy)
+        apply_mask(rounded, *pieces[2])
+        quant(*pieces[1])
+        proj(dx, *pieces[1], "bank1", nc.scalar.copy)
+        quant(*pieces[2])
+        proj(dx, *pieces[2], "bank7", nc.scalar.copy)
+        quant(f0, f1)
+        proj(dx, f0, f1, "bank5", nc.scalar.copy)
+        quant(f1, f2)
+        proj(dx, f1, f2, "bank6", nc.vector.tensor_copy)
 
         first = keep.tile([P, T], F32, name="first")
-        second = keep.tile([P, T], F32, name="second")
         result = keep.tile([P, T], F32, name="result")
-
-        def fetch(dst, lists, h):
-            t0, t1 = PARTS[h], PARTS[h + 1]
-            nc.vector.tensor_copy(dst[:, t0:t1], dx[:].indirect(lists[:, t0 // 16 : t1 // 16]))
-
-        def combine(h, engine):
-            t0, t1 = PARTS[h], PARTS[h + 1]
-            engine.tensor_tensor(result[:, t0:t1], first[:, t0:t1], second[:, t0:t1], ALU.add)
+        parts = list(zip(PARTS, PARTS[1:]))
+        for t0, t1 in parts:
+            nc.vector.tensor_copy(first[:, t0:t1], dx[:].indirect(pos1_sb[:, t0 // 16 : t1 // 16]))
+        for t0, t1 in parts:
+            nc.vector.tensor_tensor(
+                result[:, t0:t1], dx[:].indirect(pos2_sb[:, t0 // 16 : t1 // 16]), first[:, t0:t1], ALU.add
+            )
             nc.sync.dma_start(out[:, t0:t1], result[:, t0:t1])
-
-        fetch(first, pos1_sb, 0)
-        fetch(second, pos2_sb, 0)
-        combine(0, nc.gpsimd)
-        fetch(first, pos1_sb, 1)
-        fetch(second, pos2_sb, 1)
-        fetch(first, pos1_sb, 2)
-        fetch(second, pos2_sb, 2)
-        combine(1, nc.vector)
-        combine(2, nc.vector)

@@ -100,14 +100,13 @@ def tile_moe_sdb_relu_kernel(
                 )
 
         load_dy_scales(nc.sync, 0)
-        load_w2_scales(nc.sync, 0)
-        load_w2_scales(nc.sync, 1)
+        load_dy_scales(nc.sync, 1)
+        load_dy_scales(nc.sync, 2)
         load_w2(nc.sync)
+        for q in range(4):
+            load_w2_scales(nc.sync, q)
         load_dy(nc.sync, 0, HALF)
-        load_w2_scales(nc.sync, 2)
-        load_w2_scales(nc.sync, 3)
-        for q in range(1, 4):
-            load_dy_scales(nc.sync, q)
+        load_dy_scales(nc.sync, 3)
         load_dy(nc.sync, HALF, T)
         load_gate(0, MASKED)
         nc.sync.dma_start(offs_sb[:], offs)
@@ -224,10 +223,10 @@ def tile_moe_sdb_relu_kernel(
         apply_mask(rounded, *pieces[2])
         quant(*pieces[1])
         proj(dx, *pieces[1], "bank1", nc.scalar.copy)
-        quant(*pieces[2])
-        proj(dx, *pieces[2], "bank7", nc.scalar.copy)
         quant(f0, f1)
         proj(dx, f0, f1, "bank5", nc.scalar.copy)
+        quant(*pieces[2])
+        proj(dx, *pieces[2], "bank7", nc.scalar.copy)
         quant(f1, f2)
         proj(dx, f1, f2, "bank6", nc.vector.tensor_copy)
 

@@ -1,6 +1,7 @@
 from contextlib import ExitStack
 
 import concourse.mybir as mybir
+from concourse.masks import make_identity
 
 K, T, E, C, H, N = 128, 512, 8, 128, 512, 1024
 S = E * C
@@ -23,6 +24,8 @@ MASKED = 640
 FUSED = S - MASKED
 PAD = MASKED + 32 - T
 MASK_PIECES = (0, 256, 512, MASKED)
+EARLY = 128
+RUN = S // P
 FUSED_PIECES = (MASKED, MASKED + 256, S)
 PARTS = (0, 384, T)
 
@@ -49,18 +52,21 @@ def tile_moe_sdb_relu_kernel(
         dy_planes = keep.tile([P, PASSES, T], U8, name="dy_planes", align_bytes=64)
         w1_scales = keep.tile([P, E, K], U8, name="w1_scales", align_bytes=64)
         gate_sb = keep.tile([P, S], F32, name="gate_sb")
+        gate_cols = keep.tile([P, RUN], F32, name="gate_cols")
+        identity = keep.tile([P, P], F32, name="identity")
+        acts_early = keep.tile([P, PACK, EARLY], F32, name="acts_early", tag="wide", align_bytes=64)
         acts = keep.tile([P, PACK, S], F32, name="acts")
-        picked_m = keep.tile([P, PACK, MASKED], F32, name="picked_m", tag="wide")
         picked_f = keep.tile([P, PACK, FUSED], F32, name="picked_f", tag="late")
         factor = keep.tile([P, PACK, FUSED], F32, name="factor")
         dc = [keep.tile([P, T + PAD], F32, name=f"dc{r}") for r in range(PACK)]
         signs = keep.tile([P, MASKED, PACK], BF16, name="signs", tag="staged")
         passed = keep.tile([P, MASKED, PACK], BF16, name="passed")
-        da = keep.tile([P, S, PACK], BF16, name="da", align_bytes=64)
+        da = keep.tile([P, MASKED, PACK], BF16, name="da", align_bytes=64)
         da_codes = keep.tile([P, S], I32, name="da_codes", align_bytes=64)
         da_scales = keep.tile([P, S], U8, name="da_scales", align_bytes=64)
 
         nc.gpsimd.memset(w2_scales_raw[:].bitcast(I32), 0)
+        make_identity(nc, identity[:])
         for r in range(PACK):
             nc.gpsimd.memset(dc[r][:, T:], 0.0)
 
@@ -85,8 +91,8 @@ def tile_moe_sdb_relu_kernel(
         def load_dy(queue, t0, t1):
             queue.dma_start(dy_codes[:, :, t0:t1], dy_rows[:, :, t0:t1])
 
-        def load_gate(j0, j1):
-            nc.sync.dma_start(gate_sb[:, j0:j1], gate[:, j0:j1])
+        def load_gate():
+            nc.sync.dma_start(gate_cols[:], gate[0, :].rearrange("(n c) -> n c", c=RUN))
 
         def load_acts(j0, j1):
             nc.sync.dma_start(acts[:, :, j0:j1], a_rows[:, :, j0:j1])
@@ -99,6 +105,7 @@ def tile_moe_sdb_relu_kernel(
                     w1t_scales[:, 0, 4 * q : 4 * q + 4, :].rearrange("e b k -> b e k").bitcast(I32),
                 )
 
+        load_gate()
         load_dy_scales(nc.sync, 0)
         load_dy_scales(nc.sync, 1)
         load_dy_scales(nc.sync, 2)
@@ -108,15 +115,24 @@ def tile_moe_sdb_relu_kernel(
         load_dy(nc.sync, 0, HALF)
         load_dy_scales(nc.sync, 3)
         load_dy(nc.sync, HALF, T)
-        load_gate(0, MASKED)
+        nc.sync.dma_start(acts_early[:], a_rows[:, :, MASKED : MASKED + EARLY])
         nc.sync.dma_start(offs_sb[:], offs)
         load_acts(0, 256)
         load_acts(256, MASKED)
-        load_gate(MASKED, S)
-        load_acts(MASKED, S)
+        load_acts(MASKED + EARLY, S)
         load_w1(nc.sync)
         nc.sync.dma_start(pos1_sb[:], pos1)
         nc.sync.dma_start(pos2_sb[:], pos2)
+
+        for h in range(RUN // 4):
+            spread = psum.tile([P, 4, P], F32, name=f"spread{h}", tag=f"bank{5 + h}")
+            for c in range(4):
+                column = gate_cols[:, 4 * h + c : 4 * h + c + 1]
+                nc.tensor.transpose(spread[:, c, :], column.to_broadcast([P, P]), identity[:])
+            nc.scalar.copy(
+                gate_sb[:].rearrange("p (n h c) -> p n h c", h=RUN // 4, c=4)[:, :, h, :],
+                spread[:].rearrange("p c n -> p n c"),
+            )
 
         def sort_words(dst, rows):
             nc.vector.tensor_copy(
@@ -161,9 +177,8 @@ def tile_moe_sdb_relu_kernel(
         def planes(ap):
             return ap.rearrange("p r (c i) -> p c r i", i=4)
 
-        def mask(j0, j1):
+        def sign(j0, j1):
             nc.scalar.activation(interleaved(signs[:, j0:j1, :]), planes(acts[:, :, j0:j1]), ACT.Sign)
-            nc.scalar.activation(passed[:, j0:j1, :], signs[:, j0:j1, :], ACT.Relu)
 
         def gather(dst, r, j0, j1, other):
             nc.vector.tensor_tensor(dst, dc[r][:].indirect(offs_sb[:, j0 // 16 : j1 // 16]), other, ALU.mult)
@@ -171,24 +186,24 @@ def tile_moe_sdb_relu_kernel(
         def apply_mask(rounded, j0, j1):
             nc.vector.tensor_tensor(da[:, j0:j1, :], rounded[:, j0:j1, :], passed[:, j0:j1, :], ALU.mult)
 
-        def make_factor():
+        def make_factor(src, j0, j1):
             nc.vector.scalar_tensor_tensor(
-                factor[:],
-                acts[:, :, MASKED:],
+                factor[:, :, j0 - MASKED : j1 - MASKED],
+                src,
                 0.0,
-                gate_sb[:, MASKED:].unsqueeze(1).to_broadcast([P, PACK, FUSED]),
+                gate_sb[:, j0:j1].unsqueeze(1).to_broadcast([P, PACK, j1 - j0]),
                 ALU.is_gt,
                 ALU.mult,
             )
 
-        def quant(j0, j1):
+        def quant(j0, j1, src):
             nc.vector.quantize_mx(
                 out=da_codes[:, j0:j1].bitcast(FP8X4),
                 scales=da_scales[:, j0:j1],
-                in_=da[:, j0:j1, :].rearrange("p j r -> p (j r)"),
+                in_=src.rearrange("p j r -> p (j r)"),
             )
 
-        def proj(dx, j0, j1, tag, copy):
+        def proj(j0, j1, tag):
             bank = psum.tile([P, j1 - j0], F32, name=f"dx_bank{j0}", tag=tag)
             for e in range(j0 // C, j1 // C):
                 nc.tensor.matmul_mx(
@@ -200,35 +215,42 @@ def tile_moe_sdb_relu_kernel(
                     start=True,
                     stop=True,
                 )
-            copy(dx[:, j0:j1], bank[:])
+            return bank
 
         pieces = list(zip(MASK_PIECES, MASK_PIECES[1:]))
-        for j0, j1 in pieces:
-            mask(j0, j1)
+        sign(0, 256)
+        sign(256, MASKED)
+        nc.scalar.activation(passed[:], signs[:], ACT.Relu)
+        make_factor(acts_early[:], MASKED, MASKED + EARLY)
+        picked_m = keep.tile([P, PACK, MASKED], F32, name="picked_m", tag="wide", align_bytes=64)
         for r in range(PACK):
             gather(picked_m[:, r, :], r, 0, MASKED, gate_sb[:, :MASKED])
-        make_factor()
+        make_factor(acts[:, :, MASKED + EARLY :], MASKED + EARLY, S)
         for r in range(PACK):
             gather(picked_f[:, r, :], r, MASKED, S, factor[:, r, :])
         rounded = keep.tile([P, MASKED, PACK], BF16, name="rounded", tag="staged")
         nc.scalar.copy(interleaved(rounded[:]), planes(picked_m[:]))
         f0, f1, f2 = FUSED_PIECES
+        da_f = keep.tile([P, FUSED, PACK], BF16, name="da_f", tag="wide", align_bytes=64)
         for j0, j1 in ((f0, f1), (f1, f2)):
-            nc.scalar.copy(interleaved(da[:, j0:j1, :]), planes(picked_f[:, :, j0 - MASKED : j1 - MASKED]))
+            nc.scalar.copy(interleaved(da_f[:, j0 - MASKED : j1 - MASKED, :]), planes(picked_f[:, :, j0 - MASKED : j1 - MASKED]))
         dx = keep.tile([P, S], F32, name="dx", tag="late")
-        apply_mask(rounded, *pieces[0])
-        apply_mask(rounded, *pieces[1])
-        quant(*pieces[0])
-        proj(dx, *pieces[0], "bank0", nc.scalar.copy)
-        apply_mask(rounded, *pieces[2])
-        quant(*pieces[1])
-        proj(dx, *pieces[1], "bank1", nc.scalar.copy)
-        quant(f0, f1)
-        proj(dx, f0, f1, "bank5", nc.scalar.copy)
-        quant(*pieces[2])
-        proj(dx, *pieces[2], "bank7", nc.scalar.copy)
-        quant(f1, f2)
-        proj(dx, f1, f2, "bank6", nc.vector.tensor_copy)
+        (a0, a1), (b0, b1), (c0, c1) = pieces
+        apply_mask(rounded, a0, a1)
+        apply_mask(rounded, b0, b1)
+        quant(a0, a1, da[:, a0:a1, :])
+        nc.scalar.copy(dx[:, a0:a1], proj(a0, a1, "bank0")[:])
+        apply_mask(rounded, c0, c1)
+        quant(b0, b1, da[:, b0:b1, :])
+        nc.scalar.copy(dx[:, b0:b1], proj(b0, b1, "bank1")[:])
+        quant(f0, f1, da_f[:, : f1 - f0, :])
+        nc.scalar.copy(dx[:, f0:f1], proj(f0, f1, "bank5")[:])
+        quant(c0, c1, da[:, c0:c1, :])
+        bank_c = proj(c0, c1, "bank7")
+        quant(f1, f2, da_f[:, f1 - f0 :, :])
+        bank_f = proj(f1, f2, "bank6")
+        nc.vector.tensor_copy(dx[:, c0:c1], bank_c[:])
+        nc.vector.tensor_copy(dx[:, f1:f2], bank_f[:])
 
         first = keep.tile([P, T], F32, name="first")
         result = keep.tile([P, T], F32, name="result")

@@ -19,12 +19,11 @@ ACT = mybir.ActivationFunctionType
 P = 128
 PACK = 4
 PASSES = N // (P * PACK)
-HALF = T // 2
+FIRST = 256
 MASKED = 640
 FUSED = S - MASKED
 PAD = MASKED + 32 - T
 MASK_PIECES = (0, 256, 512, MASKED)
-EARLY = 128
 RUN = S // P
 FUSED_PIECES = (MASKED, MASKED + 256, S)
 PARTS = (0, 384, T)
@@ -51,15 +50,16 @@ def tile_moe_sdb_relu_kernel(
         w2_scales = keep.tile([P, PACK, P], U8, name="w2_scales", align_bytes=64)
         dy_planes = keep.tile([P, PASSES, T], U8, name="dy_planes", align_bytes=64)
         w1_scales = keep.tile([P, E, K], U8, name="w1_scales", align_bytes=64)
-        gate_sb = keep.tile([P, S], F32, name="gate_sb")
+        gate_sb = keep.tile([P, S + FUSED], F32, name="gate_sb")
         gate_cols = keep.tile([P, RUN], F32, name="gate_cols")
         identity = keep.tile([P, P], F32, name="identity")
-        acts_early = keep.tile([P, PACK, EARLY], F32, name="acts_early", tag="wide", align_bytes=64)
-        acts = keep.tile([P, PACK, S], F32, name="acts")
-        picked_f = keep.tile([P, PACK, FUSED], F32, name="picked_f", tag="late")
-        factor = keep.tile([P, PACK, FUSED], F32, name="factor")
-        dc = [keep.tile([P, T + PAD], F32, name=f"dc{r}") for r in range(PACK)]
-        signs = keep.tile([P, MASKED, PACK], BF16, name="signs", tag="staged")
+        acts_early = keep.tile([P, FUSED], F32, name="acts_early", tag="wide")
+        acts_first = keep.tile([P, PACK, 256], F32, name="acts_first", tag="held")
+        acts = keep.tile([P, PACK, MASKED - 256], F32, name="acts")
+        acts_late = keep.tile([P, PACK - 1, FUSED], F32, name="acts_late")
+        factor = keep.tile([P, PACK - 1, FUSED], F32, name="factor")
+        dc = {r: keep.tile([P, S + 32 if r == 0 else T + PAD], F32, name=f"dc{r}") for r in (0, 1, 3)}
+        signs = keep.tile([P, MASKED, PACK], BF16, name="signs", tag="staged", align_bytes=64)
         passed = keep.tile([P, MASKED, PACK], BF16, name="passed")
         da = keep.tile([P, MASKED, PACK], BF16, name="da", align_bytes=64)
         da_codes = keep.tile([P, S], I32, name="da_codes", align_bytes=64)
@@ -67,7 +67,8 @@ def tile_moe_sdb_relu_kernel(
 
         nc.gpsimd.memset(w2_scales_raw[:].bitcast(I32), 0)
         make_identity(nc, identity[:])
-        for r in range(PACK):
+        nc.vector.memset(dc[0][:, T:], 0.0)
+        for r in (1, 3):
             nc.gpsimd.memset(dc[r][:, T:], 0.0)
 
         a_rows = a.rearrange("(p r) j -> p r j", r=PACK)
@@ -95,7 +96,7 @@ def tile_moe_sdb_relu_kernel(
             nc.sync.dma_start(gate_cols[:], gate[0, :].rearrange("(n c) -> n c", c=RUN))
 
         def load_acts(j0, j1):
-            nc.sync.dma_start(acts[:, :, j0:j1], a_rows[:, :, j0:j1])
+            nc.sync.dma_start(acts[:, :, j0 - 256 : j1 - 256], a_rows[:, :, j0:j1])
 
         def load_w1(queue):
             queue.dma_start(w1_codes[:], w1t_words.rearrange("e o p k d -> p (e o) (k d)").bitcast(I32))
@@ -112,27 +113,33 @@ def tile_moe_sdb_relu_kernel(
         load_w2(nc.sync)
         for q in range(4):
             load_w2_scales(nc.sync, q)
-        load_dy(nc.sync, 0, HALF)
+        load_dy(nc.sync, 0, FIRST)
         load_dy_scales(nc.sync, 3)
-        load_dy(nc.sync, HALF, T)
-        nc.sync.dma_start(acts_early[:], a_rows[:, :, MASKED : MASKED + EARLY])
+        load_dy(nc.sync, FIRST, T)
+        nc.sync.dma_start(acts_early[:], a_rows[:, 0, MASKED:])
         nc.sync.dma_start(offs_sb[:], offs)
-        load_acts(0, 256)
+        nc.sync.dma_start(acts_first[:], a_rows[:, :, :256])
         load_acts(256, MASKED)
-        load_acts(MASKED + EARLY, S)
+        nc.sync.dma_start(acts_late[:], a_rows[:, 1:, MASKED:])
         load_w1(nc.sync)
         nc.sync.dma_start(pos1_sb[:], pos1)
         nc.sync.dma_start(pos2_sb[:], pos2)
 
+        gate_m = gate_sb[:, :MASKED]
+        gate_f = gate_sb[:, S:]
+        spreads = []
         for h in range(RUN // 4):
             spread = psum.tile([P, 4, P], F32, name=f"spread{h}", tag=f"bank{5 + h}")
             for c in range(4):
                 column = gate_cols[:, 4 * h + c : 4 * h + c + 1]
                 nc.tensor.transpose(spread[:, c, :], column.to_broadcast([P, P]), identity[:])
-            nc.scalar.copy(
-                gate_sb[:].rearrange("p (n h c) -> p n h c", h=RUN // 4, c=4)[:, :, h, :],
-                spread[:].rearrange("p c n -> p n c"),
-            )
+            spreads.append(spread)
+        for dst, rows in ((gate_f, slice(MASKED // RUN, P)), (gate_m, slice(0, MASKED // RUN))):
+            for h in range(RUN // 4):
+                nc.scalar.copy(
+                    dst.rearrange("p (n h c) -> p n h c", h=RUN // 4, c=4)[:, :, h, :],
+                    spreads[h][:].rearrange("p c n -> p n c")[:, rows, :],
+                )
 
         def sort_words(dst, rows):
             nc.vector.tensor_copy(
@@ -152,24 +159,25 @@ def tile_moe_sdb_relu_kernel(
         sort_words(w2_rest, slice(1, PACK))
         w2_codes = [w2_first[:, 0, :, :]] + [w2_rest[:, r, :, :] for r in range(PACK - 1)]
 
-        def hidden(r, tokens, tag):
-            bank = psum.tile([P, tokens.stop - tokens.start], F32, name=f"dc_bank{r}_{tokens.start}", tag=tag)
-            for s in range(PASSES):
-                nc.tensor.matmul_mx(
-                    out=bank[:],
-                    lhsT=w2_codes[r][:, s, :].bitcast(FP8X4),
-                    lhsT_scale=w2_scales[4 * s :, r, :],
-                    rhs=dy_codes[:, s, tokens].bitcast(FP8X4),
-                    rhs_scale=dy_planes[:, s, tokens],
-                    start=(s == 0),
-                    stop=(s == PASSES - 1),
-                )
-            nc.scalar.copy(dc[r][:, tokens], bank[:])
+        def hidden(r, cuts, tag):
+            t0, t1 = cuts[0], cuts[-1]
+            bank = psum.tile([P, t1 - t0], F32, name=f"dc_bank{r}_{t0}", tag=tag)
+            for u0, u1 in zip(cuts, cuts[1:]):
+                for s in range(PASSES):
+                    nc.tensor.matmul_mx(
+                        out=bank[:, u0 - t0 : u1 - t0],
+                        lhsT=w2_codes[r][:, s, :].bitcast(FP8X4),
+                        lhsT_scale=w2_scales[4 * s :, r, :],
+                        rhs=dy_codes[:, s, u0:u1].bitcast(FP8X4),
+                        rhs_scale=dy_planes[:, s, u0:u1],
+                        start=(s == 0),
+                        stop=(s == PASSES - 1),
+                    )
+            nc.scalar.copy(dc[r][:, t0:t1], bank[:])
 
-        hidden(0, slice(0, HALF), "bank0")
-        hidden(0, slice(HALF, T), "bank1")
-        for r in range(1, PACK):
-            hidden(r, slice(0, T), f"bank{r + 1}")
+        hidden(0, (0, FIRST), "bank0")
+        hidden(0, (FIRST, T), "bank1")
+        hidden(1, (0, T), "bank2")
 
         def interleaved(ap):
             return ap.rearrange("p (c i) r -> p c r i", i=4)
@@ -177,8 +185,8 @@ def tile_moe_sdb_relu_kernel(
         def planes(ap):
             return ap.rearrange("p r (c i) -> p c r i", i=4)
 
-        def sign(j0, j1):
-            nc.scalar.activation(interleaved(signs[:, j0:j1, :]), planes(acts[:, :, j0:j1]), ACT.Sign)
+        def sign(j0, j1, src):
+            nc.scalar.activation(interleaved(signs[:, j0:j1, :]), planes(src), ACT.Sign)
 
         def gather(dst, r, j0, j1, other):
             nc.vector.tensor_tensor(dst, dc[r][:].indirect(offs_sb[:, j0 // 16 : j1 // 16]), other, ALU.mult)
@@ -186,15 +194,8 @@ def tile_moe_sdb_relu_kernel(
         def apply_mask(rounded, j0, j1):
             nc.vector.tensor_tensor(da[:, j0:j1, :], rounded[:, j0:j1, :], passed[:, j0:j1, :], ALU.mult)
 
-        def make_factor(src, j0, j1):
-            nc.vector.scalar_tensor_tensor(
-                factor[:, :, j0 - MASKED : j1 - MASKED],
-                src,
-                0.0,
-                gate_sb[:, j0:j1].unsqueeze(1).to_broadcast([P, PACK, j1 - j0]),
-                ALU.is_gt,
-                ALU.mult,
-            )
+        def make_factor(dst, src, weights):
+            nc.vector.scalar_tensor_tensor(dst, src, 0.0, weights, ALU.is_gt, ALU.mult)
 
         def quant(j0, j1, src):
             nc.vector.quantize_mx(
@@ -218,23 +219,26 @@ def tile_moe_sdb_relu_kernel(
             return bank
 
         pieces = list(zip(MASK_PIECES, MASK_PIECES[1:]))
-        sign(0, 256)
-        sign(256, MASKED)
+        sign(0, 256, acts_first[:])
+        dc[2] = keep.tile([P, T + PAD], F32, name="dc2", tag="held")
+        nc.gpsimd.memset(dc[2][:, T:], 0.0)
+        for r in (2, 3):
+            hidden(r, (0, T), f"bank{r + 1}")
+        sign(256, MASKED, acts[:])
         nc.scalar.activation(passed[:], signs[:], ACT.Relu)
-        make_factor(acts_early[:], MASKED, MASKED + EARLY)
-        picked_m = keep.tile([P, PACK, MASKED], F32, name="picked_m", tag="wide", align_bytes=64)
-        for r in range(PACK):
-            gather(picked_m[:, r, :], r, 0, MASKED, gate_sb[:, :MASKED])
-        make_factor(acts[:, :, MASKED + EARLY :], MASKED + EARLY, S)
-        for r in range(PACK):
-            gather(picked_f[:, r, :], r, MASKED, S, factor[:, r, :])
-        rounded = keep.tile([P, MASKED, PACK], BF16, name="rounded", tag="staged")
-        nc.scalar.copy(interleaved(rounded[:]), planes(picked_m[:]))
+        make_factor(gate_sb[:, MASKED:S], acts_early[:], gate_f)
+        picked = keep.tile([P, PACK, S], F32, name="picked", tag="wide")
+        gather(picked[:, 0, :], 0, 0, S, gate_sb[:, :S])
+        for r in range(1, PACK):
+            gather(picked[:, r, :MASKED], r, 0, MASKED, gate_m)
+        make_factor(factor[:], acts_late[:], gate_f.unsqueeze(1).to_broadcast([P, PACK - 1, FUSED]))
+        for r in range(1, PACK):
+            gather(picked[:, r, MASKED:], r, MASKED, S, factor[:, r - 1, :])
+        rounded = keep.tile([P, S, PACK], BF16, name="rounded", tag="staged", align_bytes=64)
         f0, f1, f2 = FUSED_PIECES
-        da_f = keep.tile([P, FUSED, PACK], BF16, name="da_f", tag="wide", align_bytes=64)
-        for j0, j1 in ((f0, f1), (f1, f2)):
-            nc.scalar.copy(interleaved(da_f[:, j0 - MASKED : j1 - MASKED, :]), planes(picked_f[:, :, j0 - MASKED : j1 - MASKED]))
-        dx = keep.tile([P, S], F32, name="dx", tag="late")
+        for j0, j1 in ((0, f0), (f0, f1), (f1, f2)):
+            nc.scalar.copy(interleaved(rounded[:, j0:j1, :]), planes(picked[:, :, j0:j1]))
+        dx = keep.tile([P, S], F32, name="dx", tag="wide")
         (a0, a1), (b0, b1), (c0, c1) = pieces
         apply_mask(rounded, a0, a1)
         apply_mask(rounded, b0, b1)
@@ -243,11 +247,11 @@ def tile_moe_sdb_relu_kernel(
         apply_mask(rounded, c0, c1)
         quant(b0, b1, da[:, b0:b1, :])
         nc.scalar.copy(dx[:, b0:b1], proj(b0, b1, "bank1")[:])
-        quant(f0, f1, da_f[:, : f1 - f0, :])
+        quant(f0, f1, rounded[:, f0:f1, :])
         nc.scalar.copy(dx[:, f0:f1], proj(f0, f1, "bank5")[:])
         quant(c0, c1, da[:, c0:c1, :])
         bank_c = proj(c0, c1, "bank7")
-        quant(f1, f2, da_f[:, f1 - f0 :, :])
+        quant(f1, f2, rounded[:, f1:f2, :])
         bank_f = proj(f1, f2, "bank6")
         nc.vector.tensor_copy(dx[:, c0:c1], bank_c[:])
         nc.vector.tensor_copy(dx[:, f1:f2], bank_f[:])

@@ -1,7 +1,6 @@
 from contextlib import ExitStack
 
 import concourse.mybir as mybir
-from concourse.masks import make_identity
 
 K, T, E, C, H, N = 128, 512, 8, 128, 512, 1024
 S = E * C
@@ -53,11 +52,12 @@ def tile_moe_sdb_relu_kernel(
         gate_sb = keep.tile([P, S + FUSED], F32, name="gate_sb")
         gate_cols = keep.tile([P, RUN], F32, name="gate_cols")
         identity = keep.tile([P, P], F32, name="identity")
-        acts_early = keep.tile([P, FUSED], F32, name="acts_early", tag="wide")
         acts_first = keep.tile([P, PACK, 256], F32, name="acts_first", tag="held")
         acts = keep.tile([P, PACK, MASKED - 256], F32, name="acts")
-        acts_late = keep.tile([P, PACK - 1, FUSED], F32, name="acts_late")
-        factor = keep.tile([P, PACK - 1, FUSED], F32, name="factor")
+        acts_second = keep.tile([P, FUSED], F32, name="acts_second")
+        acts_late = keep.tile([P, PACK - 2, FUSED], F32, name="acts_late")
+        factor_second = keep.tile([P, FUSED], F32, name="factor_second")
+        factor = keep.tile([P, PACK - 2, FUSED], F32, name="factor")
         dc = {r: keep.tile([P, S + 32 if r == 0 else T + PAD], F32, name=f"dc{r}") for r in (0, 1, 3)}
         signs = keep.tile([P, MASKED, PACK], BF16, name="signs", tag="staged", align_bytes=64)
         passed = keep.tile([P, MASKED, PACK], BF16, name="passed")
@@ -65,13 +65,19 @@ def tile_moe_sdb_relu_kernel(
         da_codes = keep.tile([P, S], I32, name="da_codes", align_bytes=64)
         da_scales = keep.tile([P, S], U8, name="da_scales", align_bytes=64)
 
+        a_rows = a.rearrange("(p r) j -> p r j", r=PACK)
         nc.gpsimd.memset(w2_scales_raw[:].bitcast(I32), 0)
-        make_identity(nc, identity[:])
+        zeros = keep.tile([P, P], F32, name="zeros", tag="wide")
+        nc.gpsimd.memset(zeros[:], 0.0)
+        nc.gpsimd.affine_select(
+            out=identity[:], in_=zeros[:], compare_op=ALU.not_equal, fill=1.0, base=0, pattern=[[-1, P]], channel_multiplier=1
+        )
+        acts_early = keep.tile([P, FUSED], F32, name="acts_early", tag="wide")
+        nc.gpsimd.dma_start(acts_early[:], a_rows[:, 0, MASKED:])
         nc.vector.memset(dc[0][:, T:], 0.0)
         for r in (1, 3):
             nc.gpsimd.memset(dc[r][:, T:], 0.0)
 
-        a_rows = a.rearrange("(p r) j -> p r j", r=PACK)
         dy_rows = dy_words.rearrange("s p t d -> p s (t d)").bitcast(I32)
 
         def load_dy_scales(queue, q):
@@ -116,11 +122,11 @@ def tile_moe_sdb_relu_kernel(
         load_dy(nc.sync, 0, FIRST)
         load_dy_scales(nc.sync, 3)
         load_dy(nc.sync, FIRST, T)
-        nc.sync.dma_start(acts_early[:], a_rows[:, 0, MASKED:])
+        nc.sync.dma_start(acts_second[:], a_rows[:, PACK - 1, MASKED:])
         nc.sync.dma_start(offs_sb[:], offs)
         nc.sync.dma_start(acts_first[:], a_rows[:, :, :256])
         load_acts(256, MASKED)
-        nc.sync.dma_start(acts_late[:], a_rows[:, 1:, MASKED:])
+        nc.sync.dma_start(acts_late[:], a_rows[:, 1 : PACK - 1, MASKED:])
         load_w1(nc.sync)
         nc.sync.dma_start(pos1_sb[:], pos1)
         nc.sync.dma_start(pos2_sb[:], pos2)
@@ -227,12 +233,14 @@ def tile_moe_sdb_relu_kernel(
         sign(256, MASKED, acts[:])
         nc.scalar.activation(passed[:], signs[:], ACT.Relu)
         make_factor(gate_sb[:, MASKED:S], acts_early[:], gate_f)
+        make_factor(factor_second[:], acts_second[:], gate_f)
         picked = keep.tile([P, PACK, S], F32, name="picked", tag="wide")
         gather(picked[:, 0, :], 0, 0, S, gate_sb[:, :S])
         for r in range(1, PACK):
             gather(picked[:, r, :MASKED], r, 0, MASKED, gate_m)
-        make_factor(factor[:], acts_late[:], gate_f.unsqueeze(1).to_broadcast([P, PACK - 1, FUSED]))
-        for r in range(1, PACK):
+        make_factor(factor[:], acts_late[:], gate_f.unsqueeze(1).to_broadcast([P, PACK - 2, FUSED]))
+        gather(picked[:, PACK - 1, MASKED:], PACK - 1, MASKED, S, factor_second[:])
+        for r in range(1, PACK - 1):
             gather(picked[:, r, MASKED:], r, MASKED, S, factor[:, r - 1, :])
         rounded = keep.tile([P, S, PACK], BF16, name="rounded", tag="staged", align_bytes=64)
         f0, f1, f2 = FUSED_PIECES
@@ -254,7 +262,7 @@ def tile_moe_sdb_relu_kernel(
         quant(f1, f2, rounded[:, f1:f2, :])
         bank_f = proj(f1, f2, "bank6")
         nc.vector.tensor_copy(dx[:, c0:c1], bank_c[:])
-        nc.vector.tensor_copy(dx[:, f1:f2], bank_f[:])
+        nc.scalar.copy(dx[:, f1:f2], bank_f[:])
 
         first = keep.tile([P, T], F32, name="first")
         result = keep.tile([P, T], F32, name="result")

@@ -19,12 +19,12 @@ P = 128
 PACK = 4
 PASSES = N // (P * PACK)
 FIRST = 256
-MASKED = 640
+MASKED = 512
 FUSED = S - MASKED
 PAD = MASKED + 32 - T
-MASK_PIECES = (0, 256, 512, MASKED)
+MASK_PIECES = (0, 256, MASKED)
 RUN = S // P
-FUSED_PIECES = (MASKED, MASKED + 256, S)
+FUSED_PIECES = (MASKED, MASKED + 256, S - C, S)
 PARTS = (0, 384, T)
 
 
@@ -57,7 +57,6 @@ def tile_moe_sdb_relu_kernel(
         acts_second = keep.tile([P, FUSED], F32, name="acts_second")
         acts_late = keep.tile([P, PACK - 2, FUSED], F32, name="acts_late")
         factor_second = keep.tile([P, FUSED], F32, name="factor_second")
-        factor = keep.tile([P, PACK - 2, FUSED], F32, name="factor")
         dc = {r: keep.tile([P, S + 32 if r == 0 else T + PAD], F32, name=f"dc{r}") for r in (0, 1, 3)}
         signs = keep.tile([P, MASKED, PACK], BF16, name="signs", tag="staged", align_bytes=64)
         passed = keep.tile([P, MASKED, PACK], BF16, name="passed")
@@ -238,31 +237,34 @@ def tile_moe_sdb_relu_kernel(
         gather(picked[:, 0, :], 0, 0, S, gate_sb[:, :S])
         for r in range(1, PACK):
             gather(picked[:, r, :MASKED], r, 0, MASKED, gate_m)
-        make_factor(factor[:], acts_late[:], gate_f.unsqueeze(1).to_broadcast([P, PACK - 2, FUSED]))
-        gather(picked[:, PACK - 1, MASKED:], PACK - 1, MASKED, S, factor_second[:])
-        for r in range(1, PACK - 1):
-            gather(picked[:, r, MASKED:], r, MASKED, S, factor[:, r - 1, :])
+        factor = gate_sb[:, : (PACK - 2) * FUSED].rearrange("p (r j) -> p r j", j=FUSED)
+        mid = MASKED + 256
+        gather(picked[:, PACK - 1, MASKED:mid], PACK - 1, MASKED, mid, factor_second[:, :256])
+        make_factor(factor, acts_late[:], gate_f.unsqueeze(1).to_broadcast([P, PACK - 2, FUSED]))
+        gather(picked[:, PACK - 1, mid:], PACK - 1, mid, S, factor_second[:, 256:])
+        for j0, j1 in ((MASKED, mid), (mid, S)):
+            for r in range(1, PACK - 1):
+                gather(picked[:, r, j0:j1], r, j0, j1, factor[:, r - 1, j0 - MASKED : j1 - MASKED])
         rounded = keep.tile([P, S, PACK], BF16, name="rounded", tag="staged", align_bytes=64)
-        f0, f1, f2 = FUSED_PIECES
-        for j0, j1 in ((0, f0), (f0, f1), (f1, f2)):
+        f0, f1, f2, f3 = FUSED_PIECES
+        for j0, j1 in ((0, f0), (f0, f1), (f1, f3)):
             nc.scalar.copy(interleaved(rounded[:, j0:j1, :]), planes(picked[:, :, j0:j1]))
         dx = keep.tile([P, S], F32, name="dx", tag="wide")
-        (a0, a1), (b0, b1), (c0, c1) = pieces
+        (a0, a1), (b0, b1) = pieces
         apply_mask(rounded, a0, a1)
         apply_mask(rounded, b0, b1)
         quant(a0, a1, da[:, a0:a1, :])
         nc.scalar.copy(dx[:, a0:a1], proj(a0, a1, "bank0")[:])
-        apply_mask(rounded, c0, c1)
         quant(b0, b1, da[:, b0:b1, :])
         nc.scalar.copy(dx[:, b0:b1], proj(b0, b1, "bank1")[:])
         quant(f0, f1, rounded[:, f0:f1, :])
         nc.scalar.copy(dx[:, f0:f1], proj(f0, f1, "bank5")[:])
-        quant(c0, c1, da[:, c0:c1, :])
-        bank_c = proj(c0, c1, "bank7")
         quant(f1, f2, rounded[:, f1:f2, :])
-        bank_f = proj(f1, f2, "bank6")
-        nc.vector.tensor_copy(dx[:, c0:c1], bank_c[:])
-        nc.scalar.copy(dx[:, f1:f2], bank_f[:])
+        bank_c = proj(f1, f2, "bank7")
+        quant(f2, f3, rounded[:, f2:f3, :])
+        bank_f = proj(f2, f3, "bank6")
+        nc.vector.tensor_copy(dx[:, f1:f2], bank_c[:])
+        nc.scalar.copy(dx[:, f2:f3], bank_f[:])
 
         first = keep.tile([P, T], F32, name="first")
         result = keep.tile([P, T], F32, name="result")

@@ -23,7 +23,7 @@ MASKED = 512
 FUSED = S - MASKED
 PAD = MASKED + 32 - T
 MASK_PIECES = (0, 256, MASKED)
-RUN = S // P
+RUN = FUSED // P
 FUSED_PIECES = (MASKED, MASKED + 256, S - C, S)
 PARTS = (0, 384, T)
 
@@ -49,8 +49,8 @@ def tile_moe_sdb_relu_kernel(
         w2_scales = keep.tile([P, PACK, P], U8, name="w2_scales", align_bytes=64)
         dy_planes = keep.tile([P, PASSES, T], U8, name="dy_planes", align_bytes=64)
         w1_scales = keep.tile([P, E, K], U8, name="w1_scales", align_bytes=64)
-        gate_sb = keep.tile([P, S + FUSED], F32, name="gate_sb")
-        gate_cols = keep.tile([P, RUN], F32, name="gate_cols")
+        gate_sb = keep.tile([P, S], F32, name="gate_sb")
+        gate_cols = keep.tile([P, 2, 8], F32, name="gate_cols")
         identity = keep.tile([P, P], F32, name="identity")
         acts_first = keep.tile([P, PACK, 256], F32, name="acts_first", tag="held")
         acts = keep.tile([P, PACK, MASKED - 256], F32, name="acts")
@@ -98,7 +98,7 @@ def tile_moe_sdb_relu_kernel(
             queue.dma_start(dy_codes[:, :, t0:t1], dy_rows[:, :, t0:t1])
 
         def load_gate():
-            nc.sync.dma_start(gate_cols[:], gate[0, :].rearrange("(n c) -> n c", c=RUN))
+            nc.sync.dma_start(gate_cols[:, :, :RUN], gate[0, :].rearrange("(h n c) -> n h c", h=2, c=RUN))
 
         def load_acts(j0, j1):
             nc.sync.dma_start(acts[:, :, j0 - 256 : j1 - 256], a_rows[:, :, j0:j1])
@@ -131,20 +131,14 @@ def tile_moe_sdb_relu_kernel(
         nc.sync.dma_start(pos2_sb[:], pos2)
 
         gate_m = gate_sb[:, :MASKED]
-        gate_f = gate_sb[:, S:]
-        spreads = []
-        for h in range(RUN // 4):
-            spread = psum.tile([P, 4, P], F32, name=f"spread{h}", tag=f"bank{5 + h}")
-            for c in range(4):
-                column = gate_cols[:, 4 * h + c : 4 * h + c + 1]
+        spreads = {}
+        for h in (1, 0):
+            spread = psum.tile([P, RUN, P], F32, name=f"spread{h}", tag=f"bank{5 + h}")
+            for c in range(RUN):
+                column = gate_cols[:, h, c : c + 1]
                 nc.tensor.transpose(spread[:, c, :], column.to_broadcast([P, P]), identity[:])
-            spreads.append(spread)
-        for dst, rows in ((gate_f, slice(MASKED // RUN, P)), (gate_m, slice(0, MASKED // RUN))):
-            for h in range(RUN // 4):
-                nc.scalar.copy(
-                    dst.rearrange("p (n h c) -> p n h c", h=RUN // 4, c=4)[:, :, h, :],
-                    spreads[h][:].rearrange("p c n -> p n c")[:, rows, :],
-                )
+            spreads[h] = spread[:].rearrange("p c n -> p n c")
+        nc.scalar.copy(gate_m.rearrange("p (n c) -> p n c", c=RUN), spreads[0])
 
         def sort_words(dst, rows):
             nc.vector.tensor_copy(
@@ -199,8 +193,15 @@ def tile_moe_sdb_relu_kernel(
         def apply_mask(rounded, j0, j1):
             nc.vector.tensor_tensor(da[:, j0:j1, :], rounded[:, j0:j1, :], passed[:, j0:j1, :], ALU.mult)
 
-        def make_factor(dst, src, weights):
-            nc.vector.scalar_tensor_tensor(dst, src, 0.0, weights, ALU.is_gt, ALU.mult)
+        def make_factor(dst, src):
+            nc.vector.scalar_tensor_tensor(
+                dst.rearrange("p (n c) -> p n c", c=RUN),
+                src.rearrange("p (n c) -> p n c", c=RUN),
+                0.0,
+                spreads[1],
+                ALU.is_gt,
+                ALU.mult,
+            )
 
         def quant(j0, j1, src):
             nc.vector.quantize_mx(
@@ -231,8 +232,8 @@ def tile_moe_sdb_relu_kernel(
             hidden(r, (0, T), f"bank{r + 1}")
         sign(256, MASKED, acts[:])
         nc.scalar.activation(passed[:], signs[:], ACT.Relu)
-        make_factor(gate_sb[:, MASKED:S], acts_early[:], gate_f)
-        make_factor(factor_second[:], acts_second[:], gate_f)
+        make_factor(gate_sb[:, MASKED:S], acts_early[:])
+        make_factor(factor_second[:], acts_second[:])
         picked = keep.tile([P, PACK, S], F32, name="picked", tag="wide")
         gather(picked[:, 0, :], 0, 0, S, gate_sb[:, :S])
         for r in range(1, PACK):
@@ -240,7 +241,8 @@ def tile_moe_sdb_relu_kernel(
         factor = gate_sb[:, : (PACK - 2) * FUSED].rearrange("p (r j) -> p r j", j=FUSED)
         mid = MASKED + 256
         gather(picked[:, PACK - 1, MASKED:mid], PACK - 1, MASKED, mid, factor_second[:, :256])
-        make_factor(factor, acts_late[:], gate_f.unsqueeze(1).to_broadcast([P, PACK - 2, FUSED]))
+        for r in range(PACK - 2):
+            make_factor(factor[:, r, :], acts_late[:, r, :])
         gather(picked[:, PACK - 1, mid:], PACK - 1, mid, S, factor_second[:, 256:])
         for j0, j1 in ((MASKED, mid), (mid, S)):
             for r in range(1, PACK - 1):

@@ -19,12 +19,12 @@ P = 128
 PACK = 4
 PASSES = N // (P * PACK)
 FIRST = 256
-MASKED = 512
+MASKED = 576
 FUSED = S - MASKED
 PAD = MASKED + 32 - T
 MASK_PIECES = (0, 256, MASKED)
-RUN = FUSED // P
-FUSED_PIECES = (MASKED, MASKED + 256, S - C, S)
+RUN = 4
+FUSED_PIECES = (MASKED, 768, S - C, S)
 PARTS = (0, 384, T)
 
 
@@ -42,10 +42,10 @@ def tile_moe_sdb_relu_kernel(
         pos2_sb = keep.tile([P, T // 16], U16, name="pos2_sb")
 
         w2_raw = keep.tile([P, PASSES, H], I32, name="w2_raw", align_bytes=64)
-        w2_first = keep.tile([P, 1, PASSES, P], I32, name="w2_first", align_bytes=64)
+        w2_sorted = keep.tile([P, PACK, PASSES, P], I32, name="w2_sorted", align_bytes=64)
         dy_codes = keep.tile([P, PASSES, T], I32, name="dy_codes", align_bytes=64)
         w1_codes = keep.tile([P, E, K], I32, name="w1_codes", align_bytes=64)
-        w2_scales_raw = keep.tile([P, H], U8, name="w2_scales_raw", tag="sorted", align_bytes=64)
+        w2_scales_raw = keep.tile([P, H], U8, name="w2_scales_raw", align_bytes=64)
         w2_scales = keep.tile([P, PACK, P], U8, name="w2_scales", align_bytes=64)
         dy_planes = keep.tile([P, PASSES, T], U8, name="dy_planes", align_bytes=64)
         w1_scales = keep.tile([P, E, K], U8, name="w1_scales", align_bytes=64)
@@ -60,7 +60,6 @@ def tile_moe_sdb_relu_kernel(
         dc = {r: keep.tile([P, S + 32 if r == 0 else T + PAD], F32, name=f"dc{r}") for r in (0, 1, 3)}
         signs = keep.tile([P, MASKED, PACK], BF16, name="signs", tag="staged", align_bytes=64)
         passed = keep.tile([P, MASKED, PACK], BF16, name="passed")
-        da = keep.tile([P, MASKED, PACK], BF16, name="da", align_bytes=64)
         da_codes = keep.tile([P, S], I32, name="da_codes", align_bytes=64)
         da_scales = keep.tile([P, S], U8, name="da_scales", align_bytes=64)
 
@@ -138,7 +137,9 @@ def tile_moe_sdb_relu_kernel(
                 column = gate_cols[:, h, c : c + 1]
                 nc.tensor.transpose(spread[:, c, :], column.to_broadcast([P, P]), identity[:])
             spreads[h] = spread[:].rearrange("p c n -> p n c")
-        nc.scalar.copy(gate_m.rearrange("p (n c) -> p n c", c=RUN), spreads[0])
+        split = (MASKED - 512) // RUN
+        nc.scalar.copy(gate_m[:, 512:].rearrange("p (n c) -> p n c", c=RUN), spreads[1][:, :split, :])
+        nc.scalar.copy(gate_m[:, :512].rearrange("p (n c) -> p n c", c=RUN), spreads[0])
 
         def sort_words(dst, rows):
             nc.vector.tensor_copy(
@@ -151,12 +152,10 @@ def tile_moe_sdb_relu_kernel(
                 w2_scales[:, rows, :], w2_scales_raw[:].rearrange("p (m r) -> p r m", r=PACK)[:, rows, :]
             )
 
-        sort_words(w2_first, slice(0, 1))
+        sort_words(w2_sorted, slice(0, PACK))
         sort_scales(slice(0, 1))
         sort_scales(slice(1, PACK))
-        w2_rest = keep.tile([P, PACK - 1, PASSES, P], I32, name="w2_rest", tag="sorted", align_bytes=64)
-        sort_words(w2_rest, slice(1, PACK))
-        w2_codes = [w2_first[:, 0, :, :]] + [w2_rest[:, r, :, :] for r in range(PACK - 1)]
+        w2_codes = [w2_sorted[:, r, :, :] for r in range(PACK)]
 
         def hidden(r, cuts, tag):
             t0, t1 = cuts[0], cuts[-1]
@@ -191,14 +190,14 @@ def tile_moe_sdb_relu_kernel(
             nc.vector.tensor_tensor(dst, dc[r][:].indirect(offs_sb[:, j0 // 16 : j1 // 16]), other, ALU.mult)
 
         def apply_mask(rounded, j0, j1):
-            nc.vector.tensor_tensor(da[:, j0:j1, :], rounded[:, j0:j1, :], passed[:, j0:j1, :], ALU.mult)
+            nc.vector.tensor_tensor(rounded[:, j0:j1, :], rounded[:, j0:j1, :], passed[:, j0:j1, :], ALU.mult)
 
         def make_factor(dst, src):
             nc.vector.scalar_tensor_tensor(
                 dst.rearrange("p (n c) -> p n c", c=RUN),
                 src.rearrange("p (n c) -> p n c", c=RUN),
                 0.0,
-                spreads[1],
+                spreads[1][:, split:, :],
                 ALU.is_gt,
                 ALU.mult,
             )
@@ -239,11 +238,11 @@ def tile_moe_sdb_relu_kernel(
         for r in range(1, PACK):
             gather(picked[:, r, :MASKED], r, 0, MASKED, gate_m)
         factor = gate_sb[:, : (PACK - 2) * FUSED].rearrange("p (r j) -> p r j", j=FUSED)
-        mid = MASKED + 256
-        gather(picked[:, PACK - 1, MASKED:mid], PACK - 1, MASKED, mid, factor_second[:, :256])
+        mid = 768
+        gather(picked[:, PACK - 1, MASKED:mid], PACK - 1, MASKED, mid, factor_second[:, : mid - MASKED])
         for r in range(PACK - 2):
             make_factor(factor[:, r, :], acts_late[:, r, :])
-        gather(picked[:, PACK - 1, mid:], PACK - 1, mid, S, factor_second[:, 256:])
+        gather(picked[:, PACK - 1, mid:], PACK - 1, mid, S, factor_second[:, mid - MASKED :])
         for j0, j1 in ((MASKED, mid), (mid, S)):
             for r in range(1, PACK - 1):
                 gather(picked[:, r, j0:j1], r, j0, j1, factor[:, r - 1, j0 - MASKED : j1 - MASKED])
@@ -255,9 +254,10 @@ def tile_moe_sdb_relu_kernel(
         (a0, a1), (b0, b1) = pieces
         apply_mask(rounded, a0, a1)
         apply_mask(rounded, b0, b1)
-        quant(a0, a1, da[:, a0:a1, :])
+        b1 = f0 = 512
+        quant(a0, a1, rounded[:, a0:a1, :])
         nc.scalar.copy(dx[:, a0:a1], proj(a0, a1, "bank0")[:])
-        quant(b0, b1, da[:, b0:b1, :])
+        quant(b0, b1, rounded[:, b0:b1, :])
         nc.scalar.copy(dx[:, b0:b1], proj(b0, b1, "bank1")[:])
         quant(f0, f1, rounded[:, f0:f1, :])
         nc.scalar.copy(dx[:, f0:f1], proj(f0, f1, "bank5")[:])

@@ -19,13 +19,10 @@ P = 128
 PACK = 4
 PASSES = N // (P * PACK)
 FIRST = 256
-MASKED = 576
-FUSED = S - MASKED
-PAD = MASKED + 32 - T
-MASK_PIECES = (0, 256, MASKED)
+HALF = S // 2
 RUN = 4
-FUSED_PIECES = (MASKED, 768, S - C, S)
-PARTS = (0, 384, T)
+PAIR = 2
+OWN = 128
 
 
 def tile_moe_sdb_relu_kernel(
@@ -42,26 +39,21 @@ def tile_moe_sdb_relu_kernel(
         pos2_sb = keep.tile([P, T // 16], U16, name="pos2_sb")
 
         w2_raw = keep.tile([P, PASSES, H], I32, name="w2_raw", align_bytes=64)
-        w2_sorted = keep.tile([P, PACK, PASSES, P], I32, name="w2_sorted", align_bytes=64)
-        dy_codes = keep.tile([P, PASSES, T], I32, name="dy_codes", align_bytes=64)
+        w2_sorted = keep.tile([P, PACK, PASSES, P], I32, name="w2_sorted", tag="w2", align_bytes=64)
+        dy_codes = keep.tile([P, PASSES, T], I32, name="dy_codes", tag="dy", align_bytes=64)
         w1_codes = keep.tile([P, E, K], I32, name="w1_codes", align_bytes=64)
         w2_scales_raw = keep.tile([P, H], U8, name="w2_scales_raw", align_bytes=64)
         w2_scales = keep.tile([P, PACK, P], U8, name="w2_scales", align_bytes=64)
         dy_planes = keep.tile([P, PASSES, T], U8, name="dy_planes", align_bytes=64)
         w1_scales = keep.tile([P, E, K], U8, name="w1_scales", align_bytes=64)
-        gate_sb = keep.tile([P, S], F32, name="gate_sb")
         gate_cols = keep.tile([P, 2, 8], F32, name="gate_cols")
         identity = keep.tile([P, P], F32, name="identity")
-        acts_first = keep.tile([P, PACK, 256], F32, name="acts_first", tag="held")
-        acts = keep.tile([P, PACK, MASKED - 256], F32, name="acts")
-        acts_second = keep.tile([P, FUSED], F32, name="acts_second")
-        acts_late = keep.tile([P, PACK - 2, FUSED], F32, name="acts_late")
-        factor_second = keep.tile([P, FUSED], F32, name="factor_second")
-        dc = {r: keep.tile([P, S + 32 if r == 0 else T + PAD], F32, name=f"dc{r}") for r in (0, 1, 3)}
-        signs = keep.tile([P, MASKED, PACK], BF16, name="signs", tag="staged", align_bytes=64)
-        passed = keep.tile([P, MASKED, PACK], BF16, name="passed")
+        dc = [keep.tile([P, T], F32, name=f"dc{r}") for r in range(PACK)]
+        factor = [keep.tile([P, PACK, HALF], F32, name=f"factor{h}") for h in range(2)]
+        rounded = keep.tile([P, S, PACK], BF16, name="rounded", align_bytes=64)
         da_codes = keep.tile([P, S], I32, name="da_codes", align_bytes=64)
         da_scales = keep.tile([P, S], U8, name="da_scales", align_bytes=64)
+        dx = keep.tile([P, S], F32, name="dx")
 
         a_rows = a.rearrange("(p r) j -> p r j", r=PACK)
         nc.gpsimd.memset(w2_scales_raw[:].bitcast(I32), 0)
@@ -70,143 +62,118 @@ def tile_moe_sdb_relu_kernel(
         nc.gpsimd.affine_select(
             out=identity[:], in_=zeros[:], compare_op=ALU.not_equal, fill=1.0, base=0, pattern=[[-1, P]], channel_multiplier=1
         )
-        acts_early = keep.tile([P, FUSED], F32, name="acts_early", tag="wide")
-        nc.gpsimd.dma_start(acts_early[:], a_rows[:, 0, MASKED:])
-        nc.vector.memset(dc[0][:, T:], 0.0)
-        for r in (1, 3):
-            nc.gpsimd.memset(dc[r][:, T:], 0.0)
+        acts = {}
+        acts[0, 0] = keep.tile([P, HALF], F32, name="acts_early", tag="wide")
+        nc.gpsimd.dma_start(acts[0, 0][:], a_rows[:, 0, :HALF])
 
         dy_rows = dy_words.rearrange("s p t d -> p s (t d)").bitcast(I32)
 
-        def load_dy_scales(queue, q):
-            queue.dma_start(
+        def load_dy_scales(q):
+            nc.sync.dma_start(
                 dy_planes[32 * q : 32 * q + 4, :, :].bitcast(I32),
                 dy_scales[:, 4 * q : 4 * q + 4, :].rearrange("s b t -> b s t").bitcast(I32),
             )
 
-        def load_w2_scales(queue, q):
-            queue.dma_start(
+        def load_w2_scales(q):
+            nc.sync.dma_start(
                 w2_scales_raw[32 * q : 32 * q + 4 * PASSES, :].bitcast(I32),
                 w2t_scales[:, 4 * q : 4 * q + 4, :].bitcast(I32),
             )
 
-        def load_w2(queue):
-            queue.dma_start(w2_raw[:], w2t_words.rearrange("s p i d -> p s (i d)").bitcast(I32))
+        def load_acts(h, r0, r1):
+            tile = keep.tile([P, r1 - r0, HALF], F32, name=f"acts{h}_{r0}")
+            nc.sync.dma_start(tile[:], a_rows[:, r0:r1, h * HALF : (h + 1) * HALF])
+            for r in range(r0, r1):
+                acts[h, r] = tile[:, r - r0, :]
 
-        def load_dy(queue, t0, t1):
-            queue.dma_start(dy_codes[:, :, t0:t1], dy_rows[:, :, t0:t1])
-
-        def load_gate():
-            nc.sync.dma_start(gate_cols[:, :, :RUN], gate[0, :].rearrange("(h n c) -> n h c", h=2, c=RUN))
-
-        def load_acts(j0, j1):
-            nc.sync.dma_start(acts[:, :, j0 - 256 : j1 - 256], a_rows[:, :, j0:j1])
-
-        def load_w1(queue):
-            queue.dma_start(w1_codes[:], w1t_words.rearrange("e o p k d -> p (e o) (k d)").bitcast(I32))
-            for q in range(4):
-                queue.dma_start(
-                    w1_scales[32 * q : 32 * q + 4, :, :].bitcast(I32),
-                    w1t_scales[:, 0, 4 * q : 4 * q + 4, :].rearrange("e b k -> b e k").bitcast(I32),
-                )
-
-        load_gate()
-        load_dy_scales(nc.sync, 0)
-        load_dy_scales(nc.sync, 1)
-        load_dy_scales(nc.sync, 2)
-        load_w2(nc.sync)
+        nc.sync.dma_start(gate_cols[:, :, :RUN], gate[0, :].rearrange("(h n c) -> n h c", h=2, c=RUN))
+        for q in range(3):
+            load_dy_scales(q)
+        nc.sync.dma_start(w2_raw[:], w2t_words.rearrange("s p i d -> p s (i d)").bitcast(I32))
         for q in range(4):
-            load_w2_scales(nc.sync, q)
-        load_dy(nc.sync, 0, FIRST)
-        load_dy_scales(nc.sync, 3)
-        load_dy(nc.sync, FIRST, T)
-        nc.sync.dma_start(acts_second[:], a_rows[:, PACK - 1, MASKED:])
+            load_w2_scales(q)
+        nc.sync.dma_start(dy_codes[:, :, :FIRST], dy_rows[:, :, :FIRST])
+        load_dy_scales(3)
+        nc.sync.dma_start(dy_codes[:, :, FIRST:], dy_rows[:, :, FIRST:])
+        load_acts(0, 1, 2)
         nc.sync.dma_start(offs_sb[:], offs)
-        nc.sync.dma_start(acts_first[:], a_rows[:, :, :256])
-        load_acts(256, MASKED)
-        nc.sync.dma_start(acts_late[:], a_rows[:, 1 : PACK - 1, MASKED:])
-        load_w1(nc.sync)
+        load_acts(0, 2, 4)
+        load_acts(1, 0, 2)
+        load_acts(1, 2, 4)
+        nc.sync.dma_start(w1_codes[:], w1t_words.rearrange("e o p k d -> p (e o) (k d)").bitcast(I32))
+        for q in range(4):
+            nc.sync.dma_start(
+                w1_scales[32 * q : 32 * q + 4, :, :].bitcast(I32),
+                w1t_scales[:, 0, 4 * q : 4 * q + 4, :].rearrange("e b k -> b e k").bitcast(I32),
+            )
         nc.sync.dma_start(pos1_sb[:], pos1)
         nc.sync.dma_start(pos2_sb[:], pos2)
 
-        gate_m = gate_sb[:, :MASKED]
-        spreads = {}
-        for h in (1, 0):
+        spreads = []
+        for h in range(2):
             spread = psum.tile([P, RUN, P], F32, name=f"spread{h}", tag=f"bank{5 + h}")
             for c in range(RUN):
                 column = gate_cols[:, h, c : c + 1]
                 nc.tensor.transpose(spread[:, c, :], column.to_broadcast([P, P]), identity[:])
-            spreads[h] = spread[:].rearrange("p c n -> p n c")
-        split = (MASKED - 512) // RUN
-        nc.scalar.copy(gate_m[:, 512:].rearrange("p (n c) -> p n c", c=RUN), spreads[1][:, :split, :])
-        nc.scalar.copy(gate_m[:, :512].rearrange("p (n c) -> p n c", c=RUN), spreads[0])
+            spreads.append(spread[:].rearrange("p c n -> p n c"))
 
-        def sort_words(dst, rows):
-            nc.vector.tensor_copy(
-                dst[:].rearrange("p r s (c i) -> p (s c) r i", i=4),
-                w2_raw[:].rearrange("p s (c i r) -> p (s c) r i", i=4, r=PACK)[:, :, rows, :],
-            )
-
-        def sort_scales(rows):
+        nc.vector.tensor_copy(
+            w2_sorted[:].rearrange("p r s (c i) -> p (s c) r i", i=4),
+            w2_raw[:].rearrange("p s (c i r) -> p (s c) r i", i=4, r=PACK),
+        )
+        for rows in (slice(0, 1), slice(1, PACK)):
             nc.vector.tensor_copy(
                 w2_scales[:, rows, :], w2_scales_raw[:].rearrange("p (m r) -> p r m", r=PACK)[:, rows, :]
             )
 
-        sort_words(w2_sorted, slice(0, PACK))
-        sort_scales(slice(0, 1))
-        sort_scales(slice(1, PACK))
-        w2_codes = [w2_sorted[:, r, :, :] for r in range(PACK)]
-
-        def hidden(r, cuts, tag):
-            t0, t1 = cuts[0], cuts[-1]
+        def hidden(r, t0, t1, tag):
             bank = psum.tile([P, t1 - t0], F32, name=f"dc_bank{r}_{t0}", tag=tag)
-            for u0, u1 in zip(cuts, cuts[1:]):
-                for s in range(PASSES):
-                    nc.tensor.matmul_mx(
-                        out=bank[:, u0 - t0 : u1 - t0],
-                        lhsT=w2_codes[r][:, s, :].bitcast(FP8X4),
-                        lhsT_scale=w2_scales[4 * s :, r, :],
-                        rhs=dy_codes[:, s, u0:u1].bitcast(FP8X4),
-                        rhs_scale=dy_planes[:, s, u0:u1],
-                        start=(s == 0),
-                        stop=(s == PASSES - 1),
-                    )
+            for s in range(PASSES):
+                nc.tensor.matmul_mx(
+                    out=bank[:],
+                    lhsT=w2_sorted[:, r, s, :].bitcast(FP8X4),
+                    lhsT_scale=w2_scales[4 * s :, r, :],
+                    rhs=dy_codes[:, s, t0:t1].bitcast(FP8X4),
+                    rhs_scale=dy_planes[:, s, t0:t1],
+                    start=(s == 0),
+                    stop=(s == PASSES - 1),
+                )
             nc.scalar.copy(dc[r][:, t0:t1], bank[:])
 
-        hidden(0, (0, FIRST), "bank0")
-        hidden(0, (FIRST, T), "bank1")
-        hidden(1, (0, T), "bank2")
+        def window(r, j0, j1):
+            return dc[r][:].indirect(offs_sb[:, j0 // 16 : j1 // 16])
 
-        def interleaved(ap):
-            return ap.rearrange("p (c i) r -> p c r i", i=4)
+        def interleaved(j0, j1):
+            return rounded[:, j0:j1, :].rearrange("p (c i) r -> p c r i", i=PAIR)
 
         def planes(ap):
-            return ap.rearrange("p r (c i) -> p c r i", i=4)
+            return ap.rearrange("p r (c i) -> p c r i", i=PAIR)
 
-        def sign(j0, j1, src):
-            nc.scalar.activation(interleaved(signs[:, j0:j1, :]), planes(src), ACT.Sign)
+        def factor_of(j0, j1):
+            h = j0 // HALF
+            return factor[h][:, :, j0 - h * HALF : j1 - h * HALF]
 
-        def gather(dst, r, j0, j1, other):
-            nc.vector.tensor_tensor(dst, dc[r][:].indirect(offs_sb[:, j0 // 16 : j1 // 16]), other, ALU.mult)
-
-        def apply_mask(rounded, j0, j1):
-            nc.vector.tensor_tensor(rounded[:, j0:j1, :], rounded[:, j0:j1, :], passed[:, j0:j1, :], ALU.mult)
-
-        def make_factor(dst, src):
+        def make_factor(h, r):
             nc.vector.scalar_tensor_tensor(
-                dst.rearrange("p (n c) -> p n c", c=RUN),
-                src.rearrange("p (n c) -> p n c", c=RUN),
+                factor[h][:, r, :].rearrange("p (n c) -> p n c", c=RUN),
+                acts[h, r][:, :].rearrange("p (n c) -> p n c", c=RUN),
                 0.0,
-                spreads[1][:, split:, :],
+                spreads[h],
                 ALU.is_gt,
                 ALU.mult,
             )
 
-        def quant(j0, j1, src):
+        def fetch(dst, r, j0, j1):
+            nc.scalar.activation(dst[:, r, :], window(r, j0, j1), ACT.Copy)
+
+        def finish(src, j0, j1):
+            nc.vector.tensor_tensor(interleaved(j0, j1), planes(src), planes(factor_of(j0, j1)), ALU.mult)
+
+        def quant(j0, j1):
             nc.vector.quantize_mx(
                 out=da_codes[:, j0:j1].bitcast(FP8X4),
                 scales=da_scales[:, j0:j1],
-                in_=src.rearrange("p j r -> p (j r)"),
+                in_=rounded[:, j0:j1, :].rearrange("p j r -> p (j r)"),
             )
 
         def proj(j0, j1, tag):
@@ -223,57 +190,51 @@ def tile_moe_sdb_relu_kernel(
                 )
             return bank
 
-        pieces = list(zip(MASK_PIECES, MASK_PIECES[1:]))
-        sign(0, 256, acts_first[:])
-        dc[2] = keep.tile([P, T + PAD], F32, name="dc2", tag="held")
-        nc.gpsimd.memset(dc[2][:, T:], 0.0)
-        for r in (2, 3):
-            hidden(r, (0, T), f"bank{r + 1}")
-        sign(256, MASKED, acts[:])
-        nc.scalar.activation(passed[:], signs[:], ACT.Relu)
-        make_factor(gate_sb[:, MASKED:S], acts_early[:])
-        make_factor(factor_second[:], acts_second[:])
-        picked = keep.tile([P, PACK, S], F32, name="picked", tag="wide")
-        gather(picked[:, 0, :], 0, 0, S, gate_sb[:, :S])
+        picked_v = keep.tile([P, PACK, 256], F32, name="picked_v")
+        picked_a = keep.tile([P, PACK, 256], F32, name="picked_a")
+        hidden(0, 0, FIRST, "bank0")
+        hidden(0, FIRST, T, "bank1")
+        fetch(picked_a, 0, 256, 512)
         for r in range(1, PACK):
-            gather(picked[:, r, :MASKED], r, 0, MASKED, gate_m)
-        factor = gate_sb[:, : (PACK - 2) * FUSED].rearrange("p (r j) -> p r j", j=FUSED)
-        mid = 768
-        gather(picked[:, PACK - 1, MASKED:mid], PACK - 1, MASKED, mid, factor_second[:, : mid - MASKED])
-        for r in range(PACK - 2):
-            make_factor(factor[:, r, :], acts_late[:, r, :])
-        gather(picked[:, PACK - 1, mid:], PACK - 1, mid, S, factor_second[:, mid - MASKED :])
-        for j0, j1 in ((MASKED, mid), (mid, S)):
-            for r in range(1, PACK - 1):
-                gather(picked[:, r, j0:j1], r, j0, j1, factor[:, r - 1, j0 - MASKED : j1 - MASKED])
-        rounded = keep.tile([P, S, PACK], BF16, name="rounded", tag="staged", align_bytes=64)
-        f0, f1, f2, f3 = FUSED_PIECES
-        for j0, j1 in ((0, f0), (f0, f1), (f1, f3)):
-            nc.scalar.copy(interleaved(rounded[:, j0:j1, :]), planes(picked[:, :, j0:j1]))
-        dx = keep.tile([P, S], F32, name="dx", tag="wide")
-        (a0, a1), (b0, b1) = pieces
-        apply_mask(rounded, a0, a1)
-        apply_mask(rounded, b0, b1)
-        b1 = f0 = 512
-        quant(a0, a1, rounded[:, a0:a1, :])
-        nc.scalar.copy(dx[:, a0:a1], proj(a0, a1, "bank0")[:])
-        quant(b0, b1, rounded[:, b0:b1, :])
-        nc.scalar.copy(dx[:, b0:b1], proj(b0, b1, "bank1")[:])
-        quant(f0, f1, rounded[:, f0:f1, :])
-        nc.scalar.copy(dx[:, f0:f1], proj(f0, f1, "bank5")[:])
-        quant(f1, f2, rounded[:, f1:f2, :])
-        bank_c = proj(f1, f2, "bank7")
-        quant(f2, f3, rounded[:, f2:f3, :])
-        bank_f = proj(f2, f3, "bank6")
-        nc.vector.tensor_copy(dx[:, f1:f2], bank_c[:])
-        nc.scalar.copy(dx[:, f2:f3], bank_f[:])
+            hidden(r, 0, T, f"bank{r + 1}")
+            fetch(picked_a, r, 256, 512)
+        picked_b = keep.tile([P, PACK, 256], F32, name="picked_b", tag="dy", align_bytes=64)
+        picked_c = keep.tile([P, 2, PACK, C], F32, name="picked_c", tag="w2", align_bytes=64)
+        for r in range(PACK):
+            fetch(picked_b, r, 512, 768)
+        for u in range(2):
+            for r in range(PACK):
+                fetch(picked_c[:, u, :, :], r, 768 + u * C, 768 + (u + 1) * C)
+
+        for r in range(PACK):
+            make_factor(0, r)
+        for r in range(PACK):
+            nc.vector.tensor_tensor(picked_v[:, r, :], window(r, 0, 256), factor[0][:, r, :256], ALU.mult)
+            make_factor(1, r)
+        finish(picked_a[:], 256, 512)
+        finish(picked_b[:], 512, 768)
+        quant(256, 512)
+        finish(picked_c[:, 0, :, :], 768, 896)
+        quant(512, 768)
+        bank_a = proj(256, 768, "bank0")
+        nc.scalar.copy(interleaved(0, 256), planes(picked_v[:]))
+        finish(picked_c[:, 1, :, :], 896, S)
+        quant(768, 896)
+        quant(896, S)
+        bank_b = proj(768, S, "bank1")
+        quant(0, 256)
+        bank_c = proj(0, 256, "bank2")
+        nc.scalar.copy(dx[:, 256:768], bank_a[:])
+        nc.scalar.copy(dx[:, 768:], bank_b[:])
+        nc.vector.tensor_copy(dx[:, :256], bank_c[:])
 
         first = keep.tile([P, T], F32, name="first")
         result = keep.tile([P, T], F32, name="result")
-        parts = list(zip(PARTS, PARTS[1:]))
-        for t0, t1 in parts:
-            nc.vector.tensor_copy(first[:, t0:t1], dx[:].indirect(pos1_sb[:, t0 // 16 : t1 // 16]))
-        for t0, t1 in parts:
+        cuts = (0, 128, T - OWN, T)
+        nc.vector.tensor_copy(first[:, T - OWN :], dx[:].indirect(pos1_sb[:, (T - OWN) // 16 :]))
+        for t0, t1 in zip(cuts[:-2], cuts[1:-1]):
+            nc.scalar.activation(first[:, t0:t1], dx[:].indirect(pos1_sb[:, t0 // 16 : t1 // 16]), ACT.Copy)
+        for t0, t1 in zip(cuts, cuts[1:]):
             nc.vector.tensor_tensor(
                 result[:, t0:t1], dx[:].indirect(pos2_sb[:, t0 // 16 : t1 // 16]), first[:, t0:t1], ALU.add
             )

@@ -22,7 +22,8 @@ FIRST = 256
 HALF = S // 2
 RUN = 4
 PAIR = 2
-OWN = 128
+OWN = 160
+MINE = 256
 
 
 def tile_moe_sdb_relu_kernel(
@@ -43,7 +44,8 @@ def tile_moe_sdb_relu_kernel(
         dy_codes = keep.tile([P, PASSES, T], I32, name="dy_codes", tag="dy", align_bytes=64)
         w1_codes = keep.tile([P, E, K], I32, name="w1_codes", align_bytes=64)
         w2_scales_raw = keep.tile([P, H], U8, name="w2_scales_raw", align_bytes=64)
-        w2_scales = keep.tile([P, PACK, P], U8, name="w2_scales", align_bytes=64)
+        scale_sets = ((0, 1, "lead"), (1, PACK, "rest"))
+        w2_scales = {}
         dy_planes = keep.tile([P, PASSES, T], U8, name="dy_planes", align_bytes=64)
         w1_scales = keep.tile([P, E, K], U8, name="w1_scales", align_bytes=64)
         gate_cols = keep.tile([P, 2, 8], F32, name="gate_cols")
@@ -63,8 +65,8 @@ def tile_moe_sdb_relu_kernel(
             out=identity[:], in_=zeros[:], compare_op=ALU.not_equal, fill=1.0, base=0, pattern=[[-1, P]], channel_multiplier=1
         )
         acts = {}
-        acts[0, 0] = keep.tile([P, HALF], F32, name="acts_early", tag="wide")
-        nc.gpsimd.dma_start(acts[0, 0][:], a_rows[:, 0, :HALF])
+        acts[0, 0] = keep.tile([P, 1, HALF], F32, name="acts_early", tag="wide")
+        nc.gpsimd.dma_start(acts[0, 0][:], a_rows[:, 0:1, :HALF])
 
         dy_rows = dy_words.rearrange("s p t d -> p s (t d)").bitcast(I32)
 
@@ -83,8 +85,7 @@ def tile_moe_sdb_relu_kernel(
         def load_acts(h, r0, r1):
             tile = keep.tile([P, r1 - r0, HALF], F32, name=f"acts{h}_{r0}")
             nc.sync.dma_start(tile[:], a_rows[:, r0:r1, h * HALF : (h + 1) * HALF])
-            for r in range(r0, r1):
-                acts[h, r] = tile[:, r - r0, :]
+            acts[h, r0] = tile
 
         nc.sync.dma_start(gate_cols[:, :, :RUN], gate[0, :].rearrange("(h n c) -> n h c", h=2, c=RUN))
         for q in range(3):
@@ -111,20 +112,21 @@ def tile_moe_sdb_relu_kernel(
 
         spreads = []
         for h in range(2):
-            spread = psum.tile([P, RUN, P], F32, name=f"spread{h}", tag=f"bank{5 + h}")
+            spread = psum.tile([P, P, RUN], F32, name=f"spread{h}", tag=f"bank{5 + h}")
             for c in range(RUN):
                 column = gate_cols[:, h, c : c + 1]
-                nc.tensor.transpose(spread[:, c, :], column.to_broadcast([P, P]), identity[:])
-            spreads.append(spread[:].rearrange("p c n -> p n c"))
+                nc.tensor.transpose(spread[:, :, c], column.to_broadcast([P, P]), identity[:])
+            spreads.append(spread[:].rearrange("p n c -> p (n c)"))
 
         nc.vector.tensor_copy(
             w2_sorted[:].rearrange("p r s (c i) -> p (s c) r i", i=4),
             w2_raw[:].rearrange("p s (c i r) -> p (s c) r i", i=4, r=PACK),
         )
-        for rows in (slice(0, 1), slice(1, PACK)):
-            nc.vector.tensor_copy(
-                w2_scales[:, rows, :], w2_scales_raw[:].rearrange("p (m r) -> p r m", r=PACK)[:, rows, :]
-            )
+        for r0, r1, tag in scale_sets:
+            tile = keep.tile([P, r1 - r0, P], U8, name=f"w2_scales{r0}", tag=tag, align_bytes=64)
+            nc.vector.tensor_copy(tile[:], w2_scales_raw[:].rearrange("p (m r) -> p r m", r=PACK)[:, r0:r1, :])
+            for r in range(r0, r1):
+                w2_scales[r] = tile[4:, r - r0, :], tile[:, r - r0, :]
 
         def hidden(r, t0, t1, tag):
             bank = psum.tile([P, t1 - t0], F32, name=f"dc_bank{r}_{t0}", tag=tag)
@@ -132,7 +134,7 @@ def tile_moe_sdb_relu_kernel(
                 nc.tensor.matmul_mx(
                     out=bank[:],
                     lhsT=w2_sorted[:, r, s, :].bitcast(FP8X4),
-                    lhsT_scale=w2_scales[4 * s :, r, :],
+                    lhsT_scale=w2_scales[r][1 - s],
                     rhs=dy_codes[:, s, t0:t1].bitcast(FP8X4),
                     rhs_scale=dy_planes[:, s, t0:t1],
                     start=(s == 0),
@@ -153,12 +155,12 @@ def tile_moe_sdb_relu_kernel(
             h = j0 // HALF
             return factor[h][:, :, j0 - h * HALF : j1 - h * HALF]
 
-        def make_factor(h, r):
+        def make_factor(h, r0, r1):
             nc.vector.scalar_tensor_tensor(
-                factor[h][:, r, :].rearrange("p (n c) -> p n c", c=RUN),
-                acts[h, r][:, :].rearrange("p (n c) -> p n c", c=RUN),
+                factor[h][:, r0:r1, :],
+                acts[h, r0][:],
                 0.0,
-                spreads[h],
+                spreads[h].unsqueeze(1).to_broadcast([P, r1 - r0, HALF]),
                 ALU.is_gt,
                 ALU.mult,
             )
@@ -178,7 +180,7 @@ def tile_moe_sdb_relu_kernel(
 
         def proj(j0, j1, tag):
             bank = psum.tile([P, j1 - j0], F32, name=f"dx_bank{j0}", tag=tag)
-            for e in range(j0 // C, j1 // C):
+            for e in reversed(range(j0 // C, j1 // C)):
                 nc.tensor.matmul_mx(
                     out=bank[:, e * C - j0 : (e + 1) * C - j0],
                     lhsT=w1_codes[:, e, :].bitcast(FP8X4),
@@ -190,52 +192,59 @@ def tile_moe_sdb_relu_kernel(
                 )
             return bank
 
-        picked_v = keep.tile([P, PACK, 256], F32, name="picked_v")
-        picked_a = keep.tile([P, PACK, 256], F32, name="picked_a")
+        picked_v = keep.tile([P, PACK, HALF - MINE], F32, name="picked_v")
+        picked_a = keep.tile([P, PACK, 384], F32, name="picked_a")
         hidden(0, 0, FIRST, "bank0")
         hidden(0, FIRST, T, "bank1")
-        fetch(picked_a, 0, 256, 512)
+        fetch(picked_a, 0, 512, 896)
+        hidden(1, 0, T, "bank2")
         for r in range(1, PACK):
-            hidden(r, 0, T, f"bank{r + 1}")
-            fetch(picked_a, r, 256, 512)
-        picked_b = keep.tile([P, PACK, 256], F32, name="picked_b", tag="dy", align_bytes=64)
-        picked_c = keep.tile([P, 2, PACK, C], F32, name="picked_c", tag="w2", align_bytes=64)
+            if r + 1 < PACK:
+                hidden(r + 1, 0, T, f"bank{r + 2}")
+            fetch(picked_a, r, 512, 896)
+        picked_b = keep.tile([P, PACK, MINE], F32, name="picked_b", tag="dy", align_bytes=64)
+        picked_c = keep.tile([P, PACK, C], F32, name="picked_c", tag="w2", align_bytes=64)
         for r in range(PACK):
-            fetch(picked_b, r, 512, 768)
-        for u in range(2):
-            for r in range(PACK):
-                fetch(picked_c[:, u, :, :], r, 768 + u * C, 768 + (u + 1) * C)
+            fetch(picked_b, r, 0, MINE)
+        for r in range(PACK):
+            fetch(picked_c, r, 896, S)
 
+        for r0, r1 in ((0, 1), (1, 2), (2, PACK)):
+            make_factor(0, r0, r1)
         for r in range(PACK):
-            make_factor(0, r)
-        for r in range(PACK):
-            nc.vector.tensor_tensor(picked_v[:, r, :], window(r, 0, 256), factor[0][:, r, :256], ALU.mult)
-            make_factor(1, r)
-        finish(picked_a[:], 256, 512)
-        finish(picked_b[:], 512, 768)
-        quant(256, 512)
-        finish(picked_c[:, 0, :, :], 768, 896)
-        quant(512, 768)
-        bank_a = proj(256, 768, "bank0")
-        nc.scalar.copy(interleaved(0, 256), planes(picked_v[:]))
-        finish(picked_c[:, 1, :, :], 896, S)
-        quant(768, 896)
-        quant(896, S)
-        bank_b = proj(768, S, "bank1")
+            nc.vector.tensor_tensor(picked_v[:, r, :], window(r, MINE, HALF), factor[0][:, r, MINE:], ALU.mult)
+            if r % 2 == 0:
+                make_factor(1, r, r + 2)
+        finish(picked_a[:], 512, 896)
+        quant(512, 896)
+        bank_a = proj(512, 896, "bank0")
+        finish(picked_b[:], 0, MINE)
+        for j0, j1 in ((384, HALF), (MINE, 384)):
+            nc.scalar.copy(interleaved(j0, j1), planes(picked_v[:, :, j0 - MINE : j1 - MINE]))
+        finish(picked_c[:], 896, S)
         quant(0, 256)
-        bank_c = proj(0, 256, "bank2")
-        nc.scalar.copy(dx[:, 256:768], bank_a[:])
-        nc.scalar.copy(dx[:, 768:], bank_b[:])
-        nc.vector.tensor_copy(dx[:, :256], bank_c[:])
+        bank_b = proj(0, 256, "bank1")
+        quant(384, HALF)
+        bank_d = proj(384, HALF, "bank4")
+        quant(896, S)
+        bank_c = proj(896, S, "bank2")
+        quant(256, 384)
+        bank_v = proj(256, 384, "bank3")
+        nc.scalar.copy(dx[:, 512:896], bank_a[:])
+        nc.scalar.copy(dx[:, :256], bank_b[:])
+        nc.scalar.copy(dx[:, 384:HALF], bank_d[:])
+        nc.vector.tensor_copy(dx[:, 896:], bank_c[:])
+        nc.vector.tensor_copy(dx[:, 256:384], bank_v[:])
 
         first = keep.tile([P, T], F32, name="first")
         result = keep.tile([P, T], F32, name="result")
-        cuts = (0, 128, T - OWN, T)
-        nc.vector.tensor_copy(first[:, T - OWN :], dx[:].indirect(pos1_sb[:, (T - OWN) // 16 :]))
-        for t0, t1 in zip(cuts[:-2], cuts[1:-1]):
+        cuts = (0, OWN, OWN + 128, T)
+        nc.vector.tensor_copy(first[:, :OWN], dx[:].indirect(pos1_sb[:, : OWN // 16]))
+        for t0, t1 in zip(cuts[1:], cuts[2:]):
             nc.scalar.activation(first[:, t0:t1], dx[:].indirect(pos1_sb[:, t0 // 16 : t1 // 16]), ACT.Copy)
-        for t0, t1 in zip(cuts, cuts[1:]):
+        for t0, t1 in ((cuts[1], cuts[2]), (cuts[0], cuts[1]), (cuts[2], cuts[3])):
             nc.vector.tensor_tensor(
                 result[:, t0:t1], dx[:].indirect(pos2_sb[:, t0 // 16 : t1 // 16]), first[:, t0:t1], ALU.add
             )
+        for t0, t1 in ((0, cuts[2]), (cuts[2], T)):
             nc.sync.dma_start(out[:, t0:t1], result[:, t0:t1])

@@ -9,6 +9,7 @@ FLOPS = 2 * N * H * T + 2 * H * K * S
 F32 = mybir.dt.float32
 BF16 = mybir.dt.bfloat16
 I32 = mybir.dt.int32
+U32 = mybir.dt.uint32
 U16 = mybir.dt.uint16
 U8 = mybir.dt.uint8
 FP8X4 = mybir.dt.float8_e4m3fn_x4
@@ -40,11 +41,11 @@ def tile_moe_sdb_relu_kernel(
         pos2_sb = keep.tile([P, T // 16], U16, name="pos2_sb")
 
         w2_raw = keep.tile([P, PASSES, H], I32, name="w2_raw", align_bytes=64)
-        w2_sorted = keep.tile([P, PACK, PASSES, P], I32, name="w2_sorted", tag="w2", align_bytes=64)
+        w2_sorted = {}
         dy_codes = keep.tile([P, PASSES, T], I32, name="dy_codes", tag="dy", align_bytes=64)
         w1_codes = keep.tile([P, E, K], I32, name="w1_codes", align_bytes=64)
         w2_scales_raw = keep.tile([P, H], U8, name="w2_scales_raw", align_bytes=64)
-        scale_sets = ((0, 1, "lead"), (1, PACK, "rest"))
+        scale_sets = ((0, 1, "lead"), (1, 2, "second"), (2, PACK, "rest"))
         w2_scales = {}
         dy_planes = keep.tile([P, PASSES, T], U8, name="dy_planes", align_bytes=64)
         w1_scales = keep.tile([P, E, K], U8, name="w1_scales", align_bytes=64)
@@ -96,8 +97,8 @@ def tile_moe_sdb_relu_kernel(
         nc.sync.dma_start(dy_codes[:, :, :FIRST], dy_rows[:, :, :FIRST])
         load_dy_scales(3)
         nc.sync.dma_start(dy_codes[:, :, FIRST:], dy_rows[:, :, FIRST:])
-        load_acts(0, 1, 2)
         nc.sync.dma_start(offs_sb[:], offs)
+        load_acts(0, 1, 2)
         load_acts(0, 2, 4)
         load_acts(1, 0, 2)
         load_acts(1, 2, 4)
@@ -118,10 +119,14 @@ def tile_moe_sdb_relu_kernel(
                 nc.tensor.transpose(spread[:, :, c], column.to_broadcast([P, P]), identity[:])
             spreads.append(spread[:].rearrange("p n c -> p (n c)"))
 
-        nc.vector.tensor_copy(
-            w2_sorted[:].rearrange("p r s (c i) -> p (s c) r i", i=4),
-            w2_raw[:].rearrange("p s (c i r) -> p (s c) r i", i=4, r=PACK),
-        )
+        for r0, tag, copy, word in ((0, "w2_low", nc.vector.tensor_copy, I32), (2, "w2", nc.scalar.copy, U32)):
+            words = keep.tile([P, 2, PASSES, P], word, name=f"w2_sorted{r0}", tag=tag, align_bytes=64)
+            copy(
+                words[:].rearrange("p r s (c i) -> p (s c) r i", i=4),
+                w2_raw[:].bitcast(word).rearrange("p s (c i r) -> p (s c) r i", i=4, r=PACK)[:, :, r0 : r0 + 2, :],
+            )
+            for r in range(2):
+                w2_sorted[r0 + r] = words[:, r, :, :]
         for r0, r1, tag in scale_sets:
             tile = keep.tile([P, r1 - r0, P], U8, name=f"w2_scales{r0}", tag=tag, align_bytes=64)
             nc.vector.tensor_copy(tile[:], w2_scales_raw[:].rearrange("p (m r) -> p r m", r=PACK)[:, r0:r1, :])
@@ -133,7 +138,7 @@ def tile_moe_sdb_relu_kernel(
             for s in range(PASSES):
                 nc.tensor.matmul_mx(
                     out=bank[:],
-                    lhsT=w2_sorted[:, r, s, :].bitcast(FP8X4),
+                    lhsT=w2_sorted[r][:, s, :].bitcast(FP8X4),
                     lhsT_scale=w2_scales[r][1 - s],
                     rhs=dy_codes[:, s, t0:t1].bitcast(FP8X4),
                     rhs_scale=dy_planes[:, s, t0:t1],
@@ -198,13 +203,14 @@ def tile_moe_sdb_relu_kernel(
         hidden(0, FIRST, T, "bank1")
         fetch(picked_a, 0, 512, 896)
         hidden(1, 0, T, "bank2")
+        picked_b = keep.tile([P, PACK, MINE], F32, name="picked_b", tag="second", align_bytes=64)
+        fetch(picked_b, 0, 0, MINE)
         for r in range(1, PACK):
             if r + 1 < PACK:
                 hidden(r + 1, 0, T, f"bank{r + 2}")
             fetch(picked_a, r, 512, 896)
-        picked_b = keep.tile([P, PACK, MINE], F32, name="picked_b", tag="dy", align_bytes=64)
         picked_c = keep.tile([P, PACK, C], F32, name="picked_c", tag="w2", align_bytes=64)
-        for r in range(PACK):
+        for r in range(1, PACK):
             fetch(picked_b, r, 0, MINE)
         for r in range(PACK):
             fetch(picked_c, r, 896, S)

@@ -23,8 +23,10 @@ FIRST = 256
 HALF = S // 2
 RUN = 4
 PAIR = 2
-OWN = 160
-MINE = 256
+OWN = 96
+MINE = 192
+LAST = 320
+MAIN = 768
 
 
 def tile_moe_sdb_relu_kernel(
@@ -45,14 +47,14 @@ def tile_moe_sdb_relu_kernel(
         dy_codes = keep.tile([P, PASSES, T], I32, name="dy_codes", tag="dy", align_bytes=64)
         w1_codes = keep.tile([P, E, K], I32, name="w1_codes", align_bytes=64)
         w2_scales_raw = keep.tile([P, H], U8, name="w2_scales_raw", align_bytes=64)
-        scale_sets = ((0, 1, "lead"), (1, 2, "second"), (2, PACK, "rest"))
+        scale_sets = ((0, 1, "lead"), (1, PACK, "rest"))
         w2_scales = {}
         dy_planes = keep.tile([P, PASSES, T], U8, name="dy_planes", align_bytes=64)
         w1_scales = keep.tile([P, E, K], U8, name="w1_scales", align_bytes=64)
         gate_cols = keep.tile([P, 2, 8], F32, name="gate_cols")
         identity = keep.tile([P, P], F32, name="identity")
         dc = [keep.tile([P, T], F32, name=f"dc{r}") for r in range(PACK)]
-        factor = [keep.tile([P, PACK, HALF], F32, name=f"factor{h}") for h in range(2)]
+        factor = keep.tile([P, PACK, S], F32, name="factor")
         rounded = keep.tile([P, S, PACK], BF16, name="rounded", align_bytes=64)
         da_codes = keep.tile([P, S], I32, name="da_codes", align_bytes=64)
         da_scales = keep.tile([P, S], U8, name="da_scales", align_bytes=64)
@@ -97,8 +99,8 @@ def tile_moe_sdb_relu_kernel(
         nc.sync.dma_start(dy_codes[:, :, :FIRST], dy_rows[:, :, :FIRST])
         load_dy_scales(3)
         nc.sync.dma_start(dy_codes[:, :, FIRST:], dy_rows[:, :, FIRST:])
-        nc.sync.dma_start(offs_sb[:], offs)
         load_acts(0, 1, 2)
+        nc.sync.dma_start(offs_sb[:], offs)
         load_acts(0, 2, 4)
         load_acts(1, 0, 2)
         load_acts(1, 2, 4)
@@ -150,19 +152,15 @@ def tile_moe_sdb_relu_kernel(
         def window(r, j0, j1):
             return dc[r][:].indirect(offs_sb[:, j0 // 16 : j1 // 16])
 
-        def interleaved(j0, j1):
-            return rounded[:, j0:j1, :].rearrange("p (c i) r -> p c r i", i=PAIR)
+        def interleaved(ap):
+            return ap.rearrange("p (c i) r -> p c r i", i=PAIR)
 
         def planes(ap):
             return ap.rearrange("p r (c i) -> p c r i", i=PAIR)
 
-        def factor_of(j0, j1):
-            h = j0 // HALF
-            return factor[h][:, :, j0 - h * HALF : j1 - h * HALF]
-
         def make_factor(h, r0, r1):
             nc.vector.scalar_tensor_tensor(
-                factor[h][:, r0:r1, :],
+                factor[:, r0:r1, h * HALF : (h + 1) * HALF],
                 acts[h, r0][:],
                 0.0,
                 spreads[h].unsqueeze(1).to_broadcast([P, r1 - r0, HALF]),
@@ -174,7 +172,7 @@ def tile_moe_sdb_relu_kernel(
             nc.scalar.activation(dst[:, r, :], window(r, j0, j1), ACT.Copy)
 
         def finish(src, j0, j1):
-            nc.vector.tensor_tensor(interleaved(j0, j1), planes(src), planes(factor_of(j0, j1)), ALU.mult)
+            nc.vector.tensor_tensor(interleaved(rounded[:, j0:j1, :]), planes(src), planes(factor[:, :, j0:j1]), ALU.mult)
 
         def quant(j0, j1):
             nc.vector.quantize_mx(
@@ -197,60 +195,64 @@ def tile_moe_sdb_relu_kernel(
                 )
             return bank
 
-        picked_v = keep.tile([P, PACK, HALF - MINE], F32, name="picked_v")
-        picked_a = keep.tile([P, PACK, 384], F32, name="picked_a")
+        picked_v = keep.tile([P, PACK, MINE], F32, name="picked_v")
+        picked_a = keep.tile([P, PACK, MAIN - LAST], F32, name="picked_a")
         hidden(0, 0, FIRST, "bank0")
         hidden(0, FIRST, T, "bank1")
-        fetch(picked_a, 0, 512, 896)
+        fetch(picked_a, 0, LAST, MAIN)
         hidden(1, 0, T, "bank2")
-        picked_b = keep.tile([P, PACK, MINE], F32, name="picked_b", tag="second", align_bytes=64)
-        fetch(picked_b, 0, 0, MINE)
         for r in range(1, PACK):
             if r + 1 < PACK:
                 hidden(r + 1, 0, T, f"bank{r + 2}")
-            fetch(picked_a, r, 512, 896)
-        picked_c = keep.tile([P, PACK, C], F32, name="picked_c", tag="w2", align_bytes=64)
-        for r in range(1, PACK):
-            fetch(picked_b, r, 0, MINE)
+            fetch(picked_a, r, LAST, MAIN)
+        picked_b = keep.tile([P, PACK, S - MAIN], F32, name="picked_b", tag="dy", align_bytes=64)
+        picked_c = keep.tile([P, PACK, LAST - MINE], F32, name="picked_c", tag="w2", align_bytes=64)
         for r in range(PACK):
-            fetch(picked_c, r, 896, S)
+            fetch(picked_b, r, MAIN, S)
+        for r in range(PACK):
+            fetch(picked_c, r, MINE, LAST)
 
         for r0, r1 in ((0, 1), (1, 2), (2, PACK)):
             make_factor(0, r0, r1)
         for r in range(PACK):
-            nc.vector.tensor_tensor(picked_v[:, r, :], window(r, MINE, HALF), factor[0][:, r, MINE:], ALU.mult)
+            nc.vector.tensor_tensor(picked_v[:, r, :], window(r, 0, MINE), factor[:, r, :MINE], ALU.mult)
             if r % 2 == 0:
                 make_factor(1, r, r + 2)
-        finish(picked_a[:], 512, 896)
-        quant(512, 896)
-        bank_a = proj(512, 896, "bank0")
-        finish(picked_b[:], 0, MINE)
-        for j0, j1 in ((384, HALF), (MINE, 384)):
-            nc.scalar.copy(interleaved(j0, j1), planes(picked_v[:, :, j0 - MINE : j1 - MINE]))
-        finish(picked_c[:], 896, S)
-        quant(0, 256)
-        bank_b = proj(0, 256, "bank1")
+        finish(picked_a[:, :, : HALF - LAST], LAST, HALF)
+        finish(picked_a[:, :, HALF - LAST :], HALF, MAIN)
         quant(384, HALF)
-        bank_d = proj(384, HALF, "bank4")
-        quant(896, S)
-        bank_c = proj(896, S, "bank2")
+        quant(HALF, MAIN)
+        bank_a = proj(384, MAIN, "bank0")
+        finish(picked_b[:, :, :C], MAIN, MAIN + C)
+        finish(picked_b[:, :, C:], MAIN + C, S)
+        quant(MAIN, MAIN + C)
+        quant(MAIN + C, S)
+        bank_b = proj(MAIN, S, "bank1")
+        finish(picked_c[:], MINE, LAST)
+        for j0, j1 in ((0, C), (C, MINE)):
+            nc.scalar.copy(interleaved(rounded[:, j0:j1, :]), planes(picked_v[:, :, j0:j1]))
+        quant(0, C)
+        bank_d = proj(0, C, "bank4")
         quant(256, 384)
-        bank_v = proj(256, 384, "bank3")
-        nc.scalar.copy(dx[:, 512:896], bank_a[:])
-        nc.scalar.copy(dx[:, :256], bank_b[:])
-        nc.scalar.copy(dx[:, 384:HALF], bank_d[:])
-        nc.vector.tensor_copy(dx[:, 896:], bank_c[:])
-        nc.vector.tensor_copy(dx[:, 256:384], bank_v[:])
+        bank_c = proj(256, 384, "bank2")
+        quant(C, 256)
+        bank_v = proj(C, 256, "bank3")
+        nc.scalar.copy(dx[:, 384:768], bank_a[:])
+        nc.scalar.copy(dx[:, 768:], bank_b[:])
+        nc.scalar.copy(dx[:, :C], bank_d[:])
+        nc.vector.tensor_copy(dx[:, 256:384], bank_c[:])
+        nc.vector.tensor_copy(dx[:, C:256], bank_v[:])
 
         first = keep.tile([P, T], F32, name="first")
         result = keep.tile([P, T], F32, name="result")
-        cuts = (0, OWN, OWN + 128, T)
+        cuts = (0, OWN, 2 * OWN, 352, T)
+        parts = list(zip(cuts, cuts[1:]))
         nc.vector.tensor_copy(first[:, :OWN], dx[:].indirect(pos1_sb[:, : OWN // 16]))
-        for t0, t1 in zip(cuts[1:], cuts[2:]):
+        for t0, t1 in parts[1:]:
             nc.scalar.activation(first[:, t0:t1], dx[:].indirect(pos1_sb[:, t0 // 16 : t1 // 16]), ACT.Copy)
-        for t0, t1 in ((cuts[1], cuts[2]), (cuts[0], cuts[1]), (cuts[2], cuts[3])):
+        for t0, t1 in (parts[1], parts[0], parts[2], parts[3]):
             nc.vector.tensor_tensor(
                 result[:, t0:t1], dx[:].indirect(pos2_sb[:, t0 // 16 : t1 // 16]), first[:, t0:t1], ALU.add
             )
-        for t0, t1 in ((0, cuts[2]), (cuts[2], T)):
+        for t0, t1 in ((0, cuts[3]), (cuts[3], T)):
             nc.sync.dma_start(out[:, t0:t1], result[:, t0:t1])

@@ -24,7 +24,7 @@ HALF = S // 2
 RUN = 4
 PAIR = 2
 OWN = 96
-MINE = 192
+MINE = 224
 LAST = 320
 MAIN = 768
 
@@ -85,10 +85,10 @@ def tile_moe_sdb_relu_kernel(
                 w2t_scales[:, 4 * q : 4 * q + 4, :].bitcast(I32),
             )
 
-        def load_acts(h, r0, r1):
-            tile = keep.tile([P, r1 - r0, HALF], F32, name=f"acts{h}_{r0}")
-            nc.sync.dma_start(tile[:], a_rows[:, r0:r1, h * HALF : (h + 1) * HALF])
-            acts[h, r0] = tile
+        def load_acts(r0, r1, j0, j1):
+            tile = keep.tile([P, r1 - r0, j1 - j0], F32, name=f"acts{r0}_{j0}")
+            nc.sync.dma_start(tile[:], a_rows[:, r0:r1, j0:j1])
+            acts[r0, j0] = tile
 
         nc.sync.dma_start(gate_cols[:, :, :RUN], gate[0, :].rearrange("(h n c) -> n h c", h=2, c=RUN))
         for q in range(3):
@@ -99,11 +99,12 @@ def tile_moe_sdb_relu_kernel(
         nc.sync.dma_start(dy_codes[:, :, :FIRST], dy_rows[:, :, :FIRST])
         load_dy_scales(3)
         nc.sync.dma_start(dy_codes[:, :, FIRST:], dy_rows[:, :, FIRST:])
-        load_acts(0, 1, 2)
+        load_acts(1, 2, 0, 256)
         nc.sync.dma_start(offs_sb[:], offs)
-        load_acts(0, 2, 4)
-        load_acts(1, 0, 2)
-        load_acts(1, 2, 4)
+        load_acts(1, 2, 256, HALF)
+        load_acts(2, PACK, 0, HALF)
+        load_acts(0, 2, HALF, S)
+        load_acts(2, PACK, HALF, S)
         nc.sync.dma_start(w1_codes[:], w1t_words.rearrange("e o p k d -> p (e o) (k d)").bitcast(I32))
         for q in range(4):
             nc.sync.dma_start(
@@ -158,12 +159,13 @@ def tile_moe_sdb_relu_kernel(
         def planes(ap):
             return ap.rearrange("p r (c i) -> p c r i", i=PAIR)
 
-        def make_factor(h, r0, r1):
+        def make_factor(r0, r1, j0, j1):
+            h = j0 // HALF
             nc.vector.scalar_tensor_tensor(
-                factor[:, r0:r1, h * HALF : (h + 1) * HALF],
-                acts[h, r0][:],
+                factor[:, r0:r1, j0:j1],
+                acts[r0, j0][:],
                 0.0,
-                spreads[h].unsqueeze(1).to_broadcast([P, r1 - r0, HALF]),
+                spreads[h][:, j0 - h * HALF : j1 - h * HALF].unsqueeze(1).to_broadcast([P, r1 - r0, j1 - j0]),
                 ALU.is_gt,
                 ALU.mult,
             )
@@ -212,36 +214,33 @@ def tile_moe_sdb_relu_kernel(
         for r in range(PACK):
             fetch(picked_c, r, MINE, LAST)
 
-        for r0, r1 in ((0, 1), (1, 2), (2, PACK)):
-            make_factor(0, r0, r1)
+        for r0, r1, j0, j1 in ((0, 1, 0, HALF), (1, 2, 0, 256), (1, 2, 256, HALF), (2, PACK, 0, HALF)):
+            make_factor(r0, r1, j0, j1)
         for r in range(PACK):
             nc.vector.tensor_tensor(picked_v[:, r, :], window(r, 0, MINE), factor[:, r, :MINE], ALU.mult)
             if r % 2 == 0:
-                make_factor(1, r, r + 2)
-        finish(picked_a[:, :, : HALF - LAST], LAST, HALF)
+                make_factor(r, r + 2, HALF, S)
         finish(picked_a[:, :, HALF - LAST :], HALF, MAIN)
-        quant(384, HALF)
+        finish(picked_a[:, :, : HALF - LAST], LAST, HALF)
         quant(HALF, MAIN)
+        quant(384, HALF)
         bank_a = proj(384, MAIN, "bank0")
-        finish(picked_b[:, :, :C], MAIN, MAIN + C)
-        finish(picked_b[:, :, C:], MAIN + C, S)
-        quant(MAIN, MAIN + C)
-        quant(MAIN + C, S)
-        bank_b = proj(MAIN, S, "bank1")
+        finish(picked_b[:], MAIN, S)
         finish(picked_c[:], MINE, LAST)
+        quant(MAIN, S)
+        bank_b = proj(MAIN, S, "bank1")
         for j0, j1 in ((0, C), (C, MINE)):
             nc.scalar.copy(interleaved(rounded[:, j0:j1, :]), planes(picked_v[:, :, j0:j1]))
         quant(0, C)
         bank_d = proj(0, C, "bank4")
-        quant(256, 384)
+        quant(C, 384)
         bank_c = proj(256, 384, "bank2")
-        quant(C, 256)
         bank_v = proj(C, 256, "bank3")
         nc.scalar.copy(dx[:, 384:768], bank_a[:])
         nc.scalar.copy(dx[:, 768:], bank_b[:])
-        nc.scalar.copy(dx[:, :C], bank_d[:])
+        nc.vector.tensor_copy(dx[:, :C], bank_d[:])
         nc.vector.tensor_copy(dx[:, 256:384], bank_c[:])
-        nc.vector.tensor_copy(dx[:, C:256], bank_v[:])
+        nc.scalar.copy(dx[:, C:256], bank_v[:])
 
         first = keep.tile([P, T], F32, name="first")
         result = keep.tile([P, T], F32, name="result")

@@ -136,7 +136,7 @@ def tile_moe_sdb_relu_kernel(
             for r in range(r0, r1):
                 w2_scales[r] = tile[4:, r - r0, :], tile[:, r - r0, :]
 
-        def hidden(r, t0, t1, tag):
+        def hidden(r, t0, t1, tag, copy=nc.scalar.copy):
             bank = psum.tile([P, t1 - t0], F32, name=f"dc_bank{r}_{t0}", tag=tag)
             for s in range(PASSES):
                 nc.tensor.matmul_mx(
@@ -148,7 +148,7 @@ def tile_moe_sdb_relu_kernel(
                     start=(s == 0),
                     stop=(s == PASSES - 1),
                 )
-            nc.scalar.copy(dc[r][:, t0:t1], bank[:])
+            copy(dc[r][:, t0:t1], bank[:])
 
         def window(r, j0, j1):
             return dc[r][:].indirect(offs_sb[:, j0 // 16 : j1 // 16])
@@ -200,7 +200,8 @@ def tile_moe_sdb_relu_kernel(
         picked_v = keep.tile([P, PACK, MINE], F32, name="picked_v")
         picked_a = keep.tile([P, PACK, MAIN - LAST], F32, name="picked_a")
         hidden(0, 0, FIRST, "bank0")
-        hidden(0, FIRST, T, "bank1")
+        hidden(0, FIRST, 384, "bank1")
+        hidden(0, 384, T, "bank7", nc.vector.tensor_copy)
         fetch(picked_a, 0, LAST, MAIN)
         hidden(1, 0, T, "bank2")
         for r in range(1, PACK):

@@ -102,7 +102,8 @@ def tile_moe_sdb_relu_kernel(
         load_acts(1, 2, 0, 256)
         nc.sync.dma_start(offs_sb[:], offs)
         load_acts(1, 2, 256, HALF)
-        load_acts(2, PACK, 0, HALF)
+        load_acts(2, 3, 0, HALF)
+        load_acts(3, PACK, 0, HALF)
         load_acts(0, 2, HALF, S)
         load_acts(2, PACK, HALF, S)
         nc.sync.dma_start(w1_codes[:], w1t_words.rearrange("e o p k d -> p (e o) (k d)").bitcast(I32))
@@ -215,7 +216,7 @@ def tile_moe_sdb_relu_kernel(
         for r in range(PACK):
             fetch(picked_c, r, MINE, LAST)
 
-        for r0, r1, j0, j1 in ((0, 1, 0, HALF), (1, 2, 0, 256), (1, 2, 256, HALF), (2, PACK, 0, HALF)):
+        for r0, r1, j0, j1 in ((0, 1, 0, HALF), (1, 2, 0, 256), (1, 2, 256, HALF), (2, 3, 0, HALF), (3, PACK, 0, HALF)):
             make_factor(r0, r1, j0, j1)
         for r in range(PACK):
             nc.vector.tensor_tensor(picked_v[:, r, :], window(r, 0, MINE), factor[:, r, :MINE], ALU.mult)

@@ -61,9 +61,9 @@ def tile_moe_sdb_relu_kernel(
         dx = keep.tile([P, S], F32, name="dx")
 
         a_rows = a.rearrange("(p r) j -> p r j", r=PACK)
-        nc.gpsimd.memset(w2_scales_raw[:].bitcast(I32), 0)
         zeros = keep.tile([P, P], F32, name="zeros", tag="wide")
         nc.gpsimd.memset(zeros[:], 0.0)
+        nc.gpsimd.memset(w2_scales_raw[:].bitcast(I32), 0)
         nc.gpsimd.affine_select(
             out=identity[:], in_=zeros[:], compare_op=ALU.not_equal, fill=1.0, base=0, pattern=[[-1, P]], channel_multiplier=1
         )
@@ -96,9 +96,9 @@ def tile_moe_sdb_relu_kernel(
         nc.sync.dma_start(w2_raw[:], w2t_words.rearrange("s p i d -> p s (i d)").bitcast(I32))
         for q in range(4):
             load_w2_scales(q)
-        nc.sync.dma_start(dy_codes[:, :, :FIRST], dy_rows[:, :, :FIRST])
+        nc.sync.dma_start(dy_codes[:, 0, :], dy_rows[:, 0, :])
         load_dy_scales(3)
-        nc.sync.dma_start(dy_codes[:, :, FIRST:], dy_rows[:, :, FIRST:])
+        nc.sync.dma_start(dy_codes[:, 1, :], dy_rows[:, 1, :])
         load_acts(1, 2, 0, 256)
         nc.sync.dma_start(offs_sb[:], offs)
         load_acts(1, 2, 256, HALF)
@@ -137,19 +137,21 @@ def tile_moe_sdb_relu_kernel(
             for r in range(r0, r1):
                 w2_scales[r] = tile[4:, r - r0, :], tile[:, r - r0, :]
 
-        def hidden(r, t0, t1, tag, copy=nc.scalar.copy):
-            bank = psum.tile([P, t1 - t0], F32, name=f"dc_bank{r}_{t0}", tag=tag)
-            for s in range(PASSES):
-                nc.tensor.matmul_mx(
-                    out=bank[:],
-                    lhsT=w2_sorted[r][:, s, :].bitcast(FP8X4),
-                    lhsT_scale=w2_scales[r][1 - s],
-                    rhs=dy_codes[:, s, t0:t1].bitcast(FP8X4),
-                    rhs_scale=dy_planes[:, s, t0:t1],
-                    start=(s == 0),
-                    stop=(s == PASSES - 1),
-                )
-            copy(dc[r][:, t0:t1], bank[:])
+        def hidden(r, order, spans):
+            banks = [psum.tile([P, t1 - t0], F32, name=f"dc_bank{r}_{t0}", tag=tag) for t0, t1, tag, copy in spans]
+            for s in order:
+                for (t0, t1, tag, copy), bank in zip(spans, banks):
+                    nc.tensor.matmul_mx(
+                        out=bank[:],
+                        lhsT=w2_sorted[r][:, s, :].bitcast(FP8X4),
+                        lhsT_scale=w2_scales[r][1 - s],
+                        rhs=dy_codes[:, s, t0:t1].bitcast(FP8X4),
+                        rhs_scale=dy_planes[:, s, t0:t1],
+                        start=(s == order[0]),
+                        stop=(s == order[-1]),
+                    )
+            for (t0, t1, tag, copy), bank in zip(spans, banks):
+                copy(dc[r][:, t0:t1], bank[:])
 
         def window(r, j0, j1):
             return dc[r][:].indirect(offs_sb[:, j0 // 16 : j1 // 16])
@@ -200,14 +202,12 @@ def tile_moe_sdb_relu_kernel(
 
         picked_v = keep.tile([P, PACK, MINE], F32, name="picked_v")
         picked_a = keep.tile([P, PACK, MAIN - LAST], F32, name="picked_a")
-        hidden(0, 0, FIRST, "bank0")
-        hidden(0, FIRST, 384, "bank1")
-        hidden(0, 384, T, "bank7", nc.vector.tensor_copy)
+        hidden(0, (0, 1), ((0, C, "bank0", nc.scalar.copy), (C, 256, "bank7", nc.vector.tensor_copy), (256, T, "bank1", nc.scalar.copy)))
         fetch(picked_a, 0, LAST, MAIN)
-        hidden(1, 0, T, "bank2")
+        hidden(1, (1, 0), ((0, T, "bank2", nc.scalar.copy),))
         for r in range(1, PACK):
             if r + 1 < PACK:
-                hidden(r + 1, 0, T, f"bank{r + 2}")
+                hidden(r + 1, (1, 0), ((0, T, f"bank{r + 2}", nc.scalar.copy),))
             fetch(picked_a, r, LAST, MAIN)
         picked_b = keep.tile([P, PACK, S - MAIN], F32, name="picked_b", tag="dy", align_bytes=64)
         picked_c = keep.tile([P, PACK, LAST - MINE], F32, name="picked_c", tag="w2", align_bytes=64)

@@ -25,7 +25,7 @@ RUN = 4
 PAIR = 2
 OWN = 96
 MINE = 224
-LAST = 320
+LAST = 352
 MAIN = 768
 
 
@@ -202,18 +202,20 @@ def tile_moe_sdb_relu_kernel(
 
         picked_v = keep.tile([P, PACK, MINE], F32, name="picked_v")
         picked_a = keep.tile([P, PACK, MAIN - LAST], F32, name="picked_a")
-        hidden(0, (0, 1), ((0, C, "bank0", nc.scalar.copy), (C, 256, "bank7", nc.vector.tensor_copy), (256, T, "bank1", nc.scalar.copy)))
+        hidden(0, (0, 1), ((0, C, "bank0", nc.scalar.copy), (C, 256, "bank7", nc.scalar.copy), (256, T, "bank1", nc.scalar.copy)))
         fetch(picked_a, 0, LAST, MAIN)
+        picked_c = keep.tile([P, PACK, LAST - MINE], F32, name="picked_c")
         hidden(1, (1, 0), ((0, T, "bank2", nc.scalar.copy),))
-        for r in range(1, PACK):
-            if r + 1 < PACK:
-                hidden(r + 1, (1, 0), ((0, T, f"bank{r + 2}", nc.scalar.copy),))
+        fetch(picked_c, 0, MINE, LAST)
+        fetch(picked_a, 1, LAST, MAIN)
+        for r in (2, 3):
+            hidden(r, (1, 0), ((0, T, f"bank{r + 1}", nc.scalar.copy),))
+        for r in (2, 3):
             fetch(picked_a, r, LAST, MAIN)
         picked_b = keep.tile([P, PACK, S - MAIN], F32, name="picked_b", tag="dy", align_bytes=64)
-        picked_c = keep.tile([P, PACK, LAST - MINE], F32, name="picked_c", tag="w2", align_bytes=64)
         for r in range(PACK):
             fetch(picked_b, r, MAIN, S)
-        for r in range(PACK):
+        for r in range(1, PACK):
             fetch(picked_c, r, MINE, LAST)
 
         for r0, r1, j0, j1 in ((0, 1, 0, HALF), (1, 2, 0, 256), (1, 2, 256, HALF), (2, 3, 0, HALF), (3, PACK, 0, HALF)):

@@ -19,14 +19,13 @@ ACT = mybir.ActivationFunctionType
 P = 128
 PACK = 4
 PASSES = N // (P * PACK)
-FIRST = 256
 HALF = S // 2
 RUN = 4
-PAIR = 2
+LINE = 4
 OWN = 96
-MINE = 224
-LAST = 352
-MAIN = 768
+MINE = 256
+CUT_A = 640
+CUT_B = 896
 
 
 def tile_moe_sdb_relu_kernel(
@@ -54,9 +53,7 @@ def tile_moe_sdb_relu_kernel(
         gate_cols = keep.tile([P, 2, 8], F32, name="gate_cols")
         identity = keep.tile([P, P], F32, name="identity")
         dc = [keep.tile([P, T], F32, name=f"dc{r}") for r in range(PACK)]
-        factor = keep.tile([P, PACK, S], F32, name="factor")
-        rounded = keep.tile([P, S, PACK], BF16, name="rounded", align_bytes=64)
-        da_codes = keep.tile([P, S], I32, name="da_codes", align_bytes=64)
+        da_codes = keep.tile([P, S - MINE], I32, name="da_codes", align_bytes=64)
         da_scales = keep.tile([P, S], U8, name="da_scales", align_bytes=64)
         dx = keep.tile([P, S], F32, name="dx")
 
@@ -86,7 +83,7 @@ def tile_moe_sdb_relu_kernel(
             )
 
         def load_acts(r0, r1, j0, j1):
-            tile = keep.tile([P, r1 - r0, j1 - j0], F32, name=f"acts{r0}_{j0}")
+            tile = keep.tile([P, r1 - r0, j1 - j0], F32, name=f"acts{r0}_{j0}", tag=f"acts{r0}_{j0}", align_bytes=64)
             nc.sync.dma_start(tile[:], a_rows[:, r0:r1, j0:j1])
             acts[r0, j0] = tile
 
@@ -157,94 +154,113 @@ def tile_moe_sdb_relu_kernel(
             return dc[r][:].indirect(offs_sb[:, j0 // 16 : j1 // 16])
 
         def interleaved(ap):
-            return ap.rearrange("p (c i) r -> p c r i", i=PAIR)
+            return ap.rearrange("p (c i) r -> p c r i", i=LINE)
 
         def planes(ap):
-            return ap.rearrange("p r (c i) -> p c r i", i=PAIR)
+            return ap.rearrange("p r (c i) -> p c r i", i=LINE)
 
-        def make_factor(r0, r1, j0, j1):
+        def make_factor(dst, src, j0, j1):
             h = j0 // HALF
+            rows = src.shape[1]
             nc.vector.scalar_tensor_tensor(
-                factor[:, r0:r1, j0:j1],
-                acts[r0, j0][:],
+                dst,
+                src,
                 0.0,
-                spreads[h][:, j0 - h * HALF : j1 - h * HALF].unsqueeze(1).to_broadcast([P, r1 - r0, j1 - j0]),
+                spreads[h][:, j0 - h * HALF : j1 - h * HALF].unsqueeze(1).to_broadcast([P, rows, j1 - j0]),
                 ALU.is_gt,
                 ALU.mult,
             )
 
-        def fetch(dst, r, j0, j1):
-            nc.scalar.activation(dst[:, r, :], window(r, j0, j1), ACT.Copy)
+        def fetch(dst, r, j0, j1, origin=None):
+            origin = j0 if origin is None else origin
+            nc.scalar.activation(dst[:, r, j0 - origin : j1 - origin], window(r, j0, j1), ACT.Copy)
 
-        def finish(src, j0, j1):
-            nc.vector.tensor_tensor(interleaved(rounded[:, j0:j1, :]), planes(src), planes(factor[:, :, j0:j1]), ALU.mult)
+        def finish(dst, src, factor):
+            nc.vector.tensor_tensor(interleaved(dst), planes(src), planes(factor), ALU.mult)
 
-        def quant(j0, j1):
+        def codes(j0, j1):
+            return codes_v[:, j0:j1] if j1 <= MINE else da_codes[:, j0 - MINE : j1 - MINE]
+
+        def quant(src, j0, j1):
             nc.vector.quantize_mx(
-                out=da_codes[:, j0:j1].bitcast(FP8X4),
+                out=codes(j0, j1).bitcast(FP8X4),
                 scales=da_scales[:, j0:j1],
-                in_=rounded[:, j0:j1, :].rearrange("p j r -> p (j r)"),
+                in_=src.rearrange("p j r -> p (j r)"),
             )
 
         def proj(j0, j1, tag):
             bank = psum.tile([P, j1 - j0], F32, name=f"dx_bank{j0}", tag=tag)
-            for e in reversed(range(j0 // C, j1 // C)):
+            for e in range(j0 // C, j1 // C):
                 nc.tensor.matmul_mx(
                     out=bank[:, e * C - j0 : (e + 1) * C - j0],
                     lhsT=w1_codes[:, e, :].bitcast(FP8X4),
                     lhsT_scale=w1_scales[:, e, :],
-                    rhs=da_codes[:, e * C : (e + 1) * C].bitcast(FP8X4),
+                    rhs=codes(e * C, (e + 1) * C).bitcast(FP8X4),
                     rhs_scale=da_scales[:, e * C : (e + 1) * C],
                     start=True,
                     stop=True,
                 )
             return bank
 
-        picked_v = keep.tile([P, PACK, MINE], F32, name="picked_v")
-        picked_a = keep.tile([P, PACK, MAIN - LAST], F32, name="picked_a")
-        hidden(0, (0, 1), ((0, C, "bank0", nc.scalar.copy), (C, 256, "bank7", nc.scalar.copy), (256, T, "bank1", nc.scalar.copy)))
-        fetch(picked_a, 0, LAST, MAIN)
-        picked_c = keep.tile([P, PACK, LAST - MINE], F32, name="picked_c")
-        hidden(1, (1, 0), ((0, T, "bank2", nc.scalar.copy),))
-        fetch(picked_c, 0, MINE, LAST)
-        fetch(picked_a, 1, LAST, MAIN)
-        for r in (2, 3):
-            hidden(r, (1, 0), ((0, T, f"bank{r + 1}", nc.scalar.copy),))
-        for r in (2, 3):
-            fetch(picked_a, r, LAST, MAIN)
-        picked_b = keep.tile([P, PACK, S - MAIN], F32, name="picked_b", tag="dy", align_bytes=64)
-        for r in range(PACK):
-            fetch(picked_b, r, MAIN, S)
-        for r in range(1, PACK):
-            fetch(picked_c, r, MINE, LAST)
+        gate_sb = keep.tile([P, MINE], F32, name="gate_sb")
+        gate_last = keep.tile([P, C], F32, name="gate_last", tag="held")
+        nc.scalar.copy(gate_sb[:], spreads[0][:, :MINE])
+        nc.scalar.copy(gate_last[:], spreads[0][:, :C])
 
-        for r0, r1, j0, j1 in ((0, 1, 0, HALF), (1, 2, 0, 256), (1, 2, 256, HALF), (2, 3, 0, HALF), (3, PACK, 0, HALF)):
-            make_factor(r0, r1, j0, j1)
+        gated = keep.tile([P, PACK, MINE], F32, name="gated")
+        mask = keep.tile([P, PACK, MINE], F32, name="mask")
+        factor_low = keep.tile([P, PACK, HALF - MINE], F32, name="factor_low", tag="low", align_bytes=64)
+        picked_a = keep.tile([P, PACK, CUT_A - MINE], F32, name="picked_a", tag="first_piece", align_bytes=64)
+        hidden(0, (0, 1), ((0, C, "bank0", nc.scalar.copy), (C, 256, "bank7", nc.scalar.copy), (256, T, "bank1", nc.scalar.copy)))
+        fetch(picked_a, 0, MINE, HALF)
+        hidden(1, (1, 0), ((0, T, "bank2", nc.scalar.copy),))
+        hidden(2, (1, 0), ((0, 256, "bank3", nc.scalar.copy), (256, T, "bank4", nc.scalar.copy)))
+        hidden(3, (1, 0), ((0, 256, "bank0", nc.scalar.copy), (256, T, "bank7", nc.scalar.copy)))
+        fetch(picked_a, 0, HALF, CUT_A, MINE)
+        for r in range(1, PACK):
+            fetch(picked_a, r, MINE, CUT_A)
+        picked_b = keep.tile([P, PACK, CUT_B - CUT_A], F32, name="picked_b", tag="dy", align_bytes=64)
         for r in range(PACK):
-            nc.vector.tensor_tensor(picked_v[:, r, :], window(r, 0, MINE), factor[:, r, :MINE], ALU.mult)
-            if r % 2 == 0:
-                make_factor(r, r + 2, HALF, S)
-        finish(picked_a[:, :, HALF - LAST :], HALF, MAIN)
-        finish(picked_a[:, :, : HALF - LAST], LAST, HALF)
-        quant(HALF, MAIN)
-        quant(384, HALF)
-        bank_a = proj(384, MAIN, "bank0")
-        finish(picked_b[:], MAIN, S)
-        finish(picked_c[:], MINE, LAST)
-        quant(MAIN, S)
-        bank_b = proj(MAIN, S, "bank1")
-        for j0, j1 in ((0, C), (C, MINE)):
-            nc.scalar.copy(interleaved(rounded[:, j0:j1, :]), planes(picked_v[:, :, j0:j1]))
-        quant(0, C)
-        bank_d = proj(0, C, "bank4")
-        quant(C, 384)
-        bank_c = proj(256, 384, "bank2")
-        bank_v = proj(C, 256, "bank3")
-        nc.scalar.copy(dx[:, 384:768], bank_a[:])
-        nc.scalar.copy(dx[:, 768:], bank_b[:])
-        nc.vector.tensor_copy(dx[:, :C], bank_d[:])
-        nc.vector.tensor_copy(dx[:, 256:384], bank_c[:])
-        nc.scalar.copy(dx[:, C:256], bank_v[:])
+            fetch(picked_b, r, CUT_A, CUT_B)
+        picked_c = keep.tile([P, PACK, S - CUT_B], F32, name="picked_c", tag="w2", align_bytes=64)
+        for r in range(PACK):
+            fetch(picked_c, r, CUT_B, S)
+
+        for r in range(PACK):
+            low = acts[r, 0][:, 0, :MINE]
+            high = acts[1, MINE][:] if r == 1 else acts[r, 0][:, :, MINE:]
+            make_factor(factor_low[:, r : r + 1, :], high, MINE, HALF)
+            nc.vector.tensor_scalar(mask[:, r, :], low, 0.0, None, ALU.is_gt)
+        for r in range(PACK - 1):
+            nc.vector.tensor_tensor(gated[:, r, :], window(r, 0, MINE), gate_sb[:], ALU.mult)
+        nc.vector.tensor_tensor(gated[:, 3, :C], window(3, 0, C), gate_last[:], ALU.mult)
+        nc.vector.tensor_tensor(gated[:, 3, C:], window(3, C, MINE), gate_sb[:, C:], ALU.mult)
+        rounded_v = keep.tile([P, MINE, PACK], BF16, name="rounded_v", align_bytes=64)
+        nc.gpsimd.tensor_tensor(interleaved(rounded_v[:]), planes(gated[:]), planes(mask[:]), ALU.mult)
+
+        factor_high = keep.tile([P, PACK, HALF], F32, name="factor_high", tag="held")
+        for r in (0, 2):
+            make_factor(factor_high[:, r : r + 2, :], acts[r, HALF][:], HALF, S)
+        rounded_a = keep.tile([P, CUT_A - MINE, PACK], BF16, name="rounded_a", tag=f"acts0_{HALF}", align_bytes=64)
+        finish(rounded_a[:, : HALF - MINE, :], picked_a[:, :, : HALF - MINE], factor_low[:])
+        finish(rounded_a[:, HALF - MINE :, :], picked_a[:, :, HALF - MINE :], factor_high[:, :, : CUT_A - HALF])
+        codes_v = keep.tile([P, MINE], I32, name="codes_v", tag="low", align_bytes=64)
+        quant(rounded_v[:], 0, MINE)
+        bank_v = proj(0, MINE, "bank1")
+        quant(rounded_a[:], MINE, CUT_A)
+        bank_a = proj(MINE, CUT_A, "bank2")
+        rounded_b = keep.tile([P, CUT_B - CUT_A, PACK], BF16, name="rounded_b", tag="first_piece", align_bytes=64)
+        rounded_c = keep.tile([P, S - CUT_B, PACK], BF16, name="rounded_c", tag=f"acts0_{HALF}", align_bytes=64)
+        finish(rounded_b[:], picked_b[:], factor_high[:, :, CUT_A - HALF : CUT_B - HALF])
+        finish(rounded_c[:], picked_c[:], factor_high[:, :, CUT_B - HALF :])
+        quant(rounded_b[:], CUT_A, CUT_B)
+        bank_b = proj(CUT_A, CUT_B, "bank3")
+        quant(rounded_c[:], CUT_B, S)
+        bank_c = proj(CUT_B, S, "bank4")
+        nc.scalar.copy(dx[:, :MINE], bank_v[:])
+        nc.scalar.copy(dx[:, MINE:CUT_A], bank_a[:])
+        nc.scalar.copy(dx[:, CUT_A:CUT_B], bank_b[:])
+        nc.vector.tensor_copy(dx[:, CUT_B:], bank_c[:])
 
         first = keep.tile([P, T], F32, name="first")
         result = keep.tile([P, T], F32, name="result")

@@ -23,6 +23,7 @@ HALF = S // 2
 RUN = 4
 LINE = 4
 OWN = 96
+POOL = 128
 MINE = 256
 CUT_A = 640
 CUT_B = 896
@@ -179,7 +180,11 @@ def tile_moe_sdb_relu_kernel(
             nc.vector.tensor_tensor(interleaved(dst), planes(src), planes(factor), ALU.mult)
 
         def codes(j0, j1):
-            return codes_v[:, j0:j1] if j1 <= MINE else da_codes[:, j0 - MINE : j1 - MINE]
+            if j1 <= POOL:
+                return codes_g[:, j0:j1]
+            if j1 <= MINE:
+                return codes_v[:, j0 - POOL : j1 - POOL]
+            return da_codes[:, j0 - MINE : j1 - MINE]
 
         def quant(src, j0, j1):
             nc.vector.quantize_mx(
@@ -202,14 +207,14 @@ def tile_moe_sdb_relu_kernel(
                 )
             return bank
 
-        gate_sb = keep.tile([P, MINE], F32, name="gate_sb")
-        gate_last = keep.tile([P, C], F32, name="gate_last", tag="held")
-        nc.scalar.copy(gate_sb[:], spreads[0][:, :MINE])
-        nc.scalar.copy(gate_last[:], spreads[0][:, :C])
+        factor_low = keep.tile([P, PACK, HALF], F32, name="factor_low", tag="low", align_bytes=64)
+        factor_high = keep.tile([P, PACK, HALF], F32, name="factor_high")
+        gate_last = factor_high[:, 1, :POOL]
+        nc.scalar.copy(factor_low[:, :3, :POOL], spreads[0][:, :POOL].unsqueeze(1).to_broadcast([P, 3, POOL]))
+        nc.scalar.copy(gate_last, spreads[0][:, :POOL])
 
         gated = keep.tile([P, PACK, MINE], F32, name="gated")
-        mask = keep.tile([P, PACK, MINE], F32, name="mask")
-        factor_low = keep.tile([P, PACK, HALF - MINE], F32, name="factor_low", tag="low", align_bytes=64)
+        mask = keep.tile([P, PACK, POOL], F32, name="mask")
         picked_a = keep.tile([P, PACK, CUT_A - MINE], F32, name="picked_a", tag="first_piece", align_bytes=64)
         hidden(0, (0, 1), ((0, C, "bank0", nc.scalar.copy), (C, 256, "bank7", nc.scalar.copy), (256, T, "bank1", nc.scalar.copy)))
         fetch(picked_a, 0, MINE, HALF)
@@ -226,27 +231,27 @@ def tile_moe_sdb_relu_kernel(
         for r in range(PACK):
             fetch(picked_c, r, CUT_B, S)
 
-        for r in range(PACK):
-            low = acts[r, 0][:, 0, :MINE]
-            high = acts[1, MINE][:] if r == 1 else acts[r, 0][:, :, MINE:]
-            make_factor(factor_low[:, r : r + 1, :], high, MINE, HALF)
-            nc.vector.tensor_scalar(mask[:, r, :], low, 0.0, None, ALU.is_gt)
+        for r, j0, j1 in ((0, POOL, HALF), (1, POOL, 256), (1, 256, HALF), (2, POOL, HALF), (3, POOL, HALF)):
+            origin = 256 if j0 == 256 else 0
+            make_factor(factor_low[:, r : r + 1, j0:j1], acts[r, origin][:, :, j0 - origin : j1 - origin], j0, j1)
+            if origin == 0:
+                nc.vector.tensor_scalar(mask[:, r, :], acts[r, 0][:, 0, :POOL], 0.0, None, ALU.is_gt)
         for r in range(PACK - 1):
-            nc.vector.tensor_tensor(gated[:, r, :], window(r, 0, MINE), gate_sb[:], ALU.mult)
-        nc.vector.tensor_tensor(gated[:, 3, :C], window(3, 0, C), gate_last[:], ALU.mult)
-        nc.vector.tensor_tensor(gated[:, 3, C:], window(3, C, MINE), gate_sb[:, C:], ALU.mult)
-        rounded_v = keep.tile([P, MINE, PACK], BF16, name="rounded_v", align_bytes=64)
-        nc.gpsimd.tensor_tensor(interleaved(rounded_v[:]), planes(gated[:]), planes(mask[:]), ALU.mult)
+            nc.vector.tensor_tensor(gated[:, r, :], window(r, 0, MINE), factor_low[:, r, :MINE], ALU.mult)
+        make_factor(factor_high[:, 0:1, :], acts[0, HALF][:, 0:1, :], HALF, S)
+        nc.vector.tensor_tensor(gated[:, 3, :POOL], window(3, 0, POOL), gate_last, ALU.mult)
+        nc.vector.tensor_tensor(gated[:, 3, POOL:], window(3, POOL, MINE), factor_low[:, 3, POOL:MINE], ALU.mult)
+        rounded_g = keep.tile([P, POOL, PACK], BF16, name="rounded_g", align_bytes=64)
+        nc.gpsimd.tensor_tensor(interleaved(rounded_g[:]), planes(gated[:, :, :POOL]), planes(mask[:]), ALU.mult)
 
-        factor_high = keep.tile([P, PACK, HALF], F32, name="factor_high", tag="held")
-        for r in (0, 2):
-            make_factor(factor_high[:, r : r + 2, :], acts[r, HALF][:], HALF, S)
+        make_factor(factor_high[:, 1:2, :], acts[0, HALF][:, 1:2, :], HALF, S)
+        make_factor(factor_high[:, 2:, :], acts[2, HALF][:], HALF, S)
         rounded_a = keep.tile([P, CUT_A - MINE, PACK], BF16, name="rounded_a", tag=f"acts0_{HALF}", align_bytes=64)
-        finish(rounded_a[:, : HALF - MINE, :], picked_a[:, :, : HALF - MINE], factor_low[:])
+        finish(rounded_a[:, : HALF - MINE, :], picked_a[:, :, : HALF - MINE], factor_low[:, :, MINE:])
         finish(rounded_a[:, HALF - MINE :, :], picked_a[:, :, HALF - MINE :], factor_high[:, :, : CUT_A - HALF])
-        codes_v = keep.tile([P, MINE], I32, name="codes_v", tag="low", align_bytes=64)
-        quant(rounded_v[:], 0, MINE)
-        bank_v = proj(0, MINE, "bank1")
+        codes_g = keep.tile([P, POOL], I32, name="codes_g", tag="low", align_bytes=64)
+        quant(rounded_g[:], 0, POOL)
+        bank_g = proj(0, POOL, "bank1")
         quant(rounded_a[:], MINE, CUT_A)
         bank_a = proj(MINE, CUT_A, "bank2")
         rounded_b = keep.tile([P, CUT_B - CUT_A, PACK], BF16, name="rounded_b", tag="first_piece", align_bytes=64)
@@ -257,10 +262,16 @@ def tile_moe_sdb_relu_kernel(
         bank_b = proj(CUT_A, CUT_B, "bank3")
         quant(rounded_c[:], CUT_B, S)
         bank_c = proj(CUT_B, S, "bank4")
-        nc.scalar.copy(dx[:, :MINE], bank_v[:])
+        rounded_v = keep.tile([P, MINE - POOL, PACK], BF16, name="rounded_v", align_bytes=64)
+        nc.scalar.copy(interleaved(rounded_v[:]), planes(gated[:, :, POOL:]))
+        codes_v = keep.tile([P, MINE - POOL], I32, name="codes_v", tag="dy", align_bytes=64)
+        quant(rounded_v[:], POOL, MINE)
+        bank_v = proj(POOL, MINE, "bank0")
+        nc.scalar.copy(dx[:, :POOL], bank_g[:])
         nc.scalar.copy(dx[:, MINE:CUT_A], bank_a[:])
         nc.scalar.copy(dx[:, CUT_A:CUT_B], bank_b[:])
         nc.vector.tensor_copy(dx[:, CUT_B:], bank_c[:])
+        nc.scalar.copy(dx[:, POOL:MINE], bank_v[:])
 
         first = keep.tile([P, T], F32, name="first")
         result = keep.tile([P, T], F32, name="result")

@@ -23,9 +23,9 @@ HALF = S // 2
 RUN = 4
 LINE = 4
 OWN = 96
-POOL = 128
+KEPT = 64
 MINE = 256
-CUT_A = 640
+CUT_A = 768
 CUT_B = 896
 
 
@@ -54,7 +54,7 @@ def tile_moe_sdb_relu_kernel(
         gate_cols = keep.tile([P, 2, 8], F32, name="gate_cols")
         identity = keep.tile([P, P], F32, name="identity")
         dc = [keep.tile([P, T], F32, name=f"dc{r}") for r in range(PACK)]
-        da_codes = keep.tile([P, S - MINE], I32, name="da_codes", align_bytes=64)
+        da_codes = keep.tile([P, S], I32, name="da_codes", align_bytes=64)
         da_scales = keep.tile([P, S], U8, name="da_scales", align_bytes=64)
         dx = keep.tile([P, S], F32, name="dx")
 
@@ -180,11 +180,7 @@ def tile_moe_sdb_relu_kernel(
             nc.vector.tensor_tensor(interleaved(dst), planes(src), planes(factor), ALU.mult)
 
         def codes(j0, j1):
-            if j1 <= POOL:
-                return codes_g[:, j0:j1]
-            if j1 <= MINE:
-                return codes_v[:, j0 - POOL : j1 - POOL]
-            return da_codes[:, j0 - MINE : j1 - MINE]
+            return codes_v[:] if j0 == C else da_codes[:, j0:j1]
 
         def quant(src, j0, j1):
             nc.vector.quantize_mx(
@@ -207,71 +203,74 @@ def tile_moe_sdb_relu_kernel(
                 )
             return bank
 
-        factor_low = keep.tile([P, PACK, HALF], F32, name="factor_low", tag="low", align_bytes=64)
-        factor_high = keep.tile([P, PACK, HALF], F32, name="factor_high")
-        gate_last = factor_high[:, 1, :POOL]
-        nc.scalar.copy(factor_low[:, :3, :POOL], spreads[0][:, :POOL].unsqueeze(1).to_broadcast([P, 3, POOL]))
-        nc.scalar.copy(gate_last, spreads[0][:, :POOL])
-
         gated = keep.tile([P, PACK, MINE], F32, name="gated")
-        mask = keep.tile([P, PACK, POOL], F32, name="mask")
-        picked_a = keep.tile([P, PACK, CUT_A - MINE], F32, name="picked_a", tag="first_piece", align_bytes=64)
+        factor_own = keep.tile([P, PACK, MINE], F32, name="factor_own", tag="held")
+        factor_low = keep.tile([P, PACK, HALF - MINE], F32, name="factor_low")
+        picked_a = keep.tile([P, PACK, HALF - MINE], F32, name="picked_a")
         hidden(0, (0, 1), ((0, C, "bank0", nc.scalar.copy), (C, 256, "bank7", nc.scalar.copy), (256, T, "bank1", nc.scalar.copy)))
         fetch(picked_a, 0, MINE, HALF)
         hidden(1, (1, 0), ((0, T, "bank2", nc.scalar.copy),))
-        hidden(2, (1, 0), ((0, 256, "bank3", nc.scalar.copy), (256, T, "bank4", nc.scalar.copy)))
-        hidden(3, (1, 0), ((0, 256, "bank0", nc.scalar.copy), (256, T, "bank7", nc.scalar.copy)))
-        fetch(picked_a, 0, HALF, CUT_A, MINE)
-        for r in range(1, PACK):
-            fetch(picked_a, r, MINE, CUT_A)
-        picked_b = keep.tile([P, PACK, CUT_B - CUT_A], F32, name="picked_b", tag="dy", align_bytes=64)
-        for r in range(PACK):
-            fetch(picked_b, r, CUT_A, CUT_B)
-        picked_c = keep.tile([P, PACK, S - CUT_B], F32, name="picked_c", tag="w2", align_bytes=64)
-        for r in range(PACK):
-            fetch(picked_c, r, CUT_B, S)
+        hidden(2, (1, 0), ((0, T, "bank3", nc.scalar.copy),))
+        fetch(picked_a, 1, MINE, HALF)
+        hidden(3, (1, 0), ((0, T, "bank4", nc.scalar.copy),))
+        for r in (2, 3):
+            fetch(picked_a, r, MINE, HALF)
+        picked_b = keep.tile([P, PACK, CUT_A - HALF], F32, name="picked_b", tag="dy", align_bytes=64)
+        picked_c = keep.tile([P, PACK, CUT_B - CUT_A], F32, name="picked_c", tag="w2", align_bytes=64)
+        picked_d = keep.tile([P, PACK, S - CUT_B], F32, name="picked_d", tag="w2_low", align_bytes=64)
+        for picked, j0, j1 in ((picked_b, HALF, CUT_A), (picked_c, CUT_A, CUT_B), (picked_d, CUT_B, S)):
+            for r in range(PACK):
+                fetch(picked, r, j0, j1)
 
-        for r, j0, j1 in ((0, POOL, HALF), (1, POOL, 256), (1, 256, HALF), (2, POOL, HALF), (3, POOL, HALF)):
-            origin = 256 if j0 == 256 else 0
-            make_factor(factor_low[:, r : r + 1, j0:j1], acts[r, origin][:, :, j0 - origin : j1 - origin], j0, j1)
-            if origin == 0:
-                nc.vector.tensor_scalar(mask[:, r, :], acts[r, 0][:, 0, :POOL], 0.0, None, ALU.is_gt)
-        for r in range(PACK - 1):
-            nc.vector.tensor_tensor(gated[:, r, :], window(r, 0, MINE), factor_low[:, r, :MINE], ALU.mult)
-        make_factor(factor_high[:, 0:1, :], acts[0, HALF][:, 0:1, :], HALF, S)
-        nc.vector.tensor_tensor(gated[:, 3, :POOL], window(3, 0, POOL), gate_last, ALU.mult)
-        nc.vector.tensor_tensor(gated[:, 3, POOL:], window(3, POOL, MINE), factor_low[:, 3, POOL:MINE], ALU.mult)
-        rounded_g = keep.tile([P, POOL, PACK], BF16, name="rounded_g", align_bytes=64)
-        nc.gpsimd.tensor_tensor(interleaved(rounded_g[:]), planes(gated[:, :, :POOL]), planes(mask[:]), ALU.mult)
+        def gather_own(r, j0, j1):
+            nc.vector.tensor_tensor(gated[:, r, j0:j1], window(r, j0, j1), factor_own[:, r, j0:j1], ALU.mult)
 
-        make_factor(factor_high[:, 1:2, :], acts[0, HALF][:, 1:2, :], HALF, S)
-        make_factor(factor_high[:, 2:, :], acts[2, HALF][:], HALF, S)
-        rounded_a = keep.tile([P, CUT_A - MINE, PACK], BF16, name="rounded_a", tag=f"acts0_{HALF}", align_bytes=64)
-        finish(rounded_a[:, : HALF - MINE, :], picked_a[:, :, : HALF - MINE], factor_low[:, :, MINE:])
-        finish(rounded_a[:, HALF - MINE :, :], picked_a[:, :, HALF - MINE :], factor_high[:, :, : CUT_A - HALF])
-        codes_g = keep.tile([P, POOL], I32, name="codes_g", tag="low", align_bytes=64)
-        quant(rounded_g[:], 0, POOL)
-        bank_g = proj(0, POOL, "bank1")
-        quant(rounded_a[:], MINE, CUT_A)
-        bank_a = proj(MINE, CUT_A, "bank2")
-        rounded_b = keep.tile([P, CUT_B - CUT_A, PACK], BF16, name="rounded_b", tag="first_piece", align_bytes=64)
-        rounded_c = keep.tile([P, S - CUT_B, PACK], BF16, name="rounded_c", tag=f"acts0_{HALF}", align_bytes=64)
-        finish(rounded_b[:], picked_b[:], factor_high[:, :, CUT_A - HALF : CUT_B - HALF])
-        finish(rounded_c[:], picked_c[:], factor_high[:, :, CUT_B - HALF :])
-        quant(rounded_b[:], CUT_A, CUT_B)
-        bank_b = proj(CUT_A, CUT_B, "bank3")
-        quant(rounded_c[:], CUT_B, S)
-        bank_c = proj(CUT_B, S, "bank4")
-        rounded_v = keep.tile([P, MINE - POOL, PACK], BF16, name="rounded_v", align_bytes=64)
-        nc.scalar.copy(interleaved(rounded_v[:]), planes(gated[:, :, POOL:]))
-        codes_v = keep.tile([P, MINE - POOL], I32, name="codes_v", tag="dy", align_bytes=64)
-        quant(rounded_v[:], POOL, MINE)
-        bank_v = proj(POOL, MINE, "bank0")
-        nc.scalar.copy(dx[:, :POOL], bank_g[:])
-        nc.scalar.copy(dx[:, MINE:CUT_A], bank_a[:])
-        nc.scalar.copy(dx[:, CUT_A:CUT_B], bank_b[:])
-        nc.vector.tensor_copy(dx[:, CUT_B:], bank_c[:])
-        nc.scalar.copy(dx[:, POOL:MINE], bank_v[:])
+        for r in range(PACK):
+            make_factor(factor_own[:, r : r + 1, :], acts[r, 0][:, :, :MINE], 0, MINE)
+            high = acts[1, MINE][:] if r == 1 else acts[r, 0][:, :, MINE:]
+            make_factor(factor_low[:, r : r + 1, :], high, MINE, HALF)
+            if r == 2:
+                gather_own(0, 0, MINE)
+        for r in (1, 2):
+            gather_own(r, 0, MINE)
+        gather_own(3, 0, C)
+        gather_own(3, C, MINE)
+        rounded_0 = keep.tile([P, C, PACK], BF16, name="rounded_0", align_bytes=64)
+        nc.vector.tensor_copy(interleaved(rounded_0[:]), planes(gated[:, :, :C]))
+        rounded_a = keep.tile([P, HALF - MINE, PACK], BF16, name="rounded_a", align_bytes=64)
+        nc.gpsimd.tensor_tensor(
+            interleaved(rounded_a[:, KEPT:, :]), planes(picked_a[:, :, KEPT:]), planes(factor_low[:, :, KEPT:]), ALU.mult
+        )
+
+        factor_high = keep.tile([P, PACK, HALF], F32, name="factor_high", tag="held")
+        for r in (0, 2):
+            make_factor(factor_high[:, r : r + 2, :], acts[r, HALF][:], HALF, S)
+        rounded_s = keep.tile([P, HALF, PACK], BF16, name="rounded_s", align_bytes=64)
+        finish(rounded_a[:, :KEPT, :], picked_a[:, :, :KEPT], factor_low[:, :, :KEPT])
+        finish(rounded_s[:, : CUT_A - HALF, :], picked_b[:], factor_high[:, :, : CUT_A - HALF])
+        quant(rounded_0[:], 0, C)
+        bank_0 = proj(0, C, "bank1")
+        quant(rounded_a[:], MINE, HALF)
+        bank_a = proj(MINE, HALF, "bank2")
+        quant(rounded_s[:, : CUT_A - HALF, :], HALF, CUT_A)
+        bank_b = proj(HALF, CUT_A, "bank3")
+        finish(rounded_s[:, CUT_A - HALF : CUT_B - HALF, :], picked_c[:], factor_high[:, :, CUT_A - HALF : CUT_B - HALF])
+        finish(rounded_s[:, CUT_B - HALF :, :], picked_d[:], factor_high[:, :, CUT_B - HALF :])
+        quant(rounded_s[:, CUT_A - HALF : CUT_B - HALF, :], CUT_A, CUT_B)
+        bank_c = proj(CUT_A, CUT_B, "bank4")
+        quant(rounded_s[:, CUT_B - HALF :, :], CUT_B, S)
+        bank_d = proj(CUT_B, S, "bank7")
+        rounded_v = keep.tile([P, MINE - C, PACK], BF16, name="rounded_v", align_bytes=64)
+        nc.scalar.copy(interleaved(rounded_v[:]), planes(gated[:, :, C:]))
+        codes_v = keep.tile([P, MINE - C], I32, name="codes_v", tag="dy", align_bytes=64)
+        quant(rounded_v[:], C, MINE)
+        bank_v = proj(C, MINE, "bank0")
+        nc.scalar.copy(dx[:, :C], bank_0[:])
+        nc.scalar.copy(dx[:, MINE:HALF], bank_a[:])
+        nc.scalar.copy(dx[:, HALF:CUT_A], bank_b[:])
+        nc.scalar.copy(dx[:, CUT_A:CUT_B], bank_c[:])
+        nc.vector.tensor_copy(dx[:, CUT_B:], bank_d[:])
+        nc.scalar.copy(dx[:, C:MINE], bank_v[:])
 
         first = keep.tile([P, T], F32, name="first")
         result = keep.tile([P, T], F32, name="result")

@@ -23,8 +23,8 @@ HALF = S // 2
 RUN = 4
 LINE = 4
 OWN = 96
-KEPT = 64
-MINE = 256
+POOLED = 192
+SPLIT = 384
 CUT_A = 768
 CUT_B = 896
 
@@ -54,7 +54,6 @@ def tile_moe_sdb_relu_kernel(
         gate_cols = keep.tile([P, 2, 8], F32, name="gate_cols")
         identity = keep.tile([P, P], F32, name="identity")
         dc = [keep.tile([P, T], F32, name=f"dc{r}") for r in range(PACK)]
-        da_codes = keep.tile([P, S], I32, name="da_codes", align_bytes=64)
         da_scales = keep.tile([P, S], U8, name="da_scales", align_bytes=64)
         dx = keep.tile([P, S], F32, name="dx")
 
@@ -180,7 +179,7 @@ def tile_moe_sdb_relu_kernel(
             nc.vector.tensor_tensor(interleaved(dst), planes(src), planes(factor), ALU.mult)
 
         def codes(j0, j1):
-            return codes_v[:] if j0 == C else da_codes[:, j0:j1]
+            return codes_v[:] if j0 == SPLIT else da_codes[:, j0:j1]
 
         def quant(src, j0, j1):
             nc.vector.quantize_mx(
@@ -203,18 +202,18 @@ def tile_moe_sdb_relu_kernel(
                 )
             return bank
 
-        gated = keep.tile([P, PACK, MINE], F32, name="gated")
-        factor_own = keep.tile([P, PACK, MINE], F32, name="factor_own", tag="held")
-        factor_low = keep.tile([P, PACK, HALF - MINE], F32, name="factor_low")
-        picked_a = keep.tile([P, PACK, HALF - MINE], F32, name="picked_a")
+        gated = keep.tile([P, PACK, HALF - POOLED], F32, name="gated")
+        factor_low = keep.tile([P, PACK, HALF], F32, name="factor_low")
+        factor_last = keep.tile([P, 1, C], F32, name="factor_last", tag="held")
+        picked_a = keep.tile([P, PACK, POOLED], F32, name="picked_a")
         hidden(0, (0, 1), ((0, C, "bank0", nc.scalar.copy), (C, 256, "bank7", nc.scalar.copy), (256, T, "bank1", nc.scalar.copy)))
-        fetch(picked_a, 0, MINE, HALF)
+        fetch(picked_a, 0, 0, POOLED)
         hidden(1, (1, 0), ((0, T, "bank2", nc.scalar.copy),))
         hidden(2, (1, 0), ((0, T, "bank3", nc.scalar.copy),))
-        fetch(picked_a, 1, MINE, HALF)
+        fetch(picked_a, 1, 0, POOLED)
         hidden(3, (1, 0), ((0, T, "bank4", nc.scalar.copy),))
         for r in (2, 3):
-            fetch(picked_a, r, MINE, HALF)
+            fetch(picked_a, r, 0, POOLED)
         picked_b = keep.tile([P, PACK, CUT_A - HALF], F32, name="picked_b", tag="dy", align_bytes=64)
         picked_c = keep.tile([P, PACK, CUT_B - CUT_A], F32, name="picked_c", tag="w2", align_bytes=64)
         picked_d = keep.tile([P, PACK, S - CUT_B], F32, name="picked_d", tag="w2_low", align_bytes=64)
@@ -222,36 +221,31 @@ def tile_moe_sdb_relu_kernel(
             for r in range(PACK):
                 fetch(picked, r, j0, j1)
 
-        def gather_own(r, j0, j1):
-            nc.vector.tensor_tensor(gated[:, r, j0:j1], window(r, j0, j1), factor_own[:, r, j0:j1], ALU.mult)
+        def gather_own(r, j0, j1, factor):
+            nc.vector.tensor_tensor(gated[:, r, j0 - POOLED : j1 - POOLED], window(r, j0, j1), factor, ALU.mult)
 
-        for r in range(PACK):
-            make_factor(factor_own[:, r : r + 1, :], acts[r, 0][:, :, :MINE], 0, MINE)
-            high = acts[1, MINE][:] if r == 1 else acts[r, 0][:, :, MINE:]
-            make_factor(factor_low[:, r : r + 1, :], high, MINE, HALF)
-            if r == 2:
-                gather_own(0, 0, MINE)
+        for r, j0, j1 in ((0, 0, HALF), (1, 0, 256), (1, 256, HALF), (2, 0, HALF)):
+            make_factor(factor_low[:, r : r + 1, j0:j1], acts[r, j0][:], j0, j1)
+        gather_own(0, POOLED, HALF, factor_low[:, 0, POOLED:])
+        make_factor(factor_low[:, 3:, :SPLIT], acts[3, 0][:, :, :SPLIT], 0, SPLIT)
+        make_factor(factor_last[:], acts[3, 0][:, :, SPLIT:], SPLIT, HALF)
         for r in (1, 2):
-            gather_own(r, 0, MINE)
-        gather_own(3, 0, C)
-        gather_own(3, C, MINE)
-        rounded_0 = keep.tile([P, C, PACK], BF16, name="rounded_0", align_bytes=64)
-        nc.vector.tensor_copy(interleaved(rounded_0[:]), planes(gated[:, :, :C]))
-        rounded_a = keep.tile([P, HALF - MINE, PACK], BF16, name="rounded_a", align_bytes=64)
-        nc.gpsimd.tensor_tensor(
-            interleaved(rounded_a[:, KEPT:, :]), planes(picked_a[:, :, KEPT:]), planes(factor_low[:, :, KEPT:]), ALU.mult
-        )
+            gather_own(r, POOLED, HALF, factor_low[:, r, POOLED:])
+        gather_own(3, POOLED, SPLIT, factor_low[:, 3, POOLED:SPLIT])
+        gather_own(3, SPLIT, HALF, factor_last[:, 0, :])
+        rounded_a = keep.tile([P, SPLIT, PACK], BF16, name="rounded_a", align_bytes=64)
+        nc.vector.tensor_copy(interleaved(rounded_a[:, POOLED:, :]), planes(gated[:, :, : SPLIT - POOLED]))
+        nc.gpsimd.tensor_tensor(interleaved(rounded_a[:, :POOLED, :]), planes(picked_a[:]), planes(factor_low[:, :, :POOLED]), ALU.mult)
 
         factor_high = keep.tile([P, PACK, HALF], F32, name="factor_high", tag="held")
-        for r in (0, 2):
-            make_factor(factor_high[:, r : r + 2, :], acts[r, HALF][:], HALF, S)
+        for j0, j1 in ((HALF, CUT_A), (CUT_A, S)):
+            for r in (0, 2):
+                make_factor(factor_high[:, r : r + 2, j0 - HALF : j1 - HALF], acts[r, HALF][:, :, j0 - HALF : j1 - HALF], j0, j1)
+        da_codes = keep.tile([P, S], I32, name="da_codes", tag=f"acts2_{HALF}", align_bytes=64)
         rounded_s = keep.tile([P, HALF, PACK], BF16, name="rounded_s", align_bytes=64)
-        finish(rounded_a[:, :KEPT, :], picked_a[:, :, :KEPT], factor_low[:, :, :KEPT])
         finish(rounded_s[:, : CUT_A - HALF, :], picked_b[:], factor_high[:, :, : CUT_A - HALF])
-        quant(rounded_0[:], 0, C)
-        bank_0 = proj(0, C, "bank1")
-        quant(rounded_a[:], MINE, HALF)
-        bank_a = proj(MINE, HALF, "bank2")
+        quant(rounded_a[:], 0, SPLIT)
+        bank_a = proj(0, SPLIT, "bank2")
         quant(rounded_s[:, : CUT_A - HALF, :], HALF, CUT_A)
         bank_b = proj(HALF, CUT_A, "bank3")
         finish(rounded_s[:, CUT_A - HALF : CUT_B - HALF, :], picked_c[:], factor_high[:, :, CUT_A - HALF : CUT_B - HALF])
@@ -260,17 +254,16 @@ def tile_moe_sdb_relu_kernel(
         bank_c = proj(CUT_A, CUT_B, "bank4")
         quant(rounded_s[:, CUT_B - HALF :, :], CUT_B, S)
         bank_d = proj(CUT_B, S, "bank7")
-        rounded_v = keep.tile([P, MINE - C, PACK], BF16, name="rounded_v", align_bytes=64)
-        nc.scalar.copy(interleaved(rounded_v[:]), planes(gated[:, :, C:]))
-        codes_v = keep.tile([P, MINE - C], I32, name="codes_v", tag="dy", align_bytes=64)
-        quant(rounded_v[:], C, MINE)
-        bank_v = proj(C, MINE, "bank0")
-        nc.scalar.copy(dx[:, :C], bank_0[:])
-        nc.scalar.copy(dx[:, MINE:HALF], bank_a[:])
+        rounded_v = keep.tile([P, C, PACK], BF16, name="rounded_v", align_bytes=64)
+        nc.scalar.copy(interleaved(rounded_v[:]), planes(gated[:, :, SPLIT - POOLED :]))
+        codes_v = keep.tile([P, C], I32, name="codes_v", tag="dy", align_bytes=64)
+        quant(rounded_v[:], SPLIT, HALF)
+        bank_v = proj(SPLIT, HALF, "bank0")
+        nc.scalar.copy(dx[:, :SPLIT], bank_a[:])
         nc.scalar.copy(dx[:, HALF:CUT_A], bank_b[:])
         nc.scalar.copy(dx[:, CUT_A:CUT_B], bank_c[:])
         nc.vector.tensor_copy(dx[:, CUT_B:], bank_d[:])
-        nc.scalar.copy(dx[:, C:MINE], bank_v[:])
+        nc.scalar.copy(dx[:, SPLIT:HALF], bank_v[:])
 
         first = keep.tile([P, T], F32, name="first")
         result = keep.tile([P, T], F32, name="result")

@@ -227,12 +227,13 @@ def tile_moe_sdb_relu_kernel(
         for r, j0, j1 in ((0, 0, HALF), (1, 0, 256), (1, 256, HALF), (2, 0, HALF)):
             make_factor(factor_low[:, r : r + 1, j0:j1], acts[r, j0][:], j0, j1)
         gather_own(0, POOLED, HALF, factor_low[:, 0, POOLED:])
-        make_factor(factor_low[:, 3:, :SPLIT], acts[3, 0][:, :, :SPLIT], 0, SPLIT)
+        make_factor(factor_low[:, 3:, : SPLIT - POOLED], acts[3, 0][:, :, POOLED:SPLIT], POOLED, SPLIT)
         make_factor(factor_last[:], acts[3, 0][:, :, SPLIT:], SPLIT, HALF)
         for r in (1, 2):
             gather_own(r, POOLED, HALF, factor_low[:, r, POOLED:])
-        gather_own(3, POOLED, SPLIT, factor_low[:, 3, POOLED:SPLIT])
+        gather_own(3, POOLED, SPLIT, factor_low[:, 3, : SPLIT - POOLED])
         gather_own(3, SPLIT, HALF, factor_last[:, 0, :])
+        make_factor(factor_low[:, 3:, :POOLED], acts[3, 0][:, :, :POOLED], 0, POOLED)
         rounded_a = keep.tile([P, SPLIT, PACK], BF16, name="rounded_a", align_bytes=64)
         nc.vector.tensor_copy(interleaved(rounded_a[:, POOLED:, :]), planes(gated[:, :, : SPLIT - POOLED]))
         nc.gpsimd.tensor_tensor(interleaved(rounded_a[:, :POOLED, :]), planes(picked_a[:]), planes(factor_low[:, :, :POOLED]), ALU.mult)

@@ -23,7 +23,7 @@ HALF = S // 2
 RUN = 4
 LINE = 4
 OWN = 96
-POOLED = 192
+POOLED = 224
 SPLIT = 384
 CUT_A = 768
 CUT_B = 896
@@ -46,7 +46,7 @@ def tile_moe_sdb_relu_kernel(
         w2_sorted = {}
         dy_codes = keep.tile([P, PASSES, T], I32, name="dy_codes", tag="dy", align_bytes=64)
         w1_codes = keep.tile([P, E, K], I32, name="w1_codes", align_bytes=64)
-        w2_scales_raw = keep.tile([P, H], U8, name="w2_scales_raw", align_bytes=64)
+        w2_scales_raw = keep.tile([P, PASSES, H], U8, name="w2_scales_raw", align_bytes=64)
         scale_sets = ((0, 1, "lead"), (1, PACK, "rest"))
         w2_scales = {}
         dy_planes = keep.tile([P, PASSES, T], U8, name="dy_planes", align_bytes=64)
@@ -78,8 +78,8 @@ def tile_moe_sdb_relu_kernel(
 
         def load_w2_scales(q):
             nc.sync.dma_start(
-                w2_scales_raw[32 * q : 32 * q + 4 * PASSES, :].bitcast(I32),
-                w2t_scales[:, 4 * q : 4 * q + 4, :].bitcast(I32),
+                w2_scales_raw[32 * q + 4 : 32 * q + 8, :, :].bitcast(I32),
+                w2t_scales[:, 4 * q : 4 * q + 4, :].rearrange("s b i -> b s i").bitcast(I32),
             )
 
         def load_acts(r0, r1, j0, j1):
@@ -129,10 +129,10 @@ def tile_moe_sdb_relu_kernel(
             for r in range(2):
                 w2_sorted[r0 + r] = words[:, r, :, :]
         for r0, r1, tag in scale_sets:
-            tile = keep.tile([P, r1 - r0, P], U8, name=f"w2_scales{r0}", tag=tag, align_bytes=64)
-            nc.vector.tensor_copy(tile[:], w2_scales_raw[:].rearrange("p (m r) -> p r m", r=PACK)[:, r0:r1, :])
+            tile = keep.tile([P, r1 - r0, PASSES, P], U8, name=f"w2_scales{r0}", tag=tag, align_bytes=64)
+            nc.vector.tensor_copy(tile[:], w2_scales_raw[:].rearrange("p s (m r) -> p r s m", r=PACK)[:, r0:r1, :, :])
             for r in range(r0, r1):
-                w2_scales[r] = tile[4:, r - r0, :], tile[:, r - r0, :]
+                w2_scales[r] = tile[4:, r - r0, :, :]
 
         def hidden(r, order, spans):
             banks = [psum.tile([P, t1 - t0], F32, name=f"dc_bank{r}_{t0}", tag=tag) for t0, t1, tag, copy in spans]
@@ -141,7 +141,7 @@ def tile_moe_sdb_relu_kernel(
                     nc.tensor.matmul_mx(
                         out=bank[:],
                         lhsT=w2_sorted[r][:, s, :].bitcast(FP8X4),
-                        lhsT_scale=w2_scales[r][1 - s],
+                        lhsT_scale=w2_scales[r][:, s, :],
                         rhs=dy_codes[:, s, t0:t1].bitcast(FP8X4),
                         rhs_scale=dy_planes[:, s, t0:t1],
                         start=(s == order[0]),

from contextlib import ExitStack

import concourse.mybir as mybir

K, T, E, C, H, N = 128, 512, 8, 128, 512, 1024
S = E * C
FLOPS = 2 * N * H * T + 2 * H * K * S

F32 = mybir.dt.float32
BF16 = mybir.dt.bfloat16
I32 = mybir.dt.int32
U32 = mybir.dt.uint32
U16 = mybir.dt.uint16
U8 = mybir.dt.uint8
FP8X4 = mybir.dt.float8_e4m3fn_x4
ALU = mybir.AluOpType
ACT = mybir.ActivationFunctionType

P = 128
PACK = 4
PASSES = N // (P * PACK)
HALF = S // 2
RUN = 4
LINE = 4
OWN = 96
POOLED = 224
SPLIT = 384
CUT_A = 768
CUT_B = 896


def tile_moe_sdb_relu_kernel(
    tc, dy_words, dy_scales, w2t_words, w2t_scales, w1t_words, w1t_scales, a, gate, offs, pos1, pos2, out
):
    nc = tc.nc

    with ExitStack() as ctx:
        keep = ctx.enter_context(tc.tile_pool(name="keep", bufs=1))
        psum = ctx.enter_context(tc.psum_pool(name="psum", bufs=1))

        offs_sb = keep.tile([P, S // 16], U16, name="offs_sb")
        pos1_sb = keep.tile([P, T // 16], U16, name="pos1_sb")
        pos2_sb = keep.tile([P, T // 16], U16, name="pos2_sb")

        w2_raw = keep.tile([P, PASSES, H], I32, name="w2_raw", align_bytes=64)
        w2_sorted = {}
        dy_codes = keep.tile([P, PASSES, T], I32, name="dy_codes", tag="dy", align_bytes=64)
        w1_codes = keep.tile([P, E, K], I32, name="w1_codes", align_bytes=64)
        w2_scales_raw = keep.tile([P, PASSES, H], U8, name="w2_scales_raw", align_bytes=64)
        scale_sets = ((0, 1, "lead"), (1, PACK, "rest"))
        w2_scales = {}
        dy_planes = keep.tile([P, PASSES, T], U8, name="dy_planes", align_bytes=64)
        w1_scales = keep.tile([P, E, K], U8, name="w1_scales", align_bytes=64)
        gate_cols = keep.tile([P, 2, 8], F32, name="gate_cols")
        identity = keep.tile([P, P], F32, name="identity")
        dc = [keep.tile([P, T], F32, name=f"dc{r}") for r in range(PACK)]
        da_scales = keep.tile([P, S], U8, name="da_scales", align_bytes=64)
        dx = keep.tile([P, S], F32, name="dx")

        a_rows = a.rearrange("(p r) j -> p r j", r=PACK)
        zeros = keep.tile([P, P], F32, name="zeros", tag="wide")
        nc.gpsimd.memset(zeros[:], 0.0)
        nc.gpsimd.memset(w2_scales_raw[:].bitcast(I32), 0)
        nc.gpsimd.affine_select(
            out=identity[:], in_=zeros[:], compare_op=ALU.not_equal, fill=1.0, base=0, pattern=[[-1, P]], channel_multiplier=1
        )
        acts = {}
        acts[0, 0] = keep.tile([P, 1, HALF], F32, name="acts_early", tag="wide")
        nc.gpsimd.dma_start(acts[0, 0][:], a_rows[:, 0:1, :HALF])

        dy_rows = dy_words.rearrange("s p t d -> p s (t d)").bitcast(I32)

        def load_dy_scales(q):
            nc.sync.dma_start(
                dy_planes[32 * q : 32 * q + 4, :, :].bitcast(I32),
                dy_scales[:, 4 * q : 4 * q + 4, :].rearrange("s b t -> b s t").bitcast(I32),
            )

        def load_w2_scales(q):
            nc.sync.dma_start(
                w2_scales_raw[32 * q + 4 : 32 * q + 8, :, :].bitcast(I32),
                w2t_scales[:, 4 * q : 4 * q + 4, :].rearrange("s b i -> b s i").bitcast(I32),
            )

        def load_acts(r0, r1, j0, j1):
            tile = keep.tile([P, r1 - r0, j1 - j0], F32, name=f"acts{r0}_{j0}", tag=f"acts{r0}_{j0}", align_bytes=64)
            nc.sync.dma_start(tile[:], a_rows[:, r0:r1, j0:j1])
            acts[r0, j0] = tile

        nc.sync.dma_start(gate_cols[:, :, :RUN], gate[0, :].rearrange("(h n c) -> n h c", h=2, c=RUN))
        for q in range(3):
            load_dy_scales(q)
        nc.sync.dma_start(w2_raw[:], w2t_words.rearrange("s p i d -> p s (i d)").bitcast(I32))
        for q in range(4):
            load_w2_scales(q)
        nc.sync.dma_start(dy_codes[:, 0, :], dy_rows[:, 0, :])
        load_dy_scales(3)
        nc.sync.dma_start(dy_codes[:, 1, :], dy_rows[:, 1, :])
        load_acts(1, 2, 0, 256)
        nc.sync.dma_start(offs_sb[:], offs)
        load_acts(1, 2, 256, HALF)
        load_acts(2, 3, 0, HALF)
        load_acts(3, PACK, 0, HALF)
        load_acts(0, 2, HALF, S)
        load_acts(2, PACK, HALF, S)
        nc.sync.dma_start(w1_codes[:], w1t_words.rearrange("e o p k d -> p (e o) (k d)").bitcast(I32))
        for q in range(4):
            nc.sync.dma_start(
                w1_scales[32 * q : 32 * q + 4, :, :].bitcast(I32),
                w1t_scales[:, 0, 4 * q : 4 * q + 4, :].rearrange("e b k -> b e k").bitcast(I32),
            )
        nc.sync.dma_start(pos1_sb[:], pos1)
        nc.sync.dma_start(pos2_sb[:], pos2)

        spreads = []
        for h in range(2):
            spread = psum.tile([P, P, RUN], F32, name=f"spread{h}", tag=f"bank{5 + h}")
            for c in range(RUN):
                column = gate_cols[:, h, c : c + 1]
                nc.tensor.transpose(spread[:, :, c], column.to_broadcast([P, P]), identity[:])
            spreads.append(spread[:].rearrange("p n c -> p (n c)"))

        for r0, tag, copy, word in ((0, "w2_low", nc.vector.tensor_copy, I32), (2, "w2", nc.scalar.copy, U32)):
            words = keep.tile([P, 2, PASSES, P], word, name=f"w2_sorted{r0}", tag=tag, align_bytes=64)
            copy(
                words[:].rearrange("p r s (c i) -> p (s c) r i", i=4),
                w2_raw[:].bitcast(word).rearrange("p s (c i r) -> p (s c) r i", i=4, r=PACK)[:, :, r0 : r0 + 2, :],
            )
            for r in range(2):
                w2_sorted[r0 + r] = words[:, r, :, :]
        for r0, r1, tag in scale_sets:
            tile = keep.tile([P, r1 - r0, PASSES, P], U8, name=f"w2_scales{r0}", tag=tag, align_bytes=64)
            nc.vector.tensor_copy(tile[:], w2_scales_raw[:].rearrange("p s (m r) -> p r s m", r=PACK)[:, r0:r1, :, :])
            for r in range(r0, r1):
                w2_scales[r] = tile[4:, r - r0, :, :]

        def hidden(r, order, spans):
            banks = [psum.tile([P, t1 - t0], F32, name=f"dc_bank{r}_{t0}", tag=tag) for t0, t1, tag, copy in spans]
            for s in order:
                for (t0, t1, tag, copy), bank in zip(spans, banks):
                    nc.tensor.matmul_mx(
                        out=bank[:],
                        lhsT=w2_sorted[r][:, s, :].bitcast(FP8X4),
                        lhsT_scale=w2_scales[r][:, s, :],
                        rhs=dy_codes[:, s, t0:t1].bitcast(FP8X4),
                        rhs_scale=dy_planes[:, s, t0:t1],
                        start=(s == order[0]),
                        stop=(s == order[-1]),
                    )
            for (t0, t1, tag, copy), bank in zip(spans, banks):
                copy(dc[r][:, t0:t1], bank[:])

        def window(r, j0, j1):
            return dc[r][:].indirect(offs_sb[:, j0 // 16 : j1 // 16])

        def interleaved(ap):
            return ap.rearrange("p (c i) r -> p c r i", i=LINE)

        def planes(ap):
            return ap.rearrange("p r (c i) -> p c r i", i=LINE)

        def make_factor(dst, src, j0, j1):
            h = j0 // HALF
            rows = src.shape[1]
            nc.vector.scalar_tensor_tensor(
                dst,
                src,
                0.0,
                spreads[h][:, j0 - h * HALF : j1 - h * HALF].unsqueeze(1).to_broadcast([P, rows, j1 - j0]),
                ALU.is_gt,
                ALU.mult,
            )

        def fetch(dst, r, j0, j1, origin=None):
            origin = j0 if origin is None else origin
            nc.scalar.activation(dst[:, r, j0 - origin : j1 - origin], window(r, j0, j1), ACT.Copy)

        def finish(dst, src, factor):
            nc.vector.tensor_tensor(interleaved(dst), planes(src), planes(factor), ALU.mult)

        def codes(j0, j1):
            return codes_v[:] if j0 == SPLIT else da_codes[:, j0:j1]

        def quant(src, j0, j1):
            nc.vector.quantize_mx(
                out=codes(j0, j1).bitcast(FP8X4),
                scales=da_scales[:, j0:j1],
                in_=src.rearrange("p j r -> p (j r)"),
            )

        def proj(j0, j1, tag):
            bank = psum.tile([P, j1 - j0], F32, name=f"dx_bank{j0}", tag=tag)
            for e in range(j0 // C, j1 // C):
                nc.tensor.matmul_mx(
                    out=bank[:, e * C - j0 : (e + 1) * C - j0],
                    lhsT=w1_codes[:, e, :].bitcast(FP8X4),
                    lhsT_scale=w1_scales[:, e, :],
                    rhs=codes(e * C, (e + 1) * C).bitcast(FP8X4),
                    rhs_scale=da_scales[:, e * C : (e + 1) * C],
                    start=True,
                    stop=True,
                )
            return bank

        gated = keep.tile([P, PACK, HALF - POOLED], F32, name="gated")
        factor_low = keep.tile([P, PACK, HALF], F32, name="factor_low")
        factor_last = keep.tile([P, 1, C], F32, name="factor_last", tag="held")
        picked_a = keep.tile([P, PACK, POOLED], F32, name="picked_a")
        hidden(0, (0, 1), ((0, C, "bank0", nc.scalar.copy), (C, 256, "bank7", nc.scalar.copy), (256, T, "bank1", nc.scalar.copy)))
        fetch(picked_a, 0, 0, POOLED)
        hidden(1, (1, 0), ((0, T, "bank2", nc.scalar.copy),))
        hidden(2, (1, 0), ((0, T, "bank3", nc.scalar.copy),))
        fetch(picked_a, 1, 0, POOLED)
        hidden(3, (1, 0), ((0, T, "bank4", nc.scalar.copy),))
        for r in (2, 3):
            fetch(picked_a, r, 0, POOLED)
        picked_b = keep.tile([P, PACK, CUT_A - HALF], F32, name="picked_b", tag="dy", align_bytes=64)
        picked_c = keep.tile([P, PACK, CUT_B - CUT_A], F32, name="picked_c", tag="w2", align_bytes=64)
        picked_d = keep.tile([P, PACK, S - CUT_B], F32, name="picked_d", tag="w2_low", align_bytes=64)
        for picked, j0, j1 in ((picked_b, HALF, CUT_A), (picked_c, CUT_A, CUT_B), (picked_d, CUT_B, S)):
            for r in range(PACK):
                fetch(picked, r, j0, j1)

        def gather_own(r, j0, j1, factor):
            nc.vector.tensor_tensor(gated[:, r, j0 - POOLED : j1 - POOLED], window(r, j0, j1), factor, ALU.mult)

        for r, j0, j1 in ((0, 0, HALF), (1, 0, 256), (1, 256, HALF), (2, 0, HALF)):
            make_factor(factor_low[:, r : r + 1, j0:j1], acts[r, j0][:], j0, j1)
        gather_own(0, POOLED, HALF, factor_low[:, 0, POOLED:])
        make_factor(factor_low[:, 3:, : SPLIT - POOLED], acts[3, 0][:, :, POOLED:SPLIT], POOLED, SPLIT)
        make_factor(factor_last[:], acts[3, 0][:, :, SPLIT:], SPLIT, HALF)
        for r in (1, 2):
            gather_own(r, POOLED, HALF, factor_low[:, r, POOLED:])
        gather_own(3, POOLED, SPLIT, factor_low[:, 3, : SPLIT - POOLED])
        gather_own(3, SPLIT, HALF, factor_last[:, 0, :])
        make_factor(factor_low[:, 3:, :POOLED], acts[3, 0][:, :, :POOLED], 0, POOLED)
        rounded_a = keep.tile([P, SPLIT, PACK], BF16, name="rounded_a", align_bytes=64)
        nc.vector.tensor_copy(interleaved(rounded_a[:, POOLED:, :]), planes(gated[:, :, : SPLIT - POOLED]))
        nc.gpsimd.tensor_tensor(interleaved(rounded_a[:, :POOLED, :]), planes(picked_a[:]), planes(factor_low[:, :, :POOLED]), ALU.mult)

        factor_high = keep.tile([P, PACK, HALF], F32, name="factor_high", tag="held")
        for j0, j1 in ((HALF, CUT_A), (CUT_A, S)):
            for r in (0, 2):
                make_factor(factor_high[:, r : r + 2, j0 - HALF : j1 - HALF], acts[r, HALF][:, :, j0 - HALF : j1 - HALF], j0, j1)
        da_codes = keep.tile([P, S], I32, name="da_codes", tag=f"acts2_{HALF}", align_bytes=64)
        rounded_s = keep.tile([P, HALF, PACK], BF16, name="rounded_s", align_bytes=64)
        finish(rounded_s[:, : CUT_A - HALF, :], picked_b[:], factor_high[:, :, : CUT_A - HALF])
        quant(rounded_a[:], 0, SPLIT)
        bank_a = proj(0, SPLIT, "bank2")
        quant(rounded_s[:, : CUT_A - HALF, :], HALF, CUT_A)
        bank_b = proj(HALF, CUT_A, "bank3")
        finish(rounded_s[:, CUT_A - HALF : CUT_B - HALF, :], picked_c[:], factor_high[:, :, CUT_A - HALF : CUT_B - HALF])
        finish(rounded_s[:, CUT_B - HALF :, :], picked_d[:], factor_high[:, :, CUT_B - HALF :])
        quant(rounded_s[:, CUT_A - HALF : CUT_B - HALF, :], CUT_A, CUT_B)
        bank_c = proj(CUT_A, CUT_B, "bank4")
        quant(rounded_s[:, CUT_B - HALF :, :], CUT_B, S)
        bank_d = proj(CUT_B, S, "bank7")
        rounded_v = keep.tile([P, C, PACK], BF16, name="rounded_v", align_bytes=64)
        nc.scalar.copy(interleaved(rounded_v[:]), planes(gated[:, :, SPLIT - POOLED :]))
        codes_v = keep.tile([P, C], I32, name="codes_v", tag="dy", align_bytes=64)
        quant(rounded_v[:], SPLIT, HALF)
        bank_v = proj(SPLIT, HALF, "bank0")
        nc.scalar.copy(dx[:, :SPLIT], bank_a[:])
        nc.scalar.copy(dx[:, HALF:CUT_A], bank_b[:])
        nc.scalar.copy(dx[:, CUT_A:CUT_B], bank_c[:])
        nc.vector.tensor_copy(dx[:, CUT_B:], bank_d[:])
        nc.scalar.copy(dx[:, SPLIT:HALF], bank_v[:])

        first = keep.tile([P, T], F32, name="first")
        result = keep.tile([P, T], F32, name="result")
        cuts = (0, OWN, 2 * OWN, 352, T)
        parts = list(zip(cuts, cuts[1:]))
        nc.vector.tensor_copy(first[:, :OWN], dx[:].indirect(pos1_sb[:, : OWN // 16]))
        for t0, t1 in parts[1:]:
            nc.scalar.activation(first[:, t0:t1], dx[:].indirect(pos1_sb[:, t0 // 16 : t1 // 16]), ACT.Copy)
        for t0, t1 in (parts[1], parts[0], parts[2], parts[3]):
            nc.vector.tensor_tensor(
                result[:, t0:t1], dx[:].indirect(pos2_sb[:, t0 // 16 : t1 // 16]), first[:, t0:t1], ALU.add
            )
        for t0, t1 in ((0, cuts[3]), (cuts[3], T)):
            nc.sync.dma_start(out[:, t0:t1], result[:, t0:t1])
